import numpy as np
import ml_dtypes


def mxq(x, axis, fmt="e4m3"):
    dtype, down = {"e4m3": (ml_dtypes.float8_e4m3fn, 7), "e5m2": (ml_dtypes.float8_e5m2, 14)}[fmt]
    v = np.moveaxis(np.asarray(x, np.float32).astype(ml_dtypes.bfloat16).astype(np.float64), axis, -1)
    blocks = v.reshape(v.shape[:-1] + (-1, 32))
    amax = np.abs(blocks).max(-1, keepdims=True)
    byte = np.maximum(np.where(amax > 0, np.frexp(amax)[1] - 1 + 127, 0) - down, 1)
    scale = np.exp2(byte - 127.0)
    codes = (blocks / scale).astype(np.float32).astype(dtype).astype(np.float64)
    return np.moveaxis((codes * scale).reshape(v.shape), -1, axis)


WIDE = False


def mx_kscale(k):
    if not WIDE:
        return np.ones(k)
    levels = np.array([10, -10, 5, -5, 0])
    if k % 512:
        return np.exp2(np.random.permutation(np.resize(levels, k // 32))).repeat(32)
    a = np.empty((k // 512, 16))
    for p in range(k // 512):
        a[p, :8] = np.random.permutation(np.resize(levels, 8))
        for g in range(8):
            far = levels[np.abs(levels - a[p, g]) >= 10]
            a[p, g + 8] = far[np.random.randint(len(far))]
    return np.exp2(a.ravel()).repeat(32)


def f64(x):
    return np.asarray(x).astype(np.float64)


def striped(idx):
    return np.tile(np.asarray(idx).reshape(-1, 16).T, (8, 1)).astype(np.uint16)


def unstriped(offs):
    return offs[:16].T.reshape(-1).astype(np.int64)


B, N, T, D, DV, NQ = 1, 512, 1024, 512, 256, 128
CAP = 2.0
DRAFT = 128


def setup_inputs():
    n = np.random.standard_normal
    idx = np.random.permutation(T)[:B * N]
    s = mx_kscale(D)[:, None]
    u = np.ones(T)
    u[idx] = mx_kscale(B * N)
    r = np.random.uniform(0.5, 2.0, T)
    k = n((D, T)) / s
    v = n((DV, T)) / (u * r)
    when = np.zeros(T)
    when[idx] = np.concatenate([np.concatenate([np.arange(N - DRAFT), N - DRAFT + np.random.randint(0, 16, DRAFT)]) for b in range(B)])
    return {
        "qT": (n((B, D, NQ)) * s * (0.80 / np.sqrt(D))).astype(np.float32),
        "kT": k.astype(np.float32),
        "vT": v.astype(np.float32),
        "vs": np.tile(u * r, (128, 1)).astype(np.float32),
        "pos": np.tile(when, (128, 1)).astype(np.float32),
        "qpos": np.random.randint(N - DRAFT, N - DRAFT + 16, (B, NQ, 1)).astype(np.float32),
        "offs": striped(idx),
    }


def reference(qT, kT, vT, vs, pos, qpos, offs):
    idx = unstriped(offs)
    k = f64(kT)
    v = f64(vT)
    pick = lambda x: x[:, idx].reshape(x.shape[0], B, N).transpose(1, 0, 2)
    q = f64(qT)
    score = mxq(q, 1, "e4m3").transpose(0, 2, 1) @ mxq(pick(k), 1, "e4m3")
    score = CAP * np.tanh(score / CAP)
    score = np.where(pick(f64(pos))[:, :1, :] <= f64(qpos), score, -30000.0)
    m = score.max(-1, keepdims=True)
    p = np.exp(score - m)
    total = p.sum(-1, keepdims=True)
    w = p * pick(f64(vs))[:, :1, :]
    y = mxq(w, 2, "e4m3") @ mxq(pick(v).transpose(0, 2, 1), 1, "e4m3")
    y = y / total
    return y

@@ -1,0 +1,185 @@
+from contextlib import ExitStack
+
+import concourse.mybir as mybir
+from concourse.masks import make_identity
+
+D, T, N, DV, NQ = 512, 1024, 512, 256, 128
+CAP = 2.0
+MASKED = -30000.0
+FLOPS = 2 * D * NQ * N + 2 * N * NQ * DV
+
+P = 128
+PACK = 4
+HALF = N // 2
+CHUNK = T // 2
+
+F32 = mybir.dt.float32
+BF16 = mybir.dt.bfloat16
+U32 = mybir.dt.uint32
+U16 = mybir.dt.uint16
+U8 = mybir.dt.uint8
+FP8X4 = mybir.dt.float8_e4m3fn_x4
+ALU = mybir.AluOpType
+ACT = mybir.ActivationFunctionType
+AX = mybir.AxisListType
+
+
+def tile_attend_x_draft_cap_topk_kernel(tc, qT, kT, vT, vs, pos, qpos, offs, out):
+    nc = tc.nc
+    with ExitStack() as ctx:
+        keep = ctx.enter_context(tc.tile_pool(name="keep", bufs=1))
+        psum = ctx.enter_context(tc.psum_pool(name="psum", bufs=1))
+
+        offsets = keep.tile([P, N // 16], U16, name="offsets")
+        qpos_col = keep.tile([P, 1], F32, name="qpos_col")
+        pos_pool = keep.tile([P, T], F32, name="pos_pool")
+        vs_pool = keep.tile([P, T], F32, name="vs_pool")
+        q_raw = keep.tile([P, PACK, NQ], F32, name="q_raw", tag="q_raw")
+        k_rows = kT.rearrange("(p j) t -> p j t", j=PACK)
+        v_rows = vT.rearrange("(p h) t -> p h t", h=2)
+        k_raw = {(u, c): keep.tile([P, 2, CHUNK], F32, name=f"k_raw{u}{c}") for u in range(2) for c in range(2)}
+        v_raw = [keep.tile([P, 2, CHUNK], F32, name=f"v_raw{c}") for c in range(2)]
+
+        def load_k(u, c):
+            nc.sync.dma_start(out=k_raw[u, c][:], in_=k_rows[:, 2 * u : 2 * u + 2, c * CHUNK : (c + 1) * CHUNK])
+
+        def load_v(c):
+            nc.sync.dma_start(out=v_raw[c][:], in_=v_rows[:, :, c * CHUNK : (c + 1) * CHUNK])
+
+        nc.sync.dma_start(out=pos_pool[:], in_=pos)
+        nc.sync.dma_start(offsets[:], offs)
+        load_k(0, 0)
+        load_k(0, 1)
+        load_k(1, 0)
+        load_k(1, 1)
+        nc.sync.dma_start(out=qpos_col[:], in_=qpos.rearrange("b q o -> (b q) o"))
+        nc.sync.dma_start(out=q_raw[:], in_=qT.rearrange("b (p j) q -> p (b j) q", j=PACK))
+        load_v(0)
+        nc.sync.dma_start(out=vs_pool[:], in_=vs)
+        load_v(1)
+
+        warm = keep.tile([P, 1], F32, name="warm")
+        nc.gpsimd.memset(warm[:], 0.0)
+        warm_out = keep.tile([P, 1], F32, name="warm_out")
+        nc.scalar.activation(out=warm_out[:], in_=warm[:], func=ACT.Exp)
+        ident = keep.tile([P, P], F32, name="ident")
+        make_identity(nc, ident[:])
+
+        pos_g = keep.tile([P, N], F32, name="pos_g")
+        seen = keep.tile([P, N], F32, name="seen")
+        bound = keep.tile([P, N], F32, name="bound", tag="q_raw")
+        k_pairs = [keep.tile([P, 2 * T], BF16, name=f"k_pairs{u}", align_bytes=64) for u in range(2)]
+        k_got = keep.tile([P, PACK * N], BF16, name="k_got", tag="k_got", align_bytes=64)
+        k_got_words = k_got[:].bitcast(U32).rearrange("p (s u) -> p s u", u=2)
+        v_pairs = keep.tile([P, 2 * T], BF16, name="v_pairs", align_bytes=64)
+        v_got = keep.tile([P, 2 * N], BF16, name="v_got", align_bytes=64)
+        v_words = v_got[:].bitcast(F32)
+        v_turned = psum.tile([P, PACK, P], F32, name="v_turned")
+        visible = keep.tile([NQ, N], F32, name="visible", tag="visible", align_bytes=64)
+        v_bf = keep.tile([P, DV * PACK], BF16, name="v_bf", tag="visible", align_bytes=64)
+        v_codes = keep.tile([P, DV], U32, name="v_codes", align_bytes=64)
+        v_scales = keep.tile([P, DV], U8, name="v_scales", align_bytes=64)
+        q_bf = keep.tile([P, NQ * PACK], BF16, name="q_bf", align_bytes=64)
+        q_codes = keep.tile([P, NQ], U32, name="q_codes", align_bytes=64)
+        q_scales = keep.tile([P, NQ], U8, name="q_scales", align_bytes=64)
+        k_codes = [keep.tile([P, HALF], U32, name=f"k_codes{h}", align_bytes=64) for h in range(2)]
+        k_scales = [keep.tile([P, HALF], U8, name=f"k_scales{h}", align_bytes=64) for h in range(2)]
+        score = [psum.tile([NQ, HALF], F32, name=f"score{h}") for h in range(2)]
+        vs_g = keep.tile([P, N], F32, name="vs_g", tag="k_got", align_bytes=64)
+        capped = keep.tile([NQ, N], F32, name="capped")
+        neg_max = keep.tile([NQ, 1], F32, name="neg_max")
+        prob = keep.tile([NQ, N], F32, name="prob")
+        sums = [keep.tile([NQ, 1], F32, name=f"row_sum{h}") for h in range(2)]
+        weight = keep.tile([NQ, N], BF16, name="weight", align_bytes=64)
+        w_turned = psum.tile([P, 2, NQ], F32, name="w_turned")
+        w_words = weight[:].bitcast(F32)
+        w_bf = keep.tile([P, NQ * PACK], BF16, name="w_bf", align_bytes=64)
+        w_codes = keep.tile([P, NQ], U32, name="w_codes", align_bytes=64)
+        w_scales = keep.tile([P, NQ], U8, name="w_scales", align_bytes=64)
+        row_sum = keep.tile([NQ, 1], F32, name="row_sum")
+        inverse = keep.tile([NQ, 1], F32, name="inverse")
+        y = psum.tile([NQ, DV], F32, name="y")
+        result = keep.tile([NQ, DV], F32, name="result")
+
+        def cast(engine, pairs, raw, first, a, b):
+            dst = pairs[:, 2 * (first + a) : 2 * (first + b)].rearrange("p (t h) -> p t h", h=2)
+            src = raw[:, :, a:b].rearrange("p h t -> p t h")
+            if engine == "scalar":
+                nc.scalar.copy(out=dst, in_=src)
+            else:
+                nc.vector.tensor_copy(out=dst, in_=src)
+
+        def half(h):
+            return slice(h * HALF, (h + 1) * HALF)
+
+        def mul_scores(h):
+            nc.tensor.matmul_mx(
+                out=score[h][:], lhsT=q_codes[:].bitcast(FP8X4), lhsT_scale=q_scales[:],
+                rhs=k_codes[h][:].bitcast(FP8X4), rhs_scale=k_scales[h][:], start=True, stop=True,
+            )
+
+        def gather_k1(h):
+            nc.vector.tensor_copy(
+                k_got_words[:, half(h), 1],
+                k_pairs[1][:].bitcast(U32).indirect(offsets[:, h * HALF // 16 : (h + 1) * HALF // 16]),
+            )
+
+        def quant_k(h):
+            nc.vector.quantize_mx(out=k_codes[h][:].bitcast(FP8X4), scales=k_scales[h][:], in_=k_got[:, h * PACK * HALF : (h + 1) * PACK * HALF])
+
+        nc.vector.tensor_copy(pos_g[:], pos_pool[:].indirect(offsets[:]))
+        nc.vector.tensor_scalar(out=seen[:], in0=pos_g[:], scalar1=qpos_col[:, 0:1], scalar2=CAP - MASKED, op0=ALU.is_le, op1=ALU.mult)
+        cast("scalar", k_pairs[0], k_raw[0, 0], 0 * CHUNK, 128, 512)
+        cast("vector", k_pairs[0], k_raw[0, 0], 0 * CHUNK, 0, 128)
+        cast("vector", k_pairs[0], k_raw[0, 1], 1 * CHUNK, 0, 384)
+        cast("scalar", k_pairs[0], k_raw[0, 1], 1 * CHUNK, 384, 512)
+        nc.vector.tensor_copy(k_got_words[:, :, 0], k_pairs[0][:].bitcast(U32).indirect(offsets[:]))
+        cast("scalar", k_pairs[1], k_raw[1, 0], 0 * CHUNK, 0, 512)
+        cast("vector", k_pairs[1], k_raw[1, 1], 1 * CHUNK, 0, 384)
+        cast("scalar", k_pairs[1], k_raw[1, 1], 1 * CHUNK, 384, 512)
+        gather_k1(1)
+        nc.scalar.copy(out=q_bf[:].rearrange("p (q j) -> p q j", j=PACK), in_=q_raw[:].rearrange("p j q -> p q j"))
+        nc.scalar.activation(out=bound[:], in_=seen[:], func=ACT.Copy, bias=MASKED)
+        quant_k(1)
+        nc.vector.quantize_mx(out=q_codes[:].bitcast(FP8X4), scales=q_scales[:], in_=q_bf[:])
+        gather_k1(0)
+        quant_k(0)
+        mul_scores(0)
+        mul_scores(1)
+        cast("scalar", v_pairs, v_raw[0], 0 * CHUNK, 0, 512)
+        nc.vector.tensor_copy(vs_g[:], vs_pool[:].indirect(offsets[:]))
+        nc.scalar.activation(out=capped[:, half(0)], in_=score[0][:], func=ACT.Tanh, scale=1.0 / CAP)
+        nc.scalar.activation(out=capped[:, half(1)], in_=score[1][:], func=ACT.Tanh, scale=1.0 / CAP)
+        nc.vector.scalar_tensor_tensor(out=visible[:, half(0)], in0=capped[:, half(0)], scalar=CAP, in1=bound[:, half(0)], op0=ALU.mult, op1=ALU.min)
+        nc.vector.scalar_tensor_tensor(out=visible[:, half(1)], in0=capped[:, half(1)], scalar=CAP, in1=bound[:, half(1)], op0=ALU.mult, op1=ALU.min)
+        nc.vector.tensor_reduce(out=neg_max[:], in_=visible[:], axis=AX.X, op=ALU.max, negate=True)
+        cast("scalar", v_pairs, v_raw[1], 1 * CHUNK, 0, 512)
+        nc.scalar.activation(out=prob[:, half(0)], in_=visible[:, half(0)], func=ACT.Exp, bias=neg_max[:, 0:1], accum_out=sums[0][:])
+        nc.scalar.activation(out=prob[:, half(1)], in_=visible[:, half(1)], func=ACT.Exp, bias=neg_max[:, 0:1], accum_out=sums[1][:])
+        nc.vector.tensor_copy(v_got[:].bitcast(U32).rearrange("p (t s) -> p s t", t=PACK), v_pairs[:].bitcast(U32).indirect(offsets[:]))
+        for t in range(PACK):
+            nc.tensor.transpose(v_turned[:, t, :], v_words[:, t * P : (t + 1) * P], ident[:])
+        nc.vector.tensor_tensor(out=weight[:, half(0)], in0=prob[:, half(0)], in1=vs_g[:, half(0)], op=ALU.mult)
+        nc.vector.tensor_tensor(out=weight[:, half(1)], in0=prob[:, half(1)], in1=vs_g[:, half(1)], op=ALU.mult)
+        for u in range(2):
+            nc.tensor.transpose(w_turned[:, u, :], w_words[:, u::2], ident[:])
+        nc.scalar.copy(
+            out=v_bf[:, 0:512].rearrange("p (e t) -> p e t", t=PACK),
+            in_=v_turned[:].rearrange("p t w -> p (t w)").bitcast(BF16).rearrange("p (t e) -> p e t", t=PACK)[:, 0:128, :],
+        )
+        nc.scalar.copy(
+            out=v_bf[:, 512:1024].rearrange("p (e t) -> p e t", t=PACK),
+            in_=v_turned[:].rearrange("p t w -> p (t w)").bitcast(BF16).rearrange("p (t e) -> p e t", t=PACK)[:, 128:256, :],
+        )
+        nc.vector.tensor_copy(out=w_bf[:].bitcast(F32).rearrange("p (q u) -> p q u", u=2), in_=w_turned[:].rearrange("p u q -> p q u"))
+        nc.vector.quantize_mx(out=w_codes[:].bitcast(FP8X4), scales=w_scales[:], in_=w_bf[:])
+        nc.vector.quantize_mx(out=v_codes[:, 0:128].bitcast(FP8X4), scales=v_scales[:, 0:128], in_=v_bf[:, 0:512])
+        nc.vector.quantize_mx(out=v_codes[:, 128:256].bitcast(FP8X4), scales=v_scales[:, 128:256], in_=v_bf[:, 512:1024])
+        nc.vector.tensor_tensor(out=row_sum[:], in0=sums[0][:], in1=sums[1][:], op=ALU.add)
+        nc.vector.reciprocal(out=inverse[:], in_=row_sum[:])
+        nc.tensor.matmul_mx(
+            out=y[:], lhsT=w_codes[:].bitcast(FP8X4), lhsT_scale=w_scales[:],
+            rhs=v_codes[:].bitcast(FP8X4), rhs_scale=v_scales[:], start=True, stop=True,
+        )
+        nc.vector.tensor_scalar(out=result[:], in0=y[:], scalar1=inverse[:, 0:1], scalar2=None, op0=ALU.mult)
+        nc.sync.dma_start(out=out.rearrange("b q e -> (b q) e"), in_=result[:])

@@ -7,11 +7,14 @@ D, T, N, DV, NQ = 512, 1024, 512, 256, 128
 CAP = 2.0
 MASKED = -30000.0
 FLOPS = 2 * D * NQ * N + 2 * N * NQ * DV
+BYTES = 4 * (D * T + DV * T + D * NQ + 2 * T + NQ + NQ * DV) + 2 * 128 * N // 16
 
 P = 128
 PACK = 4
 HALF = N // 2
 CHUNK = T // 2
+SHARE1 = 256
+EARLY = 384
 
 F32 = mybir.dt.float32
 BF16 = mybir.dt.bfloat16
@@ -21,7 +24,6 @@ U8 = mybir.dt.uint8
 FP8X4 = mybir.dt.float8_e4m3fn_x4
 ALU = mybir.AluOpType
 ACT = mybir.ActivationFunctionType
-AX = mybir.AxisListType
 
 
 def tile_attend_x_draft_cap_topk_kernel(tc, qT, kT, vT, vs, pos, qpos, offs, out):
@@ -34,29 +36,24 @@ def tile_attend_x_draft_cap_topk_kernel(tc, qT, kT, vT, vs, pos, qpos, offs, out
         qpos_col = keep.tile([P, 1], F32, name="qpos_col")
         pos_pool = keep.tile([P, T], F32, name="pos_pool")
         vs_pool = keep.tile([P, T], F32, name="vs_pool")
-        q_raw = keep.tile([P, PACK, NQ], F32, name="q_raw", tag="q_raw")
+        q_raw = keep.tile([P, PACK, NQ], F32, name="q_raw", tag="q_raw", align_bytes=64)
         k_rows = kT.rearrange("(p j) t -> p j t", j=PACK)
-        v_rows = vT.rearrange("(p h) t -> p h t", h=2)
-        k_raw = {(u, c): keep.tile([P, 2, CHUNK], F32, name=f"k_raw{u}{c}") for u in range(2) for c in range(2)}
-        v_raw = [keep.tile([P, 2, CHUNK], F32, name=f"v_raw{c}") for c in range(2)]
+        k_raw = {(u, c): keep.tile([P, 2, CHUNK], F32, name=f"k_raw{u}{c}", tag=f"raw{u}{c}", align_bytes=64) for u in range(2) for c in range(2)}
 
         def load_k(u, c):
             nc.sync.dma_start(out=k_raw[u, c][:], in_=k_rows[:, 2 * u : 2 * u + 2, c * CHUNK : (c + 1) * CHUNK])
 
-        def load_v(c):
-            nc.sync.dma_start(out=v_raw[c][:], in_=v_rows[:, :, c * CHUNK : (c + 1) * CHUNK])
-
-        nc.sync.dma_start(out=pos_pool[:], in_=pos)
-        nc.sync.dma_start(offsets[:], offs)
+        nc.vector.memset(pos_pool[:], 0.0)
+        nc.vector.memset(vs_pool[:], 0.0)
         load_k(0, 0)
+        nc.sync.dma_start(offsets[:], offs)
+        nc.sync.dma_start(out=qpos_col[:], in_=qpos.rearrange("b q o -> (b q) o"))
+        nc.sync.dma_start(out=pos_pool[0:1, :], in_=pos[0:1, :])
         load_k(0, 1)
+        nc.sync.dma_start(out=vs_pool[0:1, :], in_=vs[0:1, :])
         load_k(1, 0)
         load_k(1, 1)
-        nc.sync.dma_start(out=qpos_col[:], in_=qpos.rearrange("b q o -> (b q) o"))
         nc.sync.dma_start(out=q_raw[:], in_=qT.rearrange("b (p j) q -> p (b j) q", j=PACK))
-        load_v(0)
-        nc.sync.dma_start(out=vs_pool[:], in_=vs)
-        load_v(1)
 
         warm = keep.tile([P, 1], F32, name="warm")
         nc.gpsimd.memset(warm[:], 0.0)
@@ -65,45 +62,14 @@ def tile_attend_x_draft_cap_topk_kernel(tc, qT, kT, vT, vs, pos, qpos, offs, out
         ident = keep.tile([P, P], F32, name="ident")
         make_identity(nc, ident[:])
 
-        pos_g = keep.tile([P, N], F32, name="pos_g")
-        seen = keep.tile([P, N], F32, name="seen")
-        bound = keep.tile([P, N], F32, name="bound", tag="q_raw")
         k_pairs = [keep.tile([P, 2 * T], BF16, name=f"k_pairs{u}", align_bytes=64) for u in range(2)]
         k_got = keep.tile([P, PACK * N], BF16, name="k_got", tag="k_got", align_bytes=64)
-        k_got_words = k_got[:].bitcast(U32).rearrange("p (s u) -> p s u", u=2)
-        v_pairs = keep.tile([P, 2 * T], BF16, name="v_pairs", align_bytes=64)
-        v_got = keep.tile([P, 2 * N], BF16, name="v_got", align_bytes=64)
-        v_words = v_got[:].bitcast(F32)
-        v_turned = psum.tile([P, PACK, P], F32, name="v_turned")
-        visible = keep.tile([NQ, N], F32, name="visible", tag="visible", align_bytes=64)
-        v_bf = keep.tile([P, DV * PACK], BF16, name="v_bf", tag="visible", align_bytes=64)
-        v_codes = keep.tile([P, DV], U32, name="v_codes", align_bytes=64)
-        v_scales = keep.tile([P, DV], U8, name="v_scales", align_bytes=64)
-        q_bf = keep.tile([P, NQ * PACK], BF16, name="q_bf", align_bytes=64)
-        q_codes = keep.tile([P, NQ], U32, name="q_codes", align_bytes=64)
-        q_scales = keep.tile([P, NQ], U8, name="q_scales", align_bytes=64)
-        k_codes = [keep.tile([P, HALF], U32, name=f"k_codes{h}", align_bytes=64) for h in range(2)]
-        k_scales = [keep.tile([P, HALF], U8, name=f"k_scales{h}", align_bytes=64) for h in range(2)]
-        score = [psum.tile([NQ, HALF], F32, name=f"score{h}") for h in range(2)]
-        vs_g = keep.tile([P, N], F32, name="vs_g", tag="k_got", align_bytes=64)
-        capped = keep.tile([NQ, N], F32, name="capped")
-        neg_max = keep.tile([NQ, 1], F32, name="neg_max")
-        prob = keep.tile([NQ, N], F32, name="prob")
-        sums = [keep.tile([NQ, 1], F32, name=f"row_sum{h}") for h in range(2)]
-        weight = keep.tile([NQ, N], BF16, name="weight", align_bytes=64)
-        w_turned = psum.tile([P, 2, NQ], F32, name="w_turned")
-        w_words = weight[:].bitcast(F32)
-        w_bf = keep.tile([P, NQ * PACK], BF16, name="w_bf", align_bytes=64)
-        w_codes = keep.tile([P, NQ], U32, name="w_codes", align_bytes=64)
-        w_scales = keep.tile([P, NQ], U8, name="w_scales", align_bytes=64)
-        row_sum = keep.tile([NQ, 1], F32, name="row_sum")
-        inverse = keep.tile([NQ, 1], F32, name="inverse")
-        y = psum.tile([NQ, DV], F32, name="y")
-        result = keep.tile([NQ, DV], F32, name="result")
+        k_got_words = k_got[:].bitcast(U32).rearrange("p (t s u) -> p s t u", t=PACK, u=2)
 
-        def cast(engine, pairs, raw, first, a, b):
-            dst = pairs[:, 2 * (first + a) : 2 * (first + b)].rearrange("p (t h) -> p t h", h=2)
-            src = raw[:, :, a:b].rearrange("p h t -> p t h")
+        def cast(engine, u, c, a, b):
+            first = c * CHUNK
+            dst = k_pairs[u][:, 2 * (first + a) : 2 * (first + b)].rearrange("p (t h) -> p t h", h=2)
+            src = k_raw[u, c][:, :, a:b].rearrange("p h t -> p t h")
             if engine == "scalar":
                 nc.scalar.copy(out=dst, in_=src)
             else:
@@ -112,74 +78,131 @@ def tile_attend_x_draft_cap_topk_kernel(tc, qT, kT, vT, vs, pos, qpos, offs, out
         def half(h):
             return slice(h * HALF, (h + 1) * HALF)
 
-        def mul_scores(h):
+        def gather_k(u):
+            nc.vector.tensor_copy(k_got_words[:, :, :, u], k_pairs[u][:].bitcast(U32).indirect(offsets[:]))
+
+        def to_columns(name, row, turned_tag, column_tag):
+            turned = psum.tile([P, PACK, P], F32, name=f"{name}_turned", tag=turned_tag)
+            for t in range(PACK):
+                nc.tensor.transpose(turned[:, t, :], row[:, t::PACK], ident[:])
+            columns = keep.tile([P, PACK], F32, name=f"{name}_columns", tag=column_tag, align_bytes=64)
+            return turned, columns
+
+        pos_g = keep.tile([P, N], F32, name="pos_g")
+        vs_g = keep.tile([P, N], F32, name="vs_g")
+        nc.vector.tensor_copy(pos_g[:], pos_pool[:].indirect(offsets[:]))
+        nc.vector.tensor_copy(vs_g[:], vs_pool[:].indirect(offsets[:]))
+        pos_turned, pos_columns = to_columns("pos", pos_g, "bank_a", "raw10")
+
+        cast("scalar", 0, 0, 0, CHUNK)
+        cast("scalar", 0, 1, 0, CHUNK)
+        v_raw = [keep.tile([P, T], F32, name=f"v_raw{h}", tag=f"raw0{h}", align_bytes=64) for h in range(2)]
+        for h in range(2):
+            nc.sync.dma_start(out=v_raw[h][:], in_=vT[h * P : (h + 1) * P, :])
+        gather_k(0)
+        cast("scalar", 1, 0, 0, CHUNK)
+        nc.scalar.copy(out=pos_columns[:], in_=pos_turned[:, :, 0])
+        pos_spread = psum.tile([NQ, PACK, P], F32, name="pos_spread")
+        for t in range(PACK):
+            nc.tensor.transpose(pos_spread[:, t, :], pos_columns[:, t : t + 1].to_broadcast([P, P]), ident[:])
+        cast("vector", 1, 1, 0, SHARE1)
+        cast("scalar", 1, 1, SHARE1, CHUNK)
+        gather_k(1)
+
+        q_bf = keep.tile([P, NQ * PACK], BF16, name="q_bf", tag="q_bf", align_bytes=64)
+        q_codes = keep.tile([P, NQ], U32, name="q_codes", align_bytes=64)
+        q_scales = keep.tile([P, NQ], U8, name="q_scales", align_bytes=64)
+        nc.scalar.copy(out=q_bf[:].rearrange("p (q j) -> p q j", j=PACK), in_=q_raw[:].rearrange("p j q -> p q j"))
+        nc.vector.quantize_mx(out=q_codes[:].bitcast(FP8X4), scales=q_scales[:], in_=q_bf[:])
+
+        side = keep.tile([NQ, N], F32, name="side", tag="raw11", align_bytes=64)
+        bound = keep.tile([NQ, N], F32, name="bound")
+        nc.scalar.activation(out=side[:], in_=pos_spread[:].rearrange("p t s -> p (t s)"), func=ACT.Sign, scale=-1.0, bias=qpos_col[:, 0:1])
+        nc.scalar.activation(out=bound[:], in_=side[:], func=ACT.Copy, scale=1.0 - MASKED / CAP, bias=1.0)
+
+        k_codes = keep.tile([P, N], U32, name="k_codes", tag="q_raw", align_bytes=64)
+        k_scales = [keep.tile([P, HALF], U8, name=f"k_scales{h}", align_bytes=64) for h in range(2)]
+        score = [psum.tile([NQ, HALF], F32, name=f"score{h}", tag=f"score{h}") for h in range(2)]
+        capped0 = keep.tile([NQ, HALF], F32, name="capped0", tag="raw11", align_bytes=64)
+        shared = keep.tile([P, EARLY // 2 + HALF], F32, name="shared", tag="k_got", align_bytes=64)
+        capped = [capped0[:], shared[:, EARLY // 2 :]]
+        for h in range(2):
+            nc.vector.quantize_mx(out=k_codes[:, half(h)].bitcast(FP8X4), scales=k_scales[h][:], in_=k_got[:, h * PACK * HALF : (h + 1) * PACK * HALF])
+        for h in range(2):
             nc.tensor.matmul_mx(
                 out=score[h][:], lhsT=q_codes[:].bitcast(FP8X4), lhsT_scale=q_scales[:],
-                rhs=k_codes[h][:].bitcast(FP8X4), rhs_scale=k_scales[h][:], start=True, stop=True,
+                rhs=k_codes[:, half(h)].bitcast(FP8X4), rhs_scale=k_scales[h][:], start=True, stop=True,
+            )
+        for h in range(2):
+            nc.scalar.activation(out=capped[h], in_=score[h][:], func=ACT.Tanh, scale=1.0 / CAP)
+
+        v_codes = keep.tile([P, DV], U32, name="v_codes", align_bytes=64)
+        v_scales = keep.tile([P, DV], U8, name="v_scales", align_bytes=64)
+
+        def gather_v(h, got, a, b):
+            nc.vector.tensor_copy(got.bitcast(BF16)[:, a:b], v_raw[h][:].indirect(offsets[:, a // 16 : b // 16]))
+
+        def turn_v(h, got, tag):
+            turned = psum.tile([P, 2, P], F32, name=f"v_turned{h}", tag=tag)
+            for u in range(2):
+                nc.tensor.transpose(turned[:, u, :], got[:, u::2], ident[:])
+            nc.scalar.copy(
+                out=v_bf[:, h * PACK * P : (h + 1) * PACK * P].bitcast(F32).rearrange("p (e u) -> p e u", u=2),
+                in_=turned[:].rearrange("p u e -> p e u"),
             )
 
-        def gather_k1(h):
-            nc.vector.tensor_copy(
-                k_got_words[:, half(h), 1],
-                k_pairs[1][:].bitcast(U32).indirect(offsets[:, h * HALF // 16 : (h + 1) * HALF // 16]),
+        def quant_v(h):
+            nc.vector.quantize_mx(
+                out=v_codes[:, h * P : (h + 1) * P].bitcast(FP8X4), scales=v_scales[:, h * P : (h + 1) * P],
+                in_=v_bf[:, h * PACK * P : (h + 1) * PACK * P],
             )
 
-        def quant_k(h):
-            nc.vector.quantize_mx(out=k_codes[h][:].bitcast(FP8X4), scales=k_scales[h][:], in_=k_got[:, h * PACK * HALF : (h + 1) * PACK * HALF])
+        v_got0 = shared[:, 0:HALF]
+        gather_v(0, v_got0, 0, EARLY)
+        visible = keep.tile([NQ, N], F32, name="visible", tag="visible", align_bytes=64)
+        for h in range(2):
+            nc.vector.tensor_tensor(out=visible[:, half(h)], in0=capped[h], in1=bound[:, half(h)], op=ALU.min)
+        vs_turned, vs_columns = to_columns("vs", vs_g, "bank_b", "raw11")
+        nc.scalar.copy(out=vs_columns[:], in_=vs_turned[:, :, 0])
+        negated = keep.tile([NQ, N], F32, name="negated", tag="negated", align_bytes=64)
+        neg_max = keep.tile([NQ, 1], F32, name="neg_max")
+        nc.vector.tensor_scalar(out=negated[:], in0=visible[:], scalar1=-CAP, scalar2=None, op0=ALU.mult, op1=ALU.min, accum_out=neg_max[:])
 
-        nc.vector.tensor_copy(pos_g[:], pos_pool[:].indirect(offsets[:]))
-        nc.vector.tensor_scalar(out=seen[:], in0=pos_g[:], scalar1=qpos_col[:, 0:1], scalar2=CAP - MASKED, op0=ALU.is_le, op1=ALU.mult)
-        cast("scalar", k_pairs[0], k_raw[0, 0], 0 * CHUNK, 128, 512)
-        cast("vector", k_pairs[0], k_raw[0, 0], 0 * CHUNK, 0, 128)
-        cast("vector", k_pairs[0], k_raw[0, 1], 1 * CHUNK, 0, 384)
-        cast("scalar", k_pairs[0], k_raw[0, 1], 1 * CHUNK, 384, 512)
-        nc.vector.tensor_copy(k_got_words[:, :, 0], k_pairs[0][:].bitcast(U32).indirect(offsets[:]))
-        cast("scalar", k_pairs[1], k_raw[1, 0], 0 * CHUNK, 0, 512)
-        cast("vector", k_pairs[1], k_raw[1, 1], 1 * CHUNK, 0, 384)
-        cast("scalar", k_pairs[1], k_raw[1, 1], 1 * CHUNK, 384, 512)
-        gather_k1(1)
-        nc.scalar.copy(out=q_bf[:].rearrange("p (q j) -> p q j", j=PACK), in_=q_raw[:].rearrange("p j q -> p q j"))
-        nc.scalar.activation(out=bound[:], in_=seen[:], func=ACT.Copy, bias=MASKED)
-        quant_k(1)
-        nc.vector.quantize_mx(out=q_codes[:].bitcast(FP8X4), scales=q_scales[:], in_=q_bf[:])
-        gather_k1(0)
-        quant_k(0)
-        mul_scores(0)
-        mul_scores(1)
-        cast("scalar", v_pairs, v_raw[0], 0 * CHUNK, 0, 512)
-        nc.vector.tensor_copy(vs_g[:], vs_pool[:].indirect(offsets[:]))
-        nc.scalar.activation(out=capped[:, half(0)], in_=score[0][:], func=ACT.Tanh, scale=1.0 / CAP)
-        nc.scalar.activation(out=capped[:, half(1)], in_=score[1][:], func=ACT.Tanh, scale=1.0 / CAP)
-        nc.vector.scalar_tensor_tensor(out=visible[:, half(0)], in0=capped[:, half(0)], scalar=CAP, in1=bound[:, half(0)], op0=ALU.mult, op1=ALU.min)
-        nc.vector.scalar_tensor_tensor(out=visible[:, half(1)], in0=capped[:, half(1)], scalar=CAP, in1=bound[:, half(1)], op0=ALU.mult, op1=ALU.min)
-        nc.vector.tensor_reduce(out=neg_max[:], in_=visible[:], axis=AX.X, op=ALU.max, negate=True)
-        cast("scalar", v_pairs, v_raw[1], 1 * CHUNK, 0, 512)
-        nc.scalar.activation(out=prob[:, half(0)], in_=visible[:, half(0)], func=ACT.Exp, bias=neg_max[:, 0:1], accum_out=sums[0][:])
-        nc.scalar.activation(out=prob[:, half(1)], in_=visible[:, half(1)], func=ACT.Exp, bias=neg_max[:, 0:1], accum_out=sums[1][:])
-        nc.vector.tensor_copy(v_got[:].bitcast(U32).rearrange("p (t s) -> p s t", t=PACK), v_pairs[:].bitcast(U32).indirect(offsets[:]))
+        gather_v(0, v_got0, EARLY, N)
+        prob = keep.tile([NQ, N], F32, name="prob")
+        sums = [keep.tile([NQ, 1], F32, name=f"row_sum{h}") for h in range(2)]
+        p_turned = psum.tile([P, PACK, NQ], F32, name="p_turned")
+        for h in range(2):
+            nc.scalar.activation(out=prob[:, half(h)], in_=negated[:, half(h)], func=ACT.Exp, scale=-1.0, bias=neg_max[:, 0:1], accum_out=sums[h][:])
         for t in range(PACK):
-            nc.tensor.transpose(v_turned[:, t, :], v_words[:, t * P : (t + 1) * P], ident[:])
-        nc.vector.tensor_tensor(out=weight[:, half(0)], in0=prob[:, half(0)], in1=vs_g[:, half(0)], op=ALU.mult)
-        nc.vector.tensor_tensor(out=weight[:, half(1)], in0=prob[:, half(1)], in1=vs_g[:, half(1)], op=ALU.mult)
-        for u in range(2):
-            nc.tensor.transpose(w_turned[:, u, :], w_words[:, u::2], ident[:])
-        nc.scalar.copy(
-            out=v_bf[:, 0:512].rearrange("p (e t) -> p e t", t=PACK),
-            in_=v_turned[:].rearrange("p t w -> p (t w)").bitcast(BF16).rearrange("p (t e) -> p e t", t=PACK)[:, 0:128, :],
+            nc.tensor.transpose(p_turned[:, t, :], prob[:, t * P : (t + 1) * P], ident[:])
+        v_got1 = visible[:, 0:HALF]
+        gather_v(1, v_got1, 0, N)
+        v_bf = keep.tile([P, DV * PACK], BF16, name="v_bf", tag="negated", align_bytes=64)
+        turn_v(0, v_got0, "score1")
+        turn_v(1, v_got1, "score1")
+
+        w_bf = keep.tile([P, NQ * PACK], BF16, name="w_bf", align_bytes=64)
+        w_codes = keep.tile([P, NQ], U32, name="w_codes", align_bytes=64)
+        w_scales = keep.tile([P, NQ], U8, name="w_scales", align_bytes=64)
+        row_sum = keep.tile([NQ, 1], F32, name="row_sum")
+        inverse = keep.tile([NQ, 1], F32, name="inverse")
+        nc.vector.tensor_tensor(
+            out=w_bf[:].rearrange("p (q t) -> p q t", t=PACK), in0=p_turned[:].rearrange("p t q -> p q t"),
+            in1=vs_columns[:].unsqueeze(1).to_broadcast([P, NQ, PACK]), op=ALU.mult,
         )
-        nc.scalar.copy(
-            out=v_bf[:, 512:1024].rearrange("p (e t) -> p e t", t=PACK),
-            in_=v_turned[:].rearrange("p t w -> p (t w)").bitcast(BF16).rearrange("p (t e) -> p e t", t=PACK)[:, 128:256, :],
-        )
-        nc.vector.tensor_copy(out=w_bf[:].bitcast(F32).rearrange("p (q u) -> p q u", u=2), in_=w_turned[:].rearrange("p u q -> p q u"))
-        nc.vector.quantize_mx(out=w_codes[:].bitcast(FP8X4), scales=w_scales[:], in_=w_bf[:])
-        nc.vector.quantize_mx(out=v_codes[:, 0:128].bitcast(FP8X4), scales=v_scales[:, 0:128], in_=v_bf[:, 0:512])
-        nc.vector.quantize_mx(out=v_codes[:, 128:256].bitcast(FP8X4), scales=v_scales[:, 128:256], in_=v_bf[:, 512:1024])
         nc.vector.tensor_tensor(out=row_sum[:], in0=sums[0][:], in1=sums[1][:], op=ALU.add)
+        quant_v(0)
+        nc.vector.quantize_mx(out=w_codes[:].bitcast(FP8X4), scales=w_scales[:], in_=w_bf[:])
+        quant_v(1)
         nc.vector.reciprocal(out=inverse[:], in_=row_sum[:])
-        nc.tensor.matmul_mx(
-            out=y[:], lhsT=w_codes[:].bitcast(FP8X4), lhsT_scale=w_scales[:],
-            rhs=v_codes[:].bitcast(FP8X4), rhs_scale=v_scales[:], start=True, stop=True,
-        )
-        nc.vector.tensor_scalar(out=result[:], in0=y[:], scalar1=inverse[:, 0:1], scalar2=None, op0=ALU.mult)
+        result = keep.tile([NQ, DV], F32, name="result")
+        for h, tag in enumerate(("bank_a", "bank_b")):
+            cols = slice(h * P, (h + 1) * P)
+            y = psum.tile([NQ, P], F32, name=f"y{h}", tag=tag)
+            nc.tensor.matmul_mx(
+                out=y[:], lhsT=w_codes[:].bitcast(FP8X4), lhsT_scale=w_scales[:],
+                rhs=v_codes[:, cols].bitcast(FP8X4), rhs_scale=v_scales[:, cols], start=True, stop=True,
+            )
+            nc.vector.tensor_scalar(out=result[:, cols], in0=y[:], scalar1=inverse[:, 0:1], scalar2=None, op0=ALU.mult)
         nc.sync.dma_start(out=out.rearrange("b q e -> (b q) e"), in_=result[:])

@@ -19,6 +19,7 @@ EARLY = 384
 F32 = mybir.dt.float32
 BF16 = mybir.dt.bfloat16
 U32 = mybir.dt.uint32
+I32 = mybir.dt.int32
 U16 = mybir.dt.uint16
 U8 = mybir.dt.uint8
 FP8X4 = mybir.dt.float8_e4m3fn_x4
@@ -64,7 +65,7 @@ def tile_attend_x_draft_cap_topk_kernel(tc, qT, kT, vT, vs, pos, qpos, offs, out
 
         k_pairs = [keep.tile([P, 2 * T], BF16, name=f"k_pairs{u}", align_bytes=64) for u in range(2)]
         k_got = keep.tile([P, PACK * N], BF16, name="k_got", tag="k_got", align_bytes=64)
-        k_got_words = k_got[:].bitcast(U32).rearrange("p (t s u) -> p s t u", t=PACK, u=2)
+        k_planes = keep.tile([P, 2 * N], U32, name="k_planes", align_bytes=64)
 
         def cast(engine, u, c, a, b):
             first = c * CHUNK
@@ -79,7 +80,7 @@ def tile_attend_x_draft_cap_topk_kernel(tc, qT, kT, vT, vs, pos, qpos, offs, out
             return slice(h * HALF, (h + 1) * HALF)
 
         def gather_k(u):
-            nc.vector.tensor_copy(k_got_words[:, :, :, u], k_pairs[u][:].bitcast(U32).indirect(offsets[:]))
+            nc.vector.tensor_copy(k_planes[:, u * N : (u + 1) * N].rearrange("p (t s) -> p s t", t=PACK), k_pairs[u][:].bitcast(U32).indirect(offsets[:]))
 
         def to_columns(name, row, turned_tag, column_tag):
             turned = psum.tile([P, PACK, P], F32, name=f"{name}_turned", tag=turned_tag)
@@ -115,6 +116,11 @@ def tile_attend_x_draft_cap_topk_kernel(tc, qT, kT, vT, vs, pos, qpos, offs, out
         nc.scalar.copy(out=q_bf[:].rearrange("p (q j) -> p q j", j=PACK), in_=q_raw[:].rearrange("p j q -> p q j"))
         nc.vector.quantize_mx(out=q_codes[:].bitcast(FP8X4), scales=q_scales[:], in_=q_bf[:])
 
+        for h in range(2):
+            nc.vector.tensor_copy(
+                out=k_got[:].bitcast(I32)[:, h * N : (h + 1) * N].rearrange("p (c u) -> p c u", u=2),
+                in_=k_planes[:].bitcast(I32).rearrange("p (u c) -> p c u", u=2)[:, half(h), :],
+            )
         side = keep.tile([NQ, N], F32, name="side", tag="raw11", align_bytes=64)
         bound = keep.tile([NQ, N], F32, name="bound")
         nc.scalar.activation(out=side[:], in_=pos_spread[:].rearrange("p t s -> p (t s)"), func=ACT.Sign, scale=-1.0, bias=qpos_col[:, 0:1])

@@ -13,7 +13,9 @@ P = 128
 PACK = 4
 HALF = N // 2
 CHUNK = T // 2
-SHARE1 = 256
+PIECES = (((0, T // 4), (T // 4, T // 2), (T // 2, T)), ((0, T // 2), (T // 2, T)))
+SHARE0 = 128
+SHARE1 = 320
 EARLY = 384
 
 F32 = mybir.dt.float32
@@ -39,10 +41,14 @@ def tile_attend_x_draft_cap_topk_kernel(tc, qT, kT, vT, vs, pos, qpos, offs, out
         vs_pool = keep.tile([P, T], F32, name="vs_pool")
         q_raw = keep.tile([P, PACK, NQ], F32, name="q_raw", tag="q_raw", align_bytes=64)
         k_rows = kT.rearrange("(p j) t -> p j t", j=PACK)
-        k_raw = {(u, c): keep.tile([P, 2, CHUNK], F32, name=f"k_raw{u}{c}", tag=f"raw{u}{c}", align_bytes=64) for u in range(2) for c in range(2)}
+        k_raw = {
+            (u, c): keep.tile([P, 2, b - a], F32, name=f"k_raw{u}{c}", tag=f"raw{u}{c}", align_bytes=64)
+            for u in range(2) for c, (a, b) in enumerate(PIECES[u])
+        }
 
         def load_k(u, c):
-            nc.sync.dma_start(out=k_raw[u, c][:], in_=k_rows[:, 2 * u : 2 * u + 2, c * CHUNK : (c + 1) * CHUNK])
+            a, b = PIECES[u][c]
+            nc.sync.dma_start(out=k_raw[u, c][:], in_=k_rows[:, 2 * u : 2 * u + 2, a:b])
 
         nc.vector.memset(pos_pool[:], 0.0)
         nc.vector.memset(vs_pool[:], 0.0)
@@ -52,6 +58,7 @@ def tile_attend_x_draft_cap_topk_kernel(tc, qT, kT, vT, vs, pos, qpos, offs, out
         nc.sync.dma_start(out=pos_pool[0:1, :], in_=pos[0:1, :])
         load_k(0, 1)
         nc.sync.dma_start(out=vs_pool[0:1, :], in_=vs[0:1, :])
+        load_k(0, 2)
         load_k(1, 0)
         load_k(1, 1)
         nc.sync.dma_start(out=q_raw[:], in_=qT.rearrange("b (p j) q -> p (b j) q", j=PACK))
@@ -61,14 +68,15 @@ def tile_attend_x_draft_cap_topk_kernel(tc, qT, kT, vT, vs, pos, qpos, offs, out
         warm_out = keep.tile([P, 1], F32, name="warm_out")
         nc.scalar.activation(out=warm_out[:], in_=warm[:], func=ACT.Exp)
         ident = keep.tile([P, P], F32, name="ident")
-        make_identity(nc, ident[:])
+        nc.vector.memset(ident[:], 0.0)
+        make_identity(nc, ident[:], nomemset=True)
 
         k_pairs = [keep.tile([P, 2 * T], BF16, name=f"k_pairs{u}", align_bytes=64) for u in range(2)]
         k_got = keep.tile([P, PACK * N], BF16, name="k_got", tag="k_got", align_bytes=64)
         k_planes = keep.tile([P, 2 * N], U32, name="k_planes", align_bytes=64)
 
         def cast(engine, u, c, a, b):
-            first = c * CHUNK
+            first = PIECES[u][c][0]
             dst = k_pairs[u][:, 2 * (first + a) : 2 * (first + b)].rearrange("p (t h) -> p t h", h=2)
             src = k_raw[u, c][:, :, a:b].rearrange("p h t -> p t h")
             if engine == "scalar":
@@ -93,19 +101,21 @@ def tile_attend_x_draft_cap_topk_kernel(tc, qT, kT, vT, vs, pos, qpos, offs, out
         vs_g = keep.tile([P, N], F32, name="vs_g")
         nc.vector.tensor_copy(pos_g[:], pos_pool[:].indirect(offsets[:]))
         nc.vector.tensor_copy(vs_g[:], vs_pool[:].indirect(offsets[:]))
-        pos_turned, pos_columns = to_columns("pos", pos_g, "bank_a", "raw10")
+        pos_turned, pos_columns = to_columns("pos", pos_g, "bank_a", "raw02")
 
-        cast("scalar", 0, 0, 0, CHUNK)
-        cast("scalar", 0, 1, 0, CHUNK)
+        cast("scalar", 0, 0, 0, CHUNK // 2)
+        cast("scalar", 0, 1, 0, CHUNK // 2)
+        cast("vector", 0, 2, 0, SHARE0)
+        cast("scalar", 0, 2, SHARE0, CHUNK)
         v_raw = [keep.tile([P, T], F32, name=f"v_raw{h}", tag=f"raw0{h}", align_bytes=64) for h in range(2)]
         for h in range(2):
             nc.sync.dma_start(out=v_raw[h][:], in_=vT[h * P : (h + 1) * P, :])
         gather_k(0)
-        cast("scalar", 1, 0, 0, CHUNK)
         nc.scalar.copy(out=pos_columns[:], in_=pos_turned[:, :, 0])
         pos_spread = psum.tile([NQ, PACK, P], F32, name="pos_spread")
         for t in range(PACK):
             nc.tensor.transpose(pos_spread[:, t, :], pos_columns[:, t : t + 1].to_broadcast([P, P]), ident[:])
+        cast("scalar", 1, 0, 0, CHUNK)
         cast("vector", 1, 1, 0, SHARE1)
         cast("scalar", 1, 1, SHARE1, CHUNK)
         gather_k(1)

@@ -16,7 +16,6 @@ CHUNK = T // 2
 PIECES = (((0, T // 4), (T // 4, T // 2), (T // 2, T)), ((0, T // 2), (T // 2, T)))
 SHARE0 = 128
 SHARE1 = 320
-EARLY = 384
 
 F32 = mybir.dt.float32
 BF16 = mybir.dt.bfloat16
@@ -54,7 +53,6 @@ def tile_attend_x_draft_cap_topk_kernel(tc, qT, kT, vT, vs, pos, qpos, offs, out
         nc.vector.memset(vs_pool[:], 0.0)
         load_k(0, 0)
         nc.sync.dma_start(offsets[:], offs)
-        nc.sync.dma_start(out=qpos_col[:], in_=qpos.rearrange("b q o -> (b q) o"))
         nc.sync.dma_start(out=pos_pool[0:1, :], in_=pos[0:1, :])
         load_k(0, 1)
         nc.sync.dma_start(out=vs_pool[0:1, :], in_=vs[0:1, :])
@@ -62,6 +60,7 @@ def tile_attend_x_draft_cap_topk_kernel(tc, qT, kT, vT, vs, pos, qpos, offs, out
         load_k(1, 0)
         load_k(1, 1)
         nc.sync.dma_start(out=q_raw[:], in_=qT.rearrange("b (p j) q -> p (b j) q", j=PACK))
+        nc.sync.dma_start(out=qpos_col[:], in_=qpos.rearrange("b q o -> (b q) o"))
 
         warm = keep.tile([P, 1], F32, name="warm")
         nc.gpsimd.memset(warm[:], 0.0)
@@ -132,16 +131,16 @@ def tile_attend_x_draft_cap_topk_kernel(tc, qT, kT, vT, vs, pos, qpos, offs, out
                 in_=k_planes[:].bitcast(I32).rearrange("p (u c) -> p c u", u=2)[:, half(h), :],
             )
         side = keep.tile([NQ, N], F32, name="side", tag="raw11", align_bytes=64)
-        bound = keep.tile([NQ, N], F32, name="bound")
+        bound = keep.tile([NQ, N], F32, name="bound", tag="bound1", align_bytes=64)
         nc.scalar.activation(out=side[:], in_=pos_spread[:].rearrange("p t s -> p (t s)"), func=ACT.Sign, scale=-1.0, bias=qpos_col[:, 0:1])
         nc.scalar.activation(out=bound[:], in_=side[:], func=ACT.Copy, scale=1.0 - MASKED / CAP, bias=1.0)
 
         k_codes = keep.tile([P, N], U32, name="k_codes", tag="q_raw", align_bytes=64)
         k_scales = [keep.tile([P, HALF], U8, name=f"k_scales{h}", align_bytes=64) for h in range(2)]
         score = [psum.tile([NQ, HALF], F32, name=f"score{h}", tag=f"score{h}") for h in range(2)]
-        capped0 = keep.tile([NQ, HALF], F32, name="capped0", tag="raw11", align_bytes=64)
-        shared = keep.tile([P, EARLY // 2 + HALF], F32, name="shared", tag="k_got", align_bytes=64)
-        capped = [capped0[:], shared[:, EARLY // 2 :]]
+        v1_pool = keep.tile([P, T], BF16, name="v1_pool", tag="raw11", align_bytes=64)
+        nc.scalar.copy(out=v1_pool[:], in_=v_raw[1][:])
+        capped = keep.tile([NQ, N], F32, name="capped", tag="raw01", align_bytes=64)
         for h in range(2):
             nc.vector.quantize_mx(out=k_codes[:, half(h)].bitcast(FP8X4), scales=k_scales[h][:], in_=k_got[:, h * PACK * HALF : (h + 1) * PACK * HALF])
         for h in range(2):
@@ -149,68 +148,57 @@ def tile_attend_x_draft_cap_topk_kernel(tc, qT, kT, vT, vs, pos, qpos, offs, out
                 out=score[h][:], lhsT=q_codes[:].bitcast(FP8X4), lhsT_scale=q_scales[:],
                 rhs=k_codes[:, half(h)].bitcast(FP8X4), rhs_scale=k_scales[h][:], start=True, stop=True,
             )
-        for h in range(2):
-            nc.scalar.activation(out=capped[h], in_=score[h][:], func=ACT.Tanh, scale=1.0 / CAP)
 
-        v_codes = keep.tile([P, DV], U32, name="v_codes", align_bytes=64)
         v_scales = keep.tile([P, DV], U8, name="v_scales", align_bytes=64)
-
-        def gather_v(h, got, a, b):
-            nc.vector.tensor_copy(got.bitcast(BF16)[:, a:b], v_raw[h][:].indirect(offsets[:, a // 16 : b // 16]))
 
         def turn_v(h, got, tag):
             turned = psum.tile([P, 2, P], F32, name=f"v_turned{h}", tag=tag)
             for u in range(2):
                 nc.tensor.transpose(turned[:, u, :], got[:, u::2], ident[:])
-            nc.scalar.copy(
+            nc.vector.tensor_copy(
                 out=v_bf[:, h * PACK * P : (h + 1) * PACK * P].bitcast(F32).rearrange("p (e u) -> p e u", u=2),
                 in_=turned[:].rearrange("p u e -> p e u"),
             )
 
-        def quant_v(h):
-            nc.vector.quantize_mx(
-                out=v_codes[:, h * P : (h + 1) * P].bitcast(FP8X4), scales=v_scales[:, h * P : (h + 1) * P],
-                in_=v_bf[:, h * PACK * P : (h + 1) * PACK * P],
-            )
-
-        v_got0 = shared[:, 0:HALF]
-        gather_v(0, v_got0, 0, EARLY)
+        v_got0 = keep.tile([P, HALF], F32, name="v_got0", tag="k_got", align_bytes=64)
+        nc.vector.tensor_copy(v_got0[:].bitcast(BF16), v_raw[0][:].indirect(offsets[:]))
+        for h in range(2):
+            nc.scalar.activation(out=capped[:, half(h)], in_=score[h][:], func=ACT.Tanh, scale=1.0 / CAP)
         visible = keep.tile([NQ, N], F32, name="visible", tag="visible", align_bytes=64)
         for h in range(2):
-            nc.vector.tensor_tensor(out=visible[:, half(h)], in0=capped[h], in1=bound[:, half(h)], op=ALU.min)
-        vs_turned, vs_columns = to_columns("vs", vs_g, "bank_b", "raw11")
-        nc.scalar.copy(out=vs_columns[:], in_=vs_turned[:, :, 0])
-        negated = keep.tile([NQ, N], F32, name="negated", tag="negated", align_bytes=64)
+            nc.vector.tensor_tensor(out=visible[:, half(h)], in0=capped[:, half(h)], in1=bound[:, half(h)], op=ALU.min)
+        v_got1 = keep.tile([P, HALF], F32, name="v_got1", align_bytes=64)
+        nc.scalar.activation(out=v_got1[:].bitcast(BF16), in_=v1_pool[:].indirect(offsets[:]), func=ACT.Copy)
+        negated = keep.tile([NQ, N], F32, name="negated")
         neg_max = keep.tile([NQ, 1], F32, name="neg_max")
         nc.vector.tensor_scalar(out=negated[:], in0=visible[:], scalar1=-CAP, scalar2=None, op0=ALU.mult, op1=ALU.min, accum_out=neg_max[:])
 
-        gather_v(0, v_got0, EARLY, N)
-        prob = keep.tile([NQ, N], F32, name="prob")
+        vs_turned, vs_columns = to_columns("vs", vs_g, "bank_b", "bound1")
+        nc.vector.tensor_copy(out=vs_columns[:], in_=vs_turned[:, :, 0])
+        v_bf = keep.tile([P, DV * PACK], BF16, name="v_bf", tag="visible", align_bytes=64)
+        turn_v(0, v_got0[:], "score1")
+        turn_v(1, v_got1[:], "score0")
+        prob = keep.tile([NQ, N], F32, name="prob", tag="prob", align_bytes=64)
         sums = [keep.tile([NQ, 1], F32, name=f"row_sum{h}") for h in range(2)]
         p_turned = psum.tile([P, PACK, NQ], F32, name="p_turned")
         for h in range(2):
             nc.scalar.activation(out=prob[:, half(h)], in_=negated[:, half(h)], func=ACT.Exp, scale=-1.0, bias=neg_max[:, 0:1], accum_out=sums[h][:])
         for t in range(PACK):
             nc.tensor.transpose(p_turned[:, t, :], prob[:, t * P : (t + 1) * P], ident[:])
-        v_got1 = visible[:, 0:HALF]
-        gather_v(1, v_got1, 0, N)
-        v_bf = keep.tile([P, DV * PACK], BF16, name="v_bf", tag="negated", align_bytes=64)
-        turn_v(0, v_got0, "score1")
-        turn_v(1, v_got1, "score1")
 
         w_bf = keep.tile([P, NQ * PACK], BF16, name="w_bf", align_bytes=64)
         w_codes = keep.tile([P, NQ], U32, name="w_codes", align_bytes=64)
         w_scales = keep.tile([P, NQ], U8, name="w_scales", align_bytes=64)
         row_sum = keep.tile([NQ, 1], F32, name="row_sum")
-        inverse = keep.tile([NQ, 1], F32, name="inverse")
+        inverse = keep.tile([NQ, 1], F32, name="inverse", tag="bound1", align_bytes=64)
         nc.vector.tensor_tensor(
             out=w_bf[:].rearrange("p (q t) -> p q t", t=PACK), in0=p_turned[:].rearrange("p t q -> p q t"),
             in1=vs_columns[:].unsqueeze(1).to_broadcast([P, NQ, PACK]), op=ALU.mult,
         )
+        v_codes = keep.tile([P, DV], U32, name="v_codes", tag="prob", align_bytes=64)
+        nc.vector.quantize_mx(out=v_codes[:].bitcast(FP8X4), scales=v_scales[:], in_=v_bf[:])
         nc.vector.tensor_tensor(out=row_sum[:], in0=sums[0][:], in1=sums[1][:], op=ALU.add)
-        quant_v(0)
         nc.vector.quantize_mx(out=w_codes[:].bitcast(FP8X4), scales=w_scales[:], in_=w_bf[:])
-        quant_v(1)
         nc.vector.reciprocal(out=inverse[:], in_=row_sum[:])
         result = keep.tile([NQ, DV], F32, name="result")
         for h, tag in enumerate(("bank_a", "bank_b")):

@@ -35,7 +35,7 @@ def tile_attend_x_draft_cap_topk_kernel(tc, qT, kT, vT, vs, pos, qpos, offs, out
         psum = ctx.enter_context(tc.psum_pool(name="psum", bufs=1))
 
         offsets = keep.tile([P, N // 16], U16, name="offsets")
-        qpos_col = keep.tile([P, 1], F32, name="qpos_col")
+        qpos_row = keep.tile([P, NQ], F32, name="qpos_row")
         pos_pool = keep.tile([P, T], F32, name="pos_pool")
         vs_pool = keep.tile([P, T], F32, name="vs_pool")
         q_raw = keep.tile([P, PACK, NQ], F32, name="q_raw", tag="q_raw", align_bytes=64)
@@ -49,10 +49,12 @@ def tile_attend_x_draft_cap_topk_kernel(tc, qT, kT, vT, vs, pos, qpos, offs, out
             a, b = PIECES[u][c]
             nc.sync.dma_start(out=k_raw[u, c][:], in_=k_rows[:, 2 * u : 2 * u + 2, a:b])
 
+        nc.gpsimd.memset(qpos_row[:], 0.0)
         nc.vector.memset(pos_pool[:], 0.0)
         nc.vector.memset(vs_pool[:], 0.0)
         load_k(0, 0)
         nc.sync.dma_start(offsets[:], offs)
+        nc.sync.dma_start(out=qpos_row[1:2, :], in_=qpos.rearrange("b q o -> (b o) q"))
         nc.sync.dma_start(out=pos_pool[0:1, :], in_=pos[0:1, :])
         load_k(0, 1)
         nc.sync.dma_start(out=vs_pool[0:1, :], in_=vs[0:1, :])
@@ -60,7 +62,6 @@ def tile_attend_x_draft_cap_topk_kernel(tc, qT, kT, vT, vs, pos, qpos, offs, out
         load_k(1, 0)
         load_k(1, 1)
         nc.sync.dma_start(out=q_raw[:], in_=qT.rearrange("b (p j) q -> p (b j) q", j=PACK))
-        nc.sync.dma_start(out=qpos_col[:], in_=qpos.rearrange("b q o -> (b q) o"))
 
         warm = keep.tile([P, 1], F32, name="warm")
         nc.gpsimd.memset(warm[:], 0.0)
@@ -100,7 +101,12 @@ def tile_attend_x_draft_cap_topk_kernel(tc, qT, kT, vT, vs, pos, qpos, offs, out
         vs_g = keep.tile([P, N], F32, name="vs_g")
         nc.vector.tensor_copy(pos_g[:], pos_pool[:].indirect(offsets[:]))
         nc.vector.tensor_copy(vs_g[:], vs_pool[:].indirect(offsets[:]))
-        pos_turned, pos_columns = to_columns("pos", pos_g, "bank_a", "raw02")
+        pos_turned = psum.tile([P, PACK, P], F32, name="pos_turned", tag="bank_a")
+        nc.tensor.matmul(pos_turned[:, 0, :], lhsT=qpos_row[:], rhs=ident[:], is_transpose=True, start=True, stop=False)
+        nc.tensor.matmul(pos_turned[:, 0, :], lhsT=pos_g[:, 0::PACK], rhs=ident[:], is_transpose=True, start=False, stop=True)
+        for t in range(1, PACK):
+            nc.tensor.transpose(pos_turned[:, t, :], pos_g[:, t::PACK], ident[:])
+        pos_columns = keep.tile([P, PACK, 2], F32, name="pos_columns", tag="raw02", align_bytes=64)
 
         cast("scalar", 0, 0, 0, CHUNK // 2)
         cast("scalar", 0, 1, 0, CHUNK // 2)
@@ -110,10 +116,10 @@ def tile_attend_x_draft_cap_topk_kernel(tc, qT, kT, vT, vs, pos, qpos, offs, out
         for h in range(2):
             nc.sync.dma_start(out=v_raw[h][:], in_=vT[h * P : (h + 1) * P, :])
         gather_k(0)
-        nc.scalar.copy(out=pos_columns[:], in_=pos_turned[:, :, 0])
+        nc.scalar.copy(out=pos_columns[:], in_=pos_turned[:, :, 0:2])
         pos_spread = psum.tile([NQ, PACK, P], F32, name="pos_spread")
         for t in range(PACK):
-            nc.tensor.transpose(pos_spread[:, t, :], pos_columns[:, t : t + 1].to_broadcast([P, P]), ident[:])
+            nc.tensor.transpose(pos_spread[:, t, :], pos_columns[:, t, 0:1].to_broadcast([P, P]), ident[:])
         cast("scalar", 1, 0, 0, CHUNK)
         cast("vector", 1, 1, 0, SHARE1)
         cast("scalar", 1, 1, SHARE1, CHUNK)
@@ -132,7 +138,7 @@ def tile_attend_x_draft_cap_topk_kernel(tc, qT, kT, vT, vs, pos, qpos, offs, out
             )
         side = keep.tile([NQ, N], F32, name="side", tag="raw11", align_bytes=64)
         bound = keep.tile([NQ, N], F32, name="bound", tag="bound1", align_bytes=64)
-        nc.scalar.activation(out=side[:], in_=pos_spread[:].rearrange("p t s -> p (t s)"), func=ACT.Sign, scale=-1.0, bias=qpos_col[:, 0:1])
+        nc.scalar.activation(out=side[:], in_=pos_spread[:].rearrange("p t s -> p (t s)"), func=ACT.Sign, scale=-1.0, bias=pos_columns[:, 0, 1:2])
         nc.scalar.activation(out=bound[:], in_=side[:], func=ACT.Copy, scale=1.0 - MASKED / CAP, bias=1.0)
 
         k_codes = keep.tile([P, N], U32, name="k_codes", tag="q_raw", align_bytes=64)

@@ -72,7 +72,7 @@ def tile_attend_x_draft_cap_topk_kernel(tc, qT, kT, vT, vs, pos, qpos, offs, out
         make_identity(nc, ident[:], nomemset=True)
 
         k_pairs = [keep.tile([P, 2 * T], BF16, name=f"k_pairs{u}", align_bytes=64) for u in range(2)]
-        k_got = keep.tile([P, PACK * N], BF16, name="k_got", tag="k_got", align_bytes=64)
+        k_got = keep.tile([P, PACK * N], BF16, name="k_got", tag="q_raw", align_bytes=64)
         k_planes = keep.tile([P, 2 * N], U32, name="k_planes", align_bytes=64)
 
         def cast(engine, u, c, a, b):
@@ -116,7 +116,7 @@ def tile_attend_x_draft_cap_topk_kernel(tc, qT, kT, vT, vs, pos, qpos, offs, out
         for h in range(2):
             nc.sync.dma_start(out=v_raw[h][:], in_=vT[h * P : (h + 1) * P, :])
         gather_k(0)
-        nc.scalar.copy(out=pos_columns[:], in_=pos_turned[:, :, 0:2])
+        nc.vector.tensor_copy(out=pos_columns[:], in_=pos_turned[:, :, 0:2])
         pos_spread = psum.tile([NQ, PACK, P], F32, name="pos_spread")
         for t in range(PACK):
             nc.tensor.transpose(pos_spread[:, t, :], pos_columns[:, t, 0:1].to_broadcast([P, P]), ident[:])
@@ -141,7 +141,7 @@ def tile_attend_x_draft_cap_topk_kernel(tc, qT, kT, vT, vs, pos, qpos, offs, out
         nc.scalar.activation(out=side[:], in_=pos_spread[:].rearrange("p t s -> p (t s)"), func=ACT.Sign, scale=-1.0, bias=pos_columns[:, 0, 1:2])
         nc.scalar.activation(out=bound[:], in_=side[:], func=ACT.Copy, scale=1.0 - MASKED / CAP, bias=1.0)
 
-        k_codes = keep.tile([P, N], U32, name="k_codes", tag="q_raw", align_bytes=64)
+        k_codes = keep.tile([P, N], U32, name="k_codes", align_bytes=64)
         k_scales = [keep.tile([P, HALF], U8, name=f"k_scales{h}", align_bytes=64) for h in range(2)]
         score = [psum.tile([NQ, HALF], F32, name=f"score{h}", tag=f"score{h}") for h in range(2)]
         v1_pool = keep.tile([P, T], BF16, name="v1_pool", tag="raw11", align_bytes=64)
@@ -166,7 +166,7 @@ def tile_attend_x_draft_cap_topk_kernel(tc, qT, kT, vT, vs, pos, qpos, offs, out
                 in_=turned[:].rearrange("p u e -> p e u"),
             )
 
-        v_got0 = keep.tile([P, HALF], F32, name="v_got0", tag="k_got", align_bytes=64)
+        v_got0 = keep.tile([P, HALF], F32, name="v_got0", tag="q_raw", align_bytes=64)
         nc.vector.tensor_copy(v_got0[:].bitcast(BF16), v_raw[0][:].indirect(offsets[:]))
         for h in range(2):
             nc.scalar.activation(out=capped[:, half(h)], in_=score[h][:], func=ACT.Tanh, scale=1.0 / CAP)
@@ -184,7 +184,7 @@ def tile_attend_x_draft_cap_topk_kernel(tc, qT, kT, vT, vs, pos, qpos, offs, out
         v_bf = keep.tile([P, DV * PACK], BF16, name="v_bf", tag="visible", align_bytes=64)
         turn_v(0, v_got0[:], "score1")
         turn_v(1, v_got1[:], "score0")
-        prob = keep.tile([NQ, N], F32, name="prob", tag="prob", align_bytes=64)
+        prob = keep.tile([NQ, N], F32, name="prob")
         sums = [keep.tile([NQ, 1], F32, name=f"row_sum{h}") for h in range(2)]
         p_turned = psum.tile([P, PACK, NQ], F32, name="p_turned")
         for h in range(2):
@@ -197,14 +197,17 @@ def tile_attend_x_draft_cap_topk_kernel(tc, qT, kT, vT, vs, pos, qpos, offs, out
         w_scales = keep.tile([P, NQ], U8, name="w_scales", align_bytes=64)
         row_sum = keep.tile([NQ, 1], F32, name="row_sum")
         inverse = keep.tile([NQ, 1], F32, name="inverse", tag="bound1", align_bytes=64)
-        nc.vector.tensor_tensor(
-            out=w_bf[:].rearrange("p (q t) -> p q t", t=PACK), in0=p_turned[:].rearrange("p t q -> p q t"),
-            in1=vs_columns[:].unsqueeze(1).to_broadcast([P, NQ, PACK]), op=ALU.mult,
-        )
-        v_codes = keep.tile([P, DV], U32, name="v_codes", tag="prob", align_bytes=64)
+        v_codes = keep.tile([P, DV], U32, name="v_codes", align_bytes=64)
         nc.vector.quantize_mx(out=v_codes[:].bitcast(FP8X4), scales=v_scales[:], in_=v_bf[:])
         nc.vector.tensor_tensor(out=row_sum[:], in0=sums[0][:], in1=sums[1][:], op=ALU.add)
-        nc.vector.quantize_mx(out=w_codes[:].bitcast(FP8X4), scales=w_scales[:], in_=w_bf[:])
+        rows = [slice(h * NQ // 2, (h + 1) * NQ // 2) for h in range(2)]
+        for h in range(2):
+            nc.vector.tensor_tensor(
+                out=w_bf[:, half(h)].rearrange("p (q t) -> p q t", t=PACK), in0=p_turned[:].rearrange("p t q -> p q t")[:, rows[h], :],
+                in1=vs_columns[:].unsqueeze(1).to_broadcast([P, NQ // 2, PACK]), op=ALU.mult,
+            )
+        for h in range(2):
+            nc.vector.quantize_mx(out=w_codes[:, rows[h]].bitcast(FP8X4), scales=w_scales[:, rows[h]], in_=w_bf[:, half(h)])
         nc.vector.reciprocal(out=inverse[:], in_=row_sum[:])
         result = keep.tile([NQ, DV], F32, name="result")
         for h, tag in enumerate(("bank_a", "bank_b")):

@@ -16,6 +16,8 @@ CHUNK = T // 2
 PIECES = (((0, T // 4), (T // 4, T // 2), (T // 2, T)), ((0, T // 2), (T // 2, T)))
 SHARE0 = 128
 SHARE1 = 320
+LAST = P - 1
+MID = P // 2 - 1
 
 F32 = mybir.dt.float32
 BF16 = mybir.dt.bfloat16
@@ -49,15 +51,16 @@ def tile_attend_x_draft_cap_topk_kernel(tc, qT, kT, vT, vs, pos, qpos, offs, out
             a, b = PIECES[u][c]
             nc.sync.dma_start(out=k_raw[u, c][:], in_=k_rows[:, 2 * u : 2 * u + 2, a:b])
 
-        nc.gpsimd.memset(qpos_row[:], 0.0)
-        nc.vector.memset(pos_pool[:], 0.0)
-        nc.vector.memset(vs_pool[:], 0.0)
+        nc.gpsimd.memset(qpos_row[0:MID, :], 0.0)
+        nc.gpsimd.memset(qpos_row[MID + 1 : P, :], 0.0)
+        nc.vector.memset(pos_pool[0:LAST, :], 0.0)
+        nc.vector.memset(vs_pool[0:LAST, :], 0.0)
         load_k(0, 0)
         nc.sync.dma_start(offsets[:], offs)
-        nc.sync.dma_start(out=qpos_row[1:2, :], in_=qpos.rearrange("b q o -> (b o) q"))
-        nc.sync.dma_start(out=pos_pool[0:1, :], in_=pos[0:1, :])
+        nc.sync.dma_start(out=pos_pool[LAST:P, :], in_=pos[0:1, :])
+        nc.sync.dma_start(out=qpos_row[MID : MID + 1, :], in_=qpos.rearrange("b q o -> (b o) q"))
         load_k(0, 1)
-        nc.sync.dma_start(out=vs_pool[0:1, :], in_=vs[0:1, :])
+        nc.sync.dma_start(out=vs_pool[LAST:P, :], in_=vs[0:1, :])
         load_k(0, 2)
         load_k(1, 0)
         load_k(1, 1)
@@ -116,10 +119,10 @@ def tile_attend_x_draft_cap_topk_kernel(tc, qT, kT, vT, vs, pos, qpos, offs, out
         for h in range(2):
             nc.sync.dma_start(out=v_raw[h][:], in_=vT[h * P : (h + 1) * P, :])
         gather_k(0)
-        nc.vector.tensor_copy(out=pos_columns[:], in_=pos_turned[:, :, 0:2])
+        nc.vector.tensor_copy(out=pos_columns[:], in_=pos_turned[:, :, MID :: P // 2])
         pos_spread = psum.tile([NQ, PACK, P], F32, name="pos_spread")
         for t in range(PACK):
-            nc.tensor.transpose(pos_spread[:, t, :], pos_columns[:, t, 0:1].to_broadcast([P, P]), ident[:])
+            nc.tensor.transpose(pos_spread[:, t, :], pos_columns[:, t, 1:2].to_broadcast([P, P]), ident[:])
         cast("scalar", 1, 0, 0, CHUNK)
         cast("vector", 1, 1, 0, SHARE1)
         cast("scalar", 1, 1, SHARE1, CHUNK)
@@ -138,7 +141,7 @@ def tile_attend_x_draft_cap_topk_kernel(tc, qT, kT, vT, vs, pos, qpos, offs, out
             )
         side = keep.tile([NQ, N], F32, name="side", tag="raw11", align_bytes=64)
         bound = keep.tile([NQ, N], F32, name="bound", tag="bound1", align_bytes=64)
-        nc.scalar.activation(out=side[:], in_=pos_spread[:].rearrange("p t s -> p (t s)"), func=ACT.Sign, scale=-1.0, bias=pos_columns[:, 0, 1:2])
+        nc.scalar.activation(out=side[:], in_=pos_spread[:].rearrange("p t s -> p (t s)"), func=ACT.Sign, scale=-1.0, bias=pos_columns[:, 0, 0:1])
         nc.scalar.activation(out=bound[:], in_=side[:], func=ACT.Copy, scale=1.0 - MASKED / CAP, bias=1.0)
 
         k_codes = keep.tile([P, N], U32, name="k_codes", align_bytes=64)
@@ -180,7 +183,7 @@ def tile_attend_x_draft_cap_topk_kernel(tc, qT, kT, vT, vs, pos, qpos, offs, out
         nc.vector.tensor_scalar(out=negated[:], in0=visible[:], scalar1=-CAP, scalar2=None, op0=ALU.mult, op1=ALU.min, accum_out=neg_max[:])
 
         vs_turned, vs_columns = to_columns("vs", vs_g, "bank_b", "bound1")
-        nc.vector.tensor_copy(out=vs_columns[:], in_=vs_turned[:, :, 0])
+        nc.vector.tensor_copy(out=vs_columns[:], in_=vs_turned[:, :, LAST])
         v_bf = keep.tile([P, DV * PACK], BF16, name="v_bf", tag="visible", align_bytes=64)
         turn_v(0, v_got0[:], "score1")
         turn_v(1, v_got1[:], "score0")

@@ -16,6 +16,7 @@ CHUNK = T // 2
 PIECES = (((0, T // 4), (T // 4, T // 2), (T // 2, T)), ((0, T // 2), (T // 2, T)))
 SHARE0 = 128
 SHARE1 = 320
+LATE = 96
 LAST = P - 1
 MID = P // 2 - 1
 
@@ -90,15 +91,11 @@ def tile_attend_x_draft_cap_topk_kernel(tc, qT, kT, vT, vs, pos, qpos, offs, out
         def half(h):
             return slice(h * HALF, (h + 1) * HALF)
 
+        def quarter(t):
+            return slice(t * P, (t + 1) * P)
+
         def gather_k(u):
             nc.vector.tensor_copy(k_planes[:, u * N : (u + 1) * N].rearrange("p (t s) -> p s t", t=PACK), k_pairs[u][:].bitcast(U32).indirect(offsets[:]))
-
-        def to_columns(name, row, turned_tag, column_tag):
-            turned = psum.tile([P, PACK, P], F32, name=f"{name}_turned", tag=turned_tag)
-            for t in range(PACK):
-                nc.tensor.transpose(turned[:, t, :], row[:, t::PACK], ident[:])
-            columns = keep.tile([P, PACK], F32, name=f"{name}_columns", tag=column_tag, align_bytes=64)
-            return turned, columns
 
         pos_g = keep.tile([P, N], F32, name="pos_g")
         vs_g = keep.tile([P, N], F32, name="vs_g")
@@ -115,9 +112,11 @@ def tile_attend_x_draft_cap_topk_kernel(tc, qT, kT, vT, vs, pos, qpos, offs, out
         cast("scalar", 0, 1, 0, CHUNK // 2)
         cast("vector", 0, 2, 0, SHARE0)
         cast("scalar", 0, 2, SHARE0, CHUNK)
-        v_raw = [keep.tile([P, T], F32, name=f"v_raw{h}", tag=f"raw0{h}", align_bytes=64) for h in range(2)]
-        for h in range(2):
-            nc.sync.dma_start(out=v_raw[h][:], in_=vT[h * P : (h + 1) * P, :])
+        v1_raw = [keep.tile([P, CHUNK], F32, name=f"v1_raw{c}", tag=f"raw0{c}", align_bytes=64) for c in range(2)]
+        v0_pool = keep.tile([P, T], F32, name="v0_pool", align_bytes=64)
+        for c in range(2):
+            nc.sync.dma_start(out=v1_raw[c][:], in_=vT[P:DV, c * CHUNK : (c + 1) * CHUNK])
+        nc.sync.dma_start(out=v0_pool[:], in_=vT[:P, :])
         gather_k(0)
         nc.vector.tensor_copy(out=pos_columns[:], in_=pos_turned[:, :, MID :: P // 2])
         pos_spread = psum.tile([NQ, PACK, P], F32, name="pos_spread")
@@ -134,28 +133,30 @@ def tile_attend_x_draft_cap_topk_kernel(tc, qT, kT, vT, vs, pos, qpos, offs, out
         nc.scalar.copy(out=q_bf[:].rearrange("p (q j) -> p q j", j=PACK), in_=q_raw[:].rearrange("p j q -> p q j"))
         nc.vector.quantize_mx(out=q_codes[:].bitcast(FP8X4), scales=q_scales[:], in_=q_bf[:])
 
-        for h in range(2):
+        for h in (1, 0):
             nc.vector.tensor_copy(
                 out=k_got[:].bitcast(I32)[:, h * N : (h + 1) * N].rearrange("p (c u) -> p c u", u=2),
                 in_=k_planes[:].bitcast(I32).rearrange("p (u c) -> p c u", u=2)[:, half(h), :],
             )
         side = keep.tile([NQ, N], F32, name="side", tag="raw11", align_bytes=64)
-        bound = keep.tile([NQ, N], F32, name="bound", tag="bound1", align_bytes=64)
         nc.scalar.activation(out=side[:], in_=pos_spread[:].rearrange("p t s -> p (t s)"), func=ACT.Sign, scale=-1.0, bias=pos_columns[:, 0, 0:1])
-        nc.scalar.activation(out=bound[:], in_=side[:], func=ACT.Copy, scale=1.0 - MASKED / CAP, bias=1.0)
+        v1_pool = keep.tile([P, T], BF16, name="v1_pool", align_bytes=64)
+        for c in range(2):
+            nc.scalar.copy(out=v1_pool[:, c * CHUNK : (c + 1) * CHUNK], in_=v1_raw[c][:])
+        work = keep.tile([P, N + HALF], F32, name="work", tag="raw00", align_bytes=64)
+        bound = work[:, :N]
+        nc.scalar.activation(out=bound, in_=side[:], func=ACT.Copy, scale=1.0 - MASKED / CAP, bias=1.0)
 
         k_codes = keep.tile([P, N], U32, name="k_codes", align_bytes=64)
-        k_scales = [keep.tile([P, HALF], U8, name=f"k_scales{h}", align_bytes=64) for h in range(2)]
-        score = [psum.tile([NQ, HALF], F32, name=f"score{h}", tag=f"score{h}") for h in range(2)]
-        v1_pool = keep.tile([P, T], BF16, name="v1_pool", tag="raw11", align_bytes=64)
-        nc.scalar.copy(out=v1_pool[:], in_=v_raw[1][:])
-        capped = keep.tile([NQ, N], F32, name="capped", tag="raw01", align_bytes=64)
-        for h in range(2):
-            nc.vector.quantize_mx(out=k_codes[:, half(h)].bitcast(FP8X4), scales=k_scales[h][:], in_=k_got[:, h * PACK * HALF : (h + 1) * PACK * HALF])
-        for h in range(2):
+        k_scales = [keep.tile([P, P], U8, name=f"k_scales{t}", align_bytes=64) for t in range(PACK)]
+        score = [psum.tile([NQ, P], F32, name=f"score{t}", tag=f"score{t}") for t in range(PACK)]
+        capped = keep.tile([NQ, N], F32, name="capped", align_bytes=64)
+        for t in (2, 3, 0, 1):
+            nc.vector.quantize_mx(out=k_codes[:, quarter(t)].bitcast(FP8X4), scales=k_scales[t][:], in_=k_got[:, t * PACK * P : (t + 1) * PACK * P])
+        for t in (2, 3, 0, 1):
             nc.tensor.matmul_mx(
-                out=score[h][:], lhsT=q_codes[:].bitcast(FP8X4), lhsT_scale=q_scales[:],
-                rhs=k_codes[:, half(h)].bitcast(FP8X4), rhs_scale=k_scales[h][:], start=True, stop=True,
+                out=score[t][:], lhsT=q_codes[:].bitcast(FP8X4), lhsT_scale=q_scales[:],
+                rhs=k_codes[:, quarter(t)].bitcast(FP8X4), rhs_scale=k_scales[t][:], start=True, stop=True,
             )
 
         v_scales = keep.tile([P, DV], U8, name="v_scales", align_bytes=64)
@@ -169,24 +170,28 @@ def tile_attend_x_draft_cap_topk_kernel(tc, qT, kT, vT, vs, pos, qpos, offs, out
                 in_=turned[:].rearrange("p u e -> p e u"),
             )
 
-        v_got0 = keep.tile([P, HALF], F32, name="v_got0", tag="q_raw", align_bytes=64)
-        nc.vector.tensor_copy(v_got0[:].bitcast(BF16), v_raw[0][:].indirect(offsets[:]))
-        for h in range(2):
-            nc.scalar.activation(out=capped[:, half(h)], in_=score[h][:], func=ACT.Tanh, scale=1.0 / CAP)
+        v_got0 = work[:, N - LATE // 2 : N - LATE // 2 + HALF]
+        nc.vector.tensor_copy(v_got0[:, LATE // 2 :].bitcast(BF16), v0_pool[:].indirect(offsets[:, LATE // 16 :]))
+        for t in (2, 3, 0, 1):
+            nc.scalar.activation(out=capped[:, quarter(t)], in_=score[t][:], func=ACT.Tanh, scale=1.0 / CAP)
         visible = keep.tile([NQ, N], F32, name="visible", tag="visible", align_bytes=64)
-        for h in range(2):
+        for h in (1, 0):
             nc.vector.tensor_tensor(out=visible[:, half(h)], in0=capped[:, half(h)], in1=bound[:, half(h)], op=ALU.min)
+        nc.vector.tensor_copy(v_got0[:, : LATE // 2].bitcast(BF16), v0_pool[:].indirect(offsets[:, : LATE // 16]))
         v_got1 = keep.tile([P, HALF], F32, name="v_got1", align_bytes=64)
         nc.scalar.activation(out=v_got1[:].bitcast(BF16), in_=v1_pool[:].indirect(offsets[:]), func=ACT.Copy)
         negated = keep.tile([NQ, N], F32, name="negated")
         neg_max = keep.tile([NQ, 1], F32, name="neg_max")
         nc.vector.tensor_scalar(out=negated[:], in0=visible[:], scalar1=-CAP, scalar2=None, op0=ALU.mult, op1=ALU.min, accum_out=neg_max[:])
 
-        vs_turned, vs_columns = to_columns("vs", vs_g, "bank_b", "bound1")
-        nc.vector.tensor_copy(out=vs_columns[:], in_=vs_turned[:, :, LAST])
+        vs_turned = psum.tile([P, PACK, P], F32, name="vs_turned", tag="bank_b")
+        for t in range(PACK):
+            nc.tensor.transpose(vs_turned[:, t, :], vs_g[:, t::PACK], ident[:])
+        vs_columns = work[:, HALF : HALF + PACK]
+        nc.vector.tensor_copy(out=vs_columns, in_=vs_turned[:, :, LAST])
         v_bf = keep.tile([P, DV * PACK], BF16, name="v_bf", tag="visible", align_bytes=64)
-        turn_v(0, v_got0[:], "score1")
-        turn_v(1, v_got1[:], "score0")
+        turn_v(0, v_got0, "score2")
+        turn_v(1, v_got1[:], "score3")
         prob = keep.tile([NQ, N], F32, name="prob")
         sums = [keep.tile([NQ, 1], F32, name=f"row_sum{h}") for h in range(2)]
         p_turned = psum.tile([P, PACK, NQ], F32, name="p_turned")
@@ -199,7 +204,7 @@ def tile_attend_x_draft_cap_topk_kernel(tc, qT, kT, vT, vs, pos, qpos, offs, out
         w_codes = keep.tile([P, NQ], U32, name="w_codes", align_bytes=64)
         w_scales = keep.tile([P, NQ], U8, name="w_scales", align_bytes=64)
         row_sum = keep.tile([NQ, 1], F32, name="row_sum")
-        inverse = keep.tile([NQ, 1], F32, name="inverse", tag="bound1", align_bytes=64)
+        inverse = work[:, HALF : HALF + 1]
         v_codes = keep.tile([P, DV], U32, name="v_codes", align_bytes=64)
         nc.vector.quantize_mx(out=v_codes[:].bitcast(FP8X4), scales=v_scales[:], in_=v_bf[:])
         nc.vector.tensor_tensor(out=row_sum[:], in0=sums[0][:], in1=sums[1][:], op=ALU.add)
@@ -207,11 +212,11 @@ def tile_attend_x_draft_cap_topk_kernel(tc, qT, kT, vT, vs, pos, qpos, offs, out
         for h in range(2):
             nc.vector.tensor_tensor(
                 out=w_bf[:, half(h)].rearrange("p (q t) -> p q t", t=PACK), in0=p_turned[:].rearrange("p t q -> p q t")[:, rows[h], :],
-                in1=vs_columns[:].unsqueeze(1).to_broadcast([P, NQ // 2, PACK]), op=ALU.mult,
+                in1=vs_columns.unsqueeze(1).to_broadcast([P, NQ // 2, PACK]), op=ALU.mult,
             )
         for h in range(2):
             nc.vector.quantize_mx(out=w_codes[:, rows[h]].bitcast(FP8X4), scales=w_scales[:, rows[h]], in_=w_bf[:, half(h)])
-        nc.vector.reciprocal(out=inverse[:], in_=row_sum[:])
+        nc.vector.reciprocal(out=inverse, in_=row_sum[:])
         result = keep.tile([NQ, DV], F32, name="result")
         for h, tag in enumerate(("bank_a", "bank_b")):
             cols = slice(h * P, (h + 1) * P)
@@ -220,5 +225,5 @@ def tile_attend_x_draft_cap_topk_kernel(tc, qT, kT, vT, vs, pos, qpos, offs, out
                 out=y[:], lhsT=w_codes[:].bitcast(FP8X4), lhsT_scale=w_scales[:],
                 rhs=v_codes[:, cols].bitcast(FP8X4), rhs_scale=v_scales[:, cols], start=True, stop=True,
             )
-            nc.vector.tensor_scalar(out=result[:, cols], in0=y[:], scalar1=inverse[:, 0:1], scalar2=None, op0=ALU.mult)
+            nc.vector.tensor_scalar(out=result[:, cols], in0=y[:], scalar1=inverse, scalar2=None, op0=ALU.mult)
         nc.sync.dma_start(out=out.rearrange("b q e -> (b q) e"), in_=result[:])

@@ -145,12 +145,12 @@ def tile_attend_x_draft_cap_topk_kernel(tc, qT, kT, vT, vs, pos, qpos, offs, out
             nc.scalar.copy(out=v1_pool[:, c * CHUNK : (c + 1) * CHUNK], in_=v1_raw[c][:])
         work = keep.tile([P, N + HALF], F32, name="work", tag="raw00", align_bytes=64)
         bound = work[:, :N]
-        nc.scalar.activation(out=bound, in_=side[:], func=ACT.Copy, scale=1.0 - MASKED / CAP, bias=1.0)
+        nc.scalar.activation(out=bound, in_=side[:], func=ACT.Copy, scale=CAP - MASKED, bias=CAP)
 
         k_codes = keep.tile([P, N], U32, name="k_codes", align_bytes=64)
         k_scales = [keep.tile([P, P], U8, name=f"k_scales{t}", align_bytes=64) for t in range(PACK)]
         score = [psum.tile([NQ, P], F32, name=f"score{t}", tag=f"score{t}") for t in range(PACK)]
-        capped = keep.tile([NQ, N], F32, name="capped", align_bytes=64)
+        capped = keep.tile([NQ, N], F32, name="capped", tag="capped", align_bytes=64)
         for t in (2, 3, 0, 1):
             nc.vector.quantize_mx(out=k_codes[:, quarter(t)].bitcast(FP8X4), scales=k_scales[t][:], in_=k_got[:, t * PACK * P : (t + 1) * PACK * P])
         for t in (2, 3, 0, 1):
@@ -159,16 +159,17 @@ def tile_attend_x_draft_cap_topk_kernel(tc, qT, kT, vT, vs, pos, qpos, offs, out
                 rhs=k_codes[:, quarter(t)].bitcast(FP8X4), rhs_scale=k_scales[t][:], start=True, stop=True,
             )
 
-        v_scales = keep.tile([P, DV], U8, name="v_scales", align_bytes=64)
+        v_scales = [keep.tile([P, P], U8, name=f"v_scales{h}", align_bytes=64) for h in range(2)]
+        v_codes = [keep.tile([P, P], U32, name=f"v_codes{h}", align_bytes=64) for h in range(2)]
 
         def turn_v(h, got, tag):
             turned = psum.tile([P, 2, P], F32, name=f"v_turned{h}", tag=tag)
             for u in range(2):
                 nc.tensor.transpose(turned[:, u, :], got[:, u::2], ident[:])
-            nc.vector.tensor_copy(
-                out=v_bf[:, h * PACK * P : (h + 1) * PACK * P].bitcast(F32).rearrange("p (e u) -> p e u", u=2),
-                in_=turned[:].rearrange("p u e -> p e u"),
-            )
+            return turned[:].rearrange("p u e -> p e u")
+
+        def words(v_bf):
+            return v_bf[:].bitcast(F32).rearrange("p (e u) -> p e u", u=2)
 
         v_got0 = work[:, N - LATE // 2 : N - LATE // 2 + HALF]
         nc.vector.tensor_copy(v_got0[:, LATE // 2 :].bitcast(BF16), v0_pool[:].indirect(offsets[:, LATE // 16 :]))
@@ -176,37 +177,38 @@ def tile_attend_x_draft_cap_topk_kernel(tc, qT, kT, vT, vs, pos, qpos, offs, out
             nc.scalar.activation(out=capped[:, quarter(t)], in_=score[t][:], func=ACT.Tanh, scale=1.0 / CAP)
         visible = keep.tile([NQ, N], F32, name="visible", tag="visible", align_bytes=64)
         for h in (1, 0):
-            nc.vector.tensor_tensor(out=visible[:, half(h)], in0=capped[:, half(h)], in1=bound[:, half(h)], op=ALU.min)
+            nc.vector.scalar_tensor_tensor(out=visible[:, half(h)], in0=capped[:, half(h)], scalar=CAP, in1=bound[:, half(h)], op0=ALU.mult, op1=ALU.min)
         nc.vector.tensor_copy(v_got0[:, : LATE // 2].bitcast(BF16), v0_pool[:].indirect(offsets[:, : LATE // 16]))
         v_got1 = keep.tile([P, HALF], F32, name="v_got1", align_bytes=64)
         nc.scalar.activation(out=v_got1[:].bitcast(BF16), in_=v1_pool[:].indirect(offsets[:]), func=ACT.Copy)
-        negated = keep.tile([NQ, N], F32, name="negated")
         neg_max = keep.tile([NQ, 1], F32, name="neg_max")
-        nc.vector.tensor_scalar(out=negated[:], in0=visible[:], scalar1=-CAP, scalar2=None, op0=ALU.mult, op1=ALU.min, accum_out=neg_max[:])
+        nc.vector.tensor_reduce(out=neg_max[:], in_=visible[:], axis=mybir.AxisListType.X, op=ALU.max, negate=True)
 
         vs_turned = psum.tile([P, PACK, P], F32, name="vs_turned", tag="bank_b")
         for t in range(PACK):
             nc.tensor.transpose(vs_turned[:, t, :], vs_g[:, t::PACK], ident[:])
         vs_columns = work[:, HALF : HALF + PACK]
         nc.vector.tensor_copy(out=vs_columns, in_=vs_turned[:, :, LAST])
-        v_bf = keep.tile([P, DV * PACK], BF16, name="v_bf", tag="visible", align_bytes=64)
-        turn_v(0, v_got0, "score2")
-        turn_v(1, v_got1[:], "score3")
+        v_turned0 = turn_v(0, v_got0, "score2")
+        v_turned1 = turn_v(1, v_got1[:], "score3")
+        v_bf0 = keep.tile([P, P * PACK], BF16, name="v_bf0", tag="capped", align_bytes=64)
+        nc.vector.tensor_copy(out=words(v_bf0), in_=v_turned0)
+        nc.vector.quantize_mx(out=v_codes[0][:].bitcast(FP8X4), scales=v_scales[0][:], in_=v_bf0[:])
         prob = keep.tile([NQ, N], F32, name="prob")
         sums = [keep.tile([NQ, 1], F32, name=f"row_sum{h}") for h in range(2)]
         p_turned = psum.tile([P, PACK, NQ], F32, name="p_turned")
         for h in range(2):
-            nc.scalar.activation(out=prob[:, half(h)], in_=negated[:, half(h)], func=ACT.Exp, scale=-1.0, bias=neg_max[:, 0:1], accum_out=sums[h][:])
+            nc.scalar.activation(out=prob[:, half(h)], in_=visible[:, half(h)], func=ACT.Exp, bias=neg_max[:, 0:1], accum_out=sums[h][:])
         for t in range(PACK):
             nc.tensor.transpose(p_turned[:, t, :], prob[:, t * P : (t + 1) * P], ident[:])
+        v_bf1 = keep.tile([P, P * PACK], BF16, name="v_bf1", tag="visible", align_bytes=64)
+        nc.scalar.copy(out=words(v_bf1), in_=v_turned1)
 
         w_bf = keep.tile([P, NQ * PACK], BF16, name="w_bf", align_bytes=64)
         w_codes = keep.tile([P, NQ], U32, name="w_codes", align_bytes=64)
         w_scales = keep.tile([P, NQ], U8, name="w_scales", align_bytes=64)
         row_sum = keep.tile([NQ, 1], F32, name="row_sum")
         inverse = work[:, HALF : HALF + 1]
-        v_codes = keep.tile([P, DV], U32, name="v_codes", align_bytes=64)
-        nc.vector.quantize_mx(out=v_codes[:].bitcast(FP8X4), scales=v_scales[:], in_=v_bf[:])
         nc.vector.tensor_tensor(out=row_sum[:], in0=sums[0][:], in1=sums[1][:], op=ALU.add)
         rows = [slice(h * NQ // 2, (h + 1) * NQ // 2) for h in range(2)]
         for h in range(2):
@@ -214,8 +216,9 @@ def tile_attend_x_draft_cap_topk_kernel(tc, qT, kT, vT, vs, pos, qpos, offs, out
                 out=w_bf[:, half(h)].rearrange("p (q t) -> p q t", t=PACK), in0=p_turned[:].rearrange("p t q -> p q t")[:, rows[h], :],
                 in1=vs_columns.unsqueeze(1).to_broadcast([P, NQ // 2, PACK]), op=ALU.mult,
             )
-        for h in range(2):
-            nc.vector.quantize_mx(out=w_codes[:, rows[h]].bitcast(FP8X4), scales=w_scales[:, rows[h]], in_=w_bf[:, half(h)])
+        nc.vector.quantize_mx(out=w_codes[:, rows[0]].bitcast(FP8X4), scales=w_scales[:, rows[0]], in_=w_bf[:, half(0)])
+        nc.vector.quantize_mx(out=v_codes[1][:].bitcast(FP8X4), scales=v_scales[1][:], in_=v_bf1[:])
+        nc.vector.quantize_mx(out=w_codes[:, rows[1]].bitcast(FP8X4), scales=w_scales[:, rows[1]], in_=w_bf[:, half(1)])
         nc.vector.reciprocal(out=inverse, in_=row_sum[:])
         result = keep.tile([NQ, DV], F32, name="result")
         for h, tag in enumerate(("bank_a", "bank_b")):
@@ -223,7 +226,7 @@ def tile_attend_x_draft_cap_topk_kernel(tc, qT, kT, vT, vs, pos, qpos, offs, out
             y = psum.tile([NQ, P], F32, name=f"y{h}", tag=tag)
             nc.tensor.matmul_mx(
                 out=y[:], lhsT=w_codes[:].bitcast(FP8X4), lhsT_scale=w_scales[:],
-                rhs=v_codes[:, cols].bitcast(FP8X4), rhs_scale=v_scales[:, cols], start=True, stop=True,
+                rhs=v_codes[h][:].bitcast(FP8X4), rhs_scale=v_scales[h][:], start=True, stop=True,
             )
             nc.vector.tensor_scalar(out=result[:, cols], in0=y[:], scalar1=inverse, scalar2=None, op0=ALU.mult)
         nc.sync.dma_start(out=out.rearrange("b q e -> (b q) e"), in_=result[:])

@@ -162,10 +162,10 @@ def tile_attend_x_draft_cap_topk_kernel(tc, qT, kT, vT, vs, pos, qpos, offs, out
         v_scales = [keep.tile([P, P], U8, name=f"v_scales{h}", align_bytes=64) for h in range(2)]
         v_codes = [keep.tile([P, P], U32, name=f"v_codes{h}", align_bytes=64) for h in range(2)]
 
-        def turn_v(h, got, tag):
+        def turn_v(h, planes, tag):
             turned = psum.tile([P, 2, P], F32, name=f"v_turned{h}", tag=tag)
             for u in range(2):
-                nc.tensor.transpose(turned[:, u, :], got[:, u::2], ident[:])
+                nc.tensor.transpose(turned[:, u, :], planes[u], ident[:])
             return turned[:].rearrange("p u e -> p e u")
 
         def words(v_bf):
@@ -180,7 +180,7 @@ def tile_attend_x_draft_cap_topk_kernel(tc, qT, kT, vT, vs, pos, qpos, offs, out
             nc.vector.scalar_tensor_tensor(out=visible[:, half(h)], in0=capped[:, half(h)], scalar=CAP, in1=bound[:, half(h)], op0=ALU.mult, op1=ALU.min)
         nc.vector.tensor_copy(v_got0[:, : LATE // 2].bitcast(BF16), v0_pool[:].indirect(offsets[:, : LATE // 16]))
         v_got1 = keep.tile([P, HALF], F32, name="v_got1", align_bytes=64)
-        nc.scalar.activation(out=v_got1[:].bitcast(BF16), in_=v1_pool[:].indirect(offsets[:]), func=ACT.Copy)
+        nc.scalar.activation(out=v_got1[:].bitcast(BF16).rearrange("p (u s h) -> p s u h", u=2, h=2), in_=v1_pool[:].indirect(offsets[:]), func=ACT.Copy)
         neg_max = keep.tile([NQ, 1], F32, name="neg_max")
         nc.vector.tensor_reduce(out=neg_max[:], in_=visible[:], axis=mybir.AxisListType.X, op=ALU.max, negate=True)
 
@@ -189,8 +189,8 @@ def tile_attend_x_draft_cap_topk_kernel(tc, qT, kT, vT, vs, pos, qpos, offs, out
             nc.tensor.transpose(vs_turned[:, t, :], vs_g[:, t::PACK], ident[:])
         vs_columns = work[:, HALF : HALF + PACK]
         nc.vector.tensor_copy(out=vs_columns, in_=vs_turned[:, :, LAST])
-        v_turned0 = turn_v(0, v_got0, "score2")
-        v_turned1 = turn_v(1, v_got1[:], "score3")
+        v_turned0 = turn_v(0, [v_got0[:, u::2] for u in range(2)], "score2")
+        v_turned1 = turn_v(1, [v_got1[:, quarter(u)] for u in range(2)], "score3")
         v_bf0 = keep.tile([P, P * PACK], BF16, name="v_bf0", tag="capped", align_bytes=64)
         nc.vector.tensor_copy(out=words(v_bf0), in_=v_turned0)
         nc.vector.quantize_mx(out=v_codes[0][:].bitcast(FP8X4), scales=v_scales[0][:], in_=v_bf0[:])

@@ -67,10 +67,6 @@ def tile_attend_x_draft_cap_topk_kernel(tc, qT, kT, vT, vs, pos, qpos, offs, out
         load_k(1, 1)
         nc.sync.dma_start(out=q_raw[:], in_=qT.rearrange("b (p j) q -> p (b j) q", j=PACK))
 
-        warm = keep.tile([P, 1], F32, name="warm")
-        nc.gpsimd.memset(warm[:], 0.0)
-        warm_out = keep.tile([P, 1], F32, name="warm_out")
-        nc.scalar.activation(out=warm_out[:], in_=warm[:], func=ACT.Exp)
         ident = keep.tile([P, P], F32, name="ident")
         nc.vector.memset(ident[:], 0.0)
         make_identity(nc, ident[:], nomemset=True)

@@ -5,25 +5,22 @@ from concourse.masks import make_identity
 
 D, T, N, DV, NQ = 512, 1024, 512, 256, 128
 CAP = 2.0
-MASKED = -30000.0
+HIDDEN = -float(2**27)
 FLOPS = 2 * D * NQ * N + 2 * N * NQ * DV
 BYTES = 4 * (D * T + DV * T + D * NQ + 2 * T + NQ + NQ * DV) + 2 * 128 * N // 16
 
 P = 128
 PACK = 4
 HALF = N // 2
-CHUNK = T // 2
-PIECES = (((0, T // 4), (T // 4, T // 2), (T // 2, T)), ((0, T // 2), (T // 2, T)))
-SHARE0 = 128
-SHARE1 = 320
-LATE = 96
+FIRST = T // 4
+EARLY = 256
+BESIDE = 160
 LAST = P - 1
 MID = P // 2 - 1
 
 F32 = mybir.dt.float32
 BF16 = mybir.dt.bfloat16
 U32 = mybir.dt.uint32
-I32 = mybir.dt.int32
 U16 = mybir.dt.uint16
 U8 = mybir.dt.uint8
 FP8X4 = mybir.dt.float8_e4m3fn_x4
@@ -43,46 +40,27 @@ def tile_attend_x_draft_cap_topk_kernel(tc, qT, kT, vT, vs, pos, qpos, offs, out
         vs_pool = keep.tile([P, T], F32, name="vs_pool")
         q_raw = keep.tile([P, PACK, NQ], F32, name="q_raw", tag="q_raw", align_bytes=64)
         k_rows = kT.rearrange("(p j) t -> p j t", j=PACK)
-        k_raw = {
-            (u, c): keep.tile([P, 2, b - a], F32, name=f"k_raw{u}{c}", tag=f"raw{u}{c}", align_bytes=64)
-            for u in range(2) for c, (a, b) in enumerate(PIECES[u])
-        }
+        k_pool = [keep.tile([P, T], F32, name=f"k_pool{j}") for j in range(PACK)]
+        v_pool = [keep.tile([P, T], F32, name=f"v_pool{h}") for h in range(2)]
 
-        def load_k(u, c):
-            a, b = PIECES[u][c]
-            nc.sync.dma_start(out=k_raw[u, c][:], in_=k_rows[:, 2 * u : 2 * u + 2, a:b])
-
-        nc.gpsimd.memset(qpos_row[0:MID, :], 0.0)
         nc.gpsimd.memset(qpos_row[MID + 1 : P, :], 0.0)
         nc.vector.memset(pos_pool[0:LAST, :], 0.0)
-        nc.vector.memset(vs_pool[0:LAST, :], 0.0)
-        load_k(0, 0)
-        nc.sync.dma_start(offsets[:], offs)
-        nc.sync.dma_start(out=pos_pool[LAST:P, :], in_=pos[0:1, :])
-        nc.sync.dma_start(out=qpos_row[MID : MID + 1, :], in_=qpos.rearrange("b q o -> (b o) q"))
-        load_k(0, 1)
-        nc.sync.dma_start(out=vs_pool[LAST:P, :], in_=vs[0:1, :])
-        load_k(0, 2)
-        load_k(1, 0)
-        load_k(1, 1)
-        nc.sync.dma_start(out=q_raw[:], in_=qT.rearrange("b (p j) q -> p (b j) q", j=PACK))
-
+        nc.scalar.copy(out=qpos_row[0:MID, :], in_=pos_pool[0:MID, :NQ])
         ident = keep.tile([P, P], F32, name="ident")
         nc.vector.memset(ident[:], 0.0)
         make_identity(nc, ident[:], nomemset=True)
-
-        k_pairs = [keep.tile([P, 2 * T], BF16, name=f"k_pairs{u}", align_bytes=64) for u in range(2)]
-        k_got = keep.tile([P, PACK * N], BF16, name="k_got", tag="q_raw", align_bytes=64)
-        k_planes = keep.tile([P, 2 * N], U32, name="k_planes", align_bytes=64)
-
-        def cast(engine, u, c, a, b):
-            first = PIECES[u][c][0]
-            dst = k_pairs[u][:, 2 * (first + a) : 2 * (first + b)].rearrange("p (t h) -> p t h", h=2)
-            src = k_raw[u, c][:, :, a:b].rearrange("p h t -> p t h")
-            if engine == "scalar":
-                nc.scalar.copy(out=dst, in_=src)
-            else:
-                nc.vector.tensor_copy(out=dst, in_=src)
+        nc.vector.memset(vs_pool[0:LAST, :], 0.0)
+        nc.sync.dma_start(out=k_pool[0][:, :FIRST], in_=k_rows[:, 0, :FIRST])
+        nc.sync.dma_start(offsets[:], offs)
+        nc.sync.dma_start(out=pos_pool[LAST:P, :], in_=pos[0:1, :])
+        nc.sync.dma_start(out=qpos_row[MID : MID + 1, :], in_=qpos.rearrange("b q o -> (b o) q"))
+        nc.sync.dma_start(out=k_pool[0][:, FIRST:], in_=k_rows[:, 0, FIRST:])
+        nc.sync.dma_start(out=vs_pool[LAST:P, :], in_=vs[0:1, :])
+        for j in range(1, PACK):
+            nc.sync.dma_start(out=k_pool[j][:], in_=k_rows[:, j, :])
+        nc.sync.dma_start(out=q_raw[:], in_=qT.rearrange("b (p j) q -> p (b j) q", j=PACK))
+        for h in (1, 0):
+            nc.sync.dma_start(out=v_pool[h][:], in_=vT[h * P : (h + 1) * P, :])
 
         def half(h):
             return slice(h * HALF, (h + 1) * HALF)
@@ -90,121 +68,130 @@ def tile_attend_x_draft_cap_topk_kernel(tc, qT, kT, vT, vs, pos, qpos, offs, out
         def quarter(t):
             return slice(t * P, (t + 1) * P)
 
-        def gather_k(u):
-            nc.vector.tensor_copy(k_planes[:, u * N : (u + 1) * N].rearrange("p (t s) -> p s t", t=PACK), k_pairs[u][:].bitcast(U32).indirect(offsets[:]))
+        def gather(engine, dst, pool, a, b):
+            picked = pool[:].indirect(offsets[:, a // 16 : b // 16])
+            if engine == "scalar":
+                nc.scalar.activation(out=dst[:, a:b], in_=picked, func=ACT.Copy)
+            else:
+                nc.vector.tensor_copy(dst[:, a:b], picked)
 
-        pos_g = keep.tile([P, N], F32, name="pos_g")
+        front = keep.tile([P, HALF + N], F32, name="front")
+        pos_g = front[:, HALF:]
+        planes01 = front[:].bitcast(BF16).rearrange("p (r c) -> p r c", c=N)[:, 0::2, :]
+        planes23 = keep.tile([P, 2, N], BF16, name="planes23")
         vs_g = keep.tile([P, N], F32, name="vs_g")
-        nc.vector.tensor_copy(pos_g[:], pos_pool[:].indirect(offsets[:]))
-        nc.vector.tensor_copy(vs_g[:], vs_pool[:].indirect(offsets[:]))
-        pos_turned = psum.tile([P, PACK, P], F32, name="pos_turned", tag="bank_a")
-        nc.tensor.matmul(pos_turned[:, 0, :], lhsT=qpos_row[:], rhs=ident[:], is_transpose=True, start=True, stop=False)
-        nc.tensor.matmul(pos_turned[:, 0, :], lhsT=pos_g[:, 0::PACK], rhs=ident[:], is_transpose=True, start=False, stop=True)
-        for t in range(1, PACK):
-            nc.tensor.transpose(pos_turned[:, t, :], pos_g[:, t::PACK], ident[:])
-        pos_columns = keep.tile([P, PACK, 2], F32, name="pos_columns", tag="raw02", align_bytes=64)
 
-        cast("scalar", 0, 0, 0, CHUNK // 2)
-        cast("scalar", 0, 1, 0, CHUNK // 2)
-        cast("vector", 0, 2, 0, SHARE0)
-        cast("scalar", 0, 2, SHARE0, CHUNK)
-        v1_raw = [keep.tile([P, CHUNK], F32, name=f"v1_raw{c}", tag=f"raw0{c}", align_bytes=64) for c in range(2)]
-        v0_pool = keep.tile([P, T], F32, name="v0_pool", align_bytes=64)
-        for c in range(2):
-            nc.sync.dma_start(out=v1_raw[c][:], in_=vT[P:DV, c * CHUNK : (c + 1) * CHUNK])
-        nc.sync.dma_start(out=v0_pool[:], in_=vT[:P, :])
-        gather_k(0)
-        nc.vector.tensor_copy(out=pos_columns[:], in_=pos_turned[:, :, MID :: P // 2])
-        pos_spread = psum.tile([NQ, PACK, P], F32, name="pos_spread")
+        gather("vector", pos_g, pos_pool, 0, HALF)
+        gather("scalar", pos_g, pos_pool, HALF, N)
+        pos_turned = psum.tile([P, PACK, P], F32, name="pos_turned", tag="bank_a")
+        for t in range(PACK - 1):
+            nc.tensor.transpose(pos_turned[:, t, :], pos_g[:, quarter(t)], ident[:])
+        nc.tensor.matmul(pos_turned[:, PACK - 1, :], lhsT=qpos_row[:], rhs=ident[:], is_transpose=True, start=True, stop=False)
+        nc.tensor.matmul(pos_turned[:, PACK - 1, :], lhsT=pos_g[:, quarter(PACK - 1)], rhs=ident[:], is_transpose=True, start=False, stop=True)
+        gather("vector", planes01[:, 0, :], k_pool[0], 0, N)
+        gather("scalar", vs_g, vs_pool, HALF, N)
+        gather("vector", vs_g, vs_pool, 0, HALF)
+        pos_columns = keep.tile([P, PACK, 2], F32, name="pos_columns", tag="k_got", align_bytes=64)
+        nc.scalar.copy(out=pos_columns[:], in_=pos_turned[:, :, MID :: P // 2])
+        pos_spread = psum.tile([NQ, PACK, P], F32, name="pos_spread", tag="bank_b")
         for t in range(PACK):
             nc.tensor.transpose(pos_spread[:, t, :], pos_columns[:, t, 1:2].to_broadcast([P, P]), ident[:])
-        cast("scalar", 1, 0, 0, CHUNK)
-        cast("vector", 1, 1, 0, SHARE1)
-        cast("scalar", 1, 1, SHARE1, CHUNK)
-        gather_k(1)
+        vs_turned = psum.tile([P, PACK, P], F32, name="vs_turned", tag="bank_a")
+        for t in range(PACK):
+            nc.tensor.transpose(vs_turned[:, t, :], vs_g[:, t::PACK], ident[:])
+        gather("scalar", planes01[:, 1, :], k_pool[1], 0, N)
 
-        q_bf = keep.tile([P, NQ * PACK], BF16, name="q_bf", tag="q_bf", align_bytes=64)
-        q_codes = keep.tile([P, NQ], U32, name="q_codes", align_bytes=64)
+        work = keep.tile([P, HALF + BESIDE // 2 + N], F32, name="work", align_bytes=64)
+        q_bf = work[:, :HALF].bitcast(BF16)
+        v_got1 = work[:, HALF - EARLY // 2 : N - EARLY // 2]
+        hide = work[:, HALF + BESIDE // 2 :]
+        nc.vector.tensor_scalar(
+            out=hide.rearrange("p (h t s) -> p h t s", h=2, t=PACK),
+            in0=pos_spread[:].rearrange("p j s -> p (j s)").rearrange("p (h s t) -> p h t s", h=2, t=PACK),
+            scalar1=pos_columns[:, PACK - 1, 0:1], scalar2=HIDDEN, op0=ALU.is_gt, op1=ALU.mult,
+        )
+        k_got = keep.tile([P, N, PACK], BF16, name="k_got", tag="k_got", align_bytes=64)
+        nc.vector.tensor_copy(out=k_got[:, :, 0:2], in_=planes01.rearrange("p e c -> p c e"))
+
+        gather("scalar", planes23[:, 0, :], k_pool[2], 0, N)
+        for j in (2, 3):
+            gather("vector", planes23[:, 1, :], k_pool[3], j * P, (j + 1) * P)
+        gather("scalar", planes23[:, 1, :], k_pool[3], 0, HALF)
+        for slots in (quarter(2), quarter(3), half(0)):
+            nc.vector.tensor_copy(out=k_got[:, slots, 2:4], in_=planes23[:, :, slots].rearrange("p e c -> p c e"))
+
+        q_codes = keep.tile([P, NQ], U32, name="q_codes", tag="q_codes", align_bytes=64)
         q_scales = keep.tile([P, NQ], U8, name="q_scales", align_bytes=64)
-        nc.scalar.copy(out=q_bf[:].rearrange("p (q j) -> p q j", j=PACK), in_=q_raw[:].rearrange("p j q -> p q j"))
-        nc.vector.quantize_mx(out=q_codes[:].bitcast(FP8X4), scales=q_scales[:], in_=q_bf[:])
+        nc.scalar.copy(out=q_bf.rearrange("p (q j) -> p q j", j=PACK), in_=q_raw[:].rearrange("p j q -> p q j"))
+        nc.vector.quantize_mx(out=q_codes[:].bitcast(FP8X4), scales=q_scales[:], in_=q_bf)
 
-        for h in (1, 0):
-            nc.vector.tensor_copy(
-                out=k_got[:].bitcast(I32)[:, h * N : (h + 1) * N].rearrange("p (c u) -> p c u", u=2),
-                in_=k_planes[:].bitcast(I32).rearrange("p (u c) -> p c u", u=2)[:, half(h), :],
-            )
-        side = keep.tile([NQ, N], F32, name="side", tag="raw11", align_bytes=64)
-        nc.scalar.activation(out=side[:], in_=pos_spread[:].rearrange("p t s -> p (t s)"), func=ACT.Sign, scale=-1.0, bias=pos_columns[:, 0, 0:1])
-        v1_pool = keep.tile([P, T], BF16, name="v1_pool", align_bytes=64)
-        for c in range(2):
-            nc.scalar.copy(out=v1_pool[:, c * CHUNK : (c + 1) * CHUNK], in_=v1_raw[c][:])
-        work = keep.tile([P, N + HALF], F32, name="work", tag="raw00", align_bytes=64)
-        bound = work[:, :N]
-        nc.scalar.activation(out=bound, in_=side[:], func=ACT.Copy, scale=CAP - MASKED, bias=CAP)
-
-        k_codes = keep.tile([P, N], U32, name="k_codes", align_bytes=64)
-        k_scales = [keep.tile([P, P], U8, name=f"k_scales{t}", align_bytes=64) for t in range(PACK)]
-        score = [psum.tile([NQ, P], F32, name=f"score{t}", tag=f"score{t}") for t in range(PACK)]
+        k_codes = keep.tile([P, N], U32, name="k_codes", tag="q_raw", align_bytes=64)
+        k_scales = [keep.tile([P, P], U8, name=f"k_scales{j}", align_bytes=64) for j in range(PACK)]
+        score = [psum.tile([NQ, P], F32, name=f"score{j}", tag=f"score{j}") for j in range(PACK)]
         capped = keep.tile([NQ, N], F32, name="capped", tag="capped", align_bytes=64)
-        for t in (2, 3, 0, 1):
-            nc.vector.quantize_mx(out=k_codes[:, quarter(t)].bitcast(FP8X4), scales=k_scales[t][:], in_=k_got[:, t * PACK * P : (t + 1) * PACK * P])
-        for t in (2, 3, 0, 1):
+        order = (2, 3, 0, 1)
+        for j in order:
+            nc.vector.quantize_mx(
+                out=k_codes[:, quarter(j)].bitcast(FP8X4), scales=k_scales[j][:], in_=k_got[:, quarter(j), :].rearrange("p c e -> p (c e)")
+            )
+        for j in order:
             nc.tensor.matmul_mx(
-                out=score[t][:], lhsT=q_codes[:].bitcast(FP8X4), lhsT_scale=q_scales[:],
-                rhs=k_codes[:, quarter(t)].bitcast(FP8X4), rhs_scale=k_scales[t][:], start=True, stop=True,
+                out=score[j][:], lhsT=q_codes[:].bitcast(FP8X4), lhsT_scale=q_scales[:],
+                rhs=k_codes[:, quarter(j)].bitcast(FP8X4), rhs_scale=k_scales[j][:], start=True, stop=True,
             )
 
         v_scales = [keep.tile([P, P], U8, name=f"v_scales{h}", align_bytes=64) for h in range(2)]
         v_codes = [keep.tile([P, P], U32, name=f"v_codes{h}", align_bytes=64) for h in range(2)]
 
-        def turn_v(h, planes, tag):
+        def turn_v(h, v_got, tag):
             turned = psum.tile([P, 2, P], F32, name=f"v_turned{h}", tag=tag)
             for u in range(2):
-                nc.tensor.transpose(turned[:, u, :], planes[u], ident[:])
+                nc.tensor.transpose(turned[:, u, :], v_got[:, u::2], ident[:])
             return turned[:].rearrange("p u e -> p e u")
 
         def words(v_bf):
             return v_bf[:].bitcast(F32).rearrange("p (e u) -> p e u", u=2)
 
-        v_got0 = work[:, N - LATE // 2 : N - LATE // 2 + HALF]
-        nc.vector.tensor_copy(v_got0[:, LATE // 2 :].bitcast(BF16), v0_pool[:].indirect(offsets[:, LATE // 16 :]))
-        for t in (2, 3, 0, 1):
-            nc.scalar.activation(out=capped[:, quarter(t)], in_=score[t][:], func=ACT.Tanh, scale=1.0 / CAP)
+        gather("scalar", v_got1.bitcast(BF16), v_pool[1], EARLY, EARLY + BESIDE)
+        gather("vector", v_got1.bitcast(BF16), v_pool[1], 0, EARLY)
+        dealt = capped[:].rearrange("p (h t j s) -> p h j t s", h=2, t=PACK, j=2)
+        for j in order:
+            nc.scalar.activation(out=dealt[:, j // 2, j % 2, :, :], in_=score[j][:].rearrange("p (s t) -> p t s", t=PACK), func=ACT.Tanh, scale=1.0 / CAP)
         visible = keep.tile([NQ, N], F32, name="visible", tag="visible", align_bytes=64)
         for h in (1, 0):
-            nc.vector.scalar_tensor_tensor(out=visible[:, half(h)], in0=capped[:, half(h)], scalar=CAP, in1=bound[:, half(h)], op0=ALU.mult, op1=ALU.min)
-        nc.vector.tensor_copy(v_got0[:, : LATE // 2].bitcast(BF16), v0_pool[:].indirect(offsets[:, : LATE // 16]))
-        v_got1 = keep.tile([P, HALF], F32, name="v_got1", align_bytes=64)
-        nc.scalar.activation(out=v_got1[:].bitcast(BF16).rearrange("p (u s h) -> p s u h", u=2, h=2), in_=v1_pool[:].indirect(offsets[:]), func=ACT.Copy)
+            nc.vector.scalar_tensor_tensor(out=visible[:, half(h)], in0=capped[:, half(h)], scalar=CAP, in1=hide[:, half(h)], op0=ALU.mult, op1=ALU.add)
+        gather("vector", v_got1.bitcast(BF16), v_pool[1], EARLY + BESIDE, N)
+        v_got0 = keep.tile([P, HALF], F32, name="v_got0", tag="q_codes", align_bytes=64)
+        gather("scalar", v_got0[:].bitcast(BF16), v_pool[0], 0, N)
         neg_max = keep.tile([NQ, 1], F32, name="neg_max")
         nc.vector.tensor_reduce(out=neg_max[:], in_=visible[:], axis=mybir.AxisListType.X, op=ALU.max, negate=True)
 
-        vs_turned = psum.tile([P, PACK, P], F32, name="vs_turned", tag="bank_b")
-        for t in range(PACK):
-            nc.tensor.transpose(vs_turned[:, t, :], vs_g[:, t::PACK], ident[:])
-        vs_columns = work[:, HALF : HALF + PACK]
+        vs_columns = hide[:, HALF - PACK : HALF]
         nc.vector.tensor_copy(out=vs_columns, in_=vs_turned[:, :, LAST])
-        v_turned0 = turn_v(0, [v_got0[:, u::2] for u in range(2)], "score2")
-        v_turned1 = turn_v(1, [v_got1[:, quarter(u)] for u in range(2)], "score3")
-        v_bf0 = keep.tile([P, P * PACK], BF16, name="v_bf0", tag="capped", align_bytes=64)
-        nc.vector.tensor_copy(out=words(v_bf0), in_=v_turned0)
-        nc.vector.quantize_mx(out=v_codes[0][:].bitcast(FP8X4), scales=v_scales[0][:], in_=v_bf0[:])
+        v_turned1 = turn_v(1, v_got1, "score2")
+        v_turned0 = turn_v(0, v_got0[:], "score3")
+        v_bf1 = keep.tile([P, P * PACK], BF16, name="v_bf1", tag="capped", align_bytes=64)
+        nc.vector.tensor_copy(out=words(v_bf1), in_=v_turned1)
+        nc.vector.quantize_mx(out=v_codes[1][:].bitcast(FP8X4), scales=v_scales[1][:], in_=v_bf1[:])
         prob = keep.tile([NQ, N], F32, name="prob")
         sums = [keep.tile([NQ, 1], F32, name=f"row_sum{h}") for h in range(2)]
         p_turned = psum.tile([P, PACK, NQ], F32, name="p_turned")
-        for h in range(2):
-            nc.scalar.activation(out=prob[:, half(h)], in_=visible[:, half(h)], func=ACT.Exp, bias=neg_max[:, 0:1], accum_out=sums[h][:])
+        by_place = visible[:].rearrange("p (h t s) -> p t h s", h=2, t=PACK)
+        for u in range(2):
+            nc.scalar.activation(
+                out=prob[:, half(u)].rearrange("p (t h s) -> p t h s", t=2, h=2), in_=by_place[:, 2 * u : 2 * u + 2, :, :],
+                func=ACT.Exp, bias=neg_max[:, 0:1], accum_out=sums[u][:],
+            )
         for t in range(PACK):
-            nc.tensor.transpose(p_turned[:, t, :], prob[:, t * P : (t + 1) * P], ident[:])
-        v_bf1 = keep.tile([P, P * PACK], BF16, name="v_bf1", tag="visible", align_bytes=64)
-        nc.scalar.copy(out=words(v_bf1), in_=v_turned1)
+            nc.tensor.transpose(p_turned[:, t, :], prob[:, quarter(t)], ident[:])
+        v_bf0 = keep.tile([P, P * PACK], BF16, name="v_bf0", tag="visible", align_bytes=64)
+        nc.scalar.copy(out=words(v_bf0), in_=v_turned0)
 
         w_bf = keep.tile([P, NQ * PACK], BF16, name="w_bf", align_bytes=64)
         w_codes = keep.tile([P, NQ], U32, name="w_codes", align_bytes=64)
         w_scales = keep.tile([P, NQ], U8, name="w_scales", align_bytes=64)
         row_sum = keep.tile([NQ, 1], F32, name="row_sum")
-        inverse = work[:, HALF : HALF + 1]
+        inverse = vs_columns[:, 0:1]
         nc.vector.tensor_tensor(out=row_sum[:], in0=sums[0][:], in1=sums[1][:], op=ALU.add)
         rows = [slice(h * NQ // 2, (h + 1) * NQ // 2) for h in range(2)]
         for h in range(2):
@@ -213,11 +200,11 @@ def tile_attend_x_draft_cap_topk_kernel(tc, qT, kT, vT, vs, pos, qpos, offs, out
                 in1=vs_columns.unsqueeze(1).to_broadcast([P, NQ // 2, PACK]), op=ALU.mult,
             )
         nc.vector.quantize_mx(out=w_codes[:, rows[0]].bitcast(FP8X4), scales=w_scales[:, rows[0]], in_=w_bf[:, half(0)])
-        nc.vector.quantize_mx(out=v_codes[1][:].bitcast(FP8X4), scales=v_scales[1][:], in_=v_bf1[:])
+        nc.vector.quantize_mx(out=v_codes[0][:].bitcast(FP8X4), scales=v_scales[0][:], in_=v_bf0[:])
         nc.vector.quantize_mx(out=w_codes[:, rows[1]].bitcast(FP8X4), scales=w_scales[:, rows[1]], in_=w_bf[:, half(1)])
         nc.vector.reciprocal(out=inverse, in_=row_sum[:])
         result = keep.tile([NQ, DV], F32, name="result")
-        for h, tag in enumerate(("bank_a", "bank_b")):
+        for h, tag in ((1, "bank_a"), (0, "bank_b")):
             cols = slice(h * P, (h + 1) * P)
             y = psum.tile([NQ, P], F32, name=f"y{h}", tag=tag)
             nc.tensor.matmul_mx(

@@ -13,8 +13,7 @@ P = 128
 PACK = 4
 HALF = N // 2
 FIRST = T // 4
-EARLY = 256
-BESIDE = 160
+LATE = 96
 LAST = P - 1
 MID = P // 2 - 1
 
@@ -101,10 +100,11 @@ def tile_attend_x_draft_cap_topk_kernel(tc, qT, kT, vT, vs, pos, qpos, offs, out
             nc.tensor.transpose(vs_turned[:, t, :], vs_g[:, t::PACK], ident[:])
         gather("scalar", planes01[:, 1, :], k_pool[1], 0, N)
 
-        work = keep.tile([P, HALF + BESIDE // 2 + N], F32, name="work", align_bytes=64)
+        work = keep.tile([P, HALF + P + N], F32, name="work", align_bytes=64)
         q_bf = work[:, :HALF].bitcast(BF16)
-        v_got1 = work[:, HALF - EARLY // 2 : N - EARLY // 2]
-        hide = work[:, HALF + BESIDE // 2 :]
+        v_got1 = work[:, P : P + HALF]
+        hide = work[:, HALF + P :]
+        v_got0 = hide[:, HALF - LATE // 2 : N - LATE // 2]
         nc.vector.tensor_scalar(
             out=hide.rearrange("p (h t s) -> p h t s", h=2, t=PACK),
             in0=pos_spread[:].rearrange("p j s -> p (j s)").rearrange("p (h s t) -> p h t s", h=2, t=PACK),
@@ -113,6 +113,9 @@ def tile_attend_x_draft_cap_topk_kernel(tc, qT, kT, vT, vs, pos, qpos, offs, out
         k_got = keep.tile([P, N, PACK], BF16, name="k_got", tag="k_got", align_bytes=64)
         nc.vector.tensor_copy(out=k_got[:, :, 0:2], in_=planes01.rearrange("p e c -> p c e"))
 
+        vs_tile = keep.tile([P, PACK], F32, name="vs_tile")
+        vs_columns = vs_tile[:]
+        nc.vector.tensor_copy(out=vs_columns, in_=vs_turned[:, :, LAST])
         gather("scalar", planes23[:, 0, :], k_pool[2], 0, N)
         for j in (2, 3):
             gather("vector", planes23[:, 1, :], k_pool[3], j * P, (j + 1) * P)
@@ -120,9 +123,9 @@ def tile_attend_x_draft_cap_topk_kernel(tc, qT, kT, vT, vs, pos, qpos, offs, out
         for slots in (quarter(2), quarter(3), half(0)):
             nc.vector.tensor_copy(out=k_got[:, slots, 2:4], in_=planes23[:, :, slots].rearrange("p e c -> p c e"))
 
-        q_codes = keep.tile([P, NQ], U32, name="q_codes", tag="q_codes", align_bytes=64)
+        q_codes = keep.tile([P, NQ], U32, name="q_codes", align_bytes=64)
         q_scales = keep.tile([P, NQ], U8, name="q_scales", align_bytes=64)
-        nc.scalar.copy(out=q_bf.rearrange("p (q j) -> p q j", j=PACK), in_=q_raw[:].rearrange("p j q -> p q j"))
+        nc.scalar.copy(out=q_bf.rearrange("p (c i j) -> p c j i", i=PACK, j=PACK), in_=q_raw[:].rearrange("p j (c i) -> p c j i", i=PACK))
         nc.vector.quantize_mx(out=q_codes[:].bitcast(FP8X4), scales=q_scales[:], in_=q_bf)
 
         k_codes = keep.tile([P, N], U32, name="k_codes", tag="q_raw", align_bytes=64)
@@ -152,27 +155,26 @@ def tile_attend_x_draft_cap_topk_kernel(tc, qT, kT, vT, vs, pos, qpos, offs, out
         def words(v_bf):
             return v_bf[:].bitcast(F32).rearrange("p (e u) -> p e u", u=2)
 
-        gather("scalar", v_got1.bitcast(BF16), v_pool[1], EARLY, EARLY + BESIDE)
-        gather("vector", v_got1.bitcast(BF16), v_pool[1], 0, EARLY)
+        gather("scalar", v_got1.bitcast(BF16), v_pool[1], HALF, N)
+        gather("vector", v_got1.bitcast(BF16), v_pool[1], 0, HALF)
         dealt = capped[:].rearrange("p (h t j s) -> p h j t s", h=2, t=PACK, j=2)
         for j in order:
             nc.scalar.activation(out=dealt[:, j // 2, j % 2, :, :], in_=score[j][:].rearrange("p (s t) -> p t s", t=PACK), func=ACT.Tanh, scale=1.0 / CAP)
         visible = keep.tile([NQ, N], F32, name="visible", tag="visible", align_bytes=64)
-        for h in (1, 0):
-            nc.vector.scalar_tensor_tensor(out=visible[:, half(h)], in0=capped[:, half(h)], scalar=CAP, in1=hide[:, half(h)], op0=ALU.mult, op1=ALU.add)
-        gather("vector", v_got1.bitcast(BF16), v_pool[1], EARLY + BESIDE, N)
-        v_got0 = keep.tile([P, HALF], F32, name="v_got0", tag="q_codes", align_bytes=64)
-        gather("scalar", v_got0[:].bitcast(BF16), v_pool[0], 0, N)
+        nc.vector.scalar_tensor_tensor(out=visible[:, half(1)], in0=capped[:, half(1)], scalar=CAP, in1=hide[:, half(1)], op0=ALU.mult, op1=ALU.add)
+        for j in range(2):
+            part = [x[:, half(0)].rearrange("p (t j s) -> p j t s", t=PACK, j=2)[:, j, :, :] for x in (visible, capped, hide)]
+            nc.vector.scalar_tensor_tensor(out=part[0], in0=part[1], scalar=CAP, in1=part[2], op0=ALU.mult, op1=ALU.add)
+        gather("vector", v_got0.bitcast(BF16), v_pool[0], 0, LATE)
+        gather("scalar", v_got0.bitcast(BF16), v_pool[0], LATE, N)
         neg_max = keep.tile([NQ, 1], F32, name="neg_max")
         nc.vector.tensor_reduce(out=neg_max[:], in_=visible[:], axis=mybir.AxisListType.X, op=ALU.max, negate=True)
 
-        vs_columns = hide[:, HALF - PACK : HALF]
-        nc.vector.tensor_copy(out=vs_columns, in_=vs_turned[:, :, LAST])
         v_turned1 = turn_v(1, v_got1, "score2")
-        v_turned0 = turn_v(0, v_got0[:], "score3")
-        v_bf1 = keep.tile([P, P * PACK], BF16, name="v_bf1", tag="capped", align_bytes=64)
-        nc.vector.tensor_copy(out=words(v_bf1), in_=v_turned1)
-        nc.vector.quantize_mx(out=v_codes[1][:].bitcast(FP8X4), scales=v_scales[1][:], in_=v_bf1[:])
+        v_turned0 = turn_v(0, v_got0, "score3")
+        v_bf0 = keep.tile([P, P * PACK], BF16, name="v_bf0", tag="capped", align_bytes=64)
+        nc.vector.tensor_copy(out=words(v_bf0), in_=v_turned0)
+        nc.vector.quantize_mx(out=v_codes[0][:].bitcast(FP8X4), scales=v_scales[0][:], in_=v_bf0[:])
         prob = keep.tile([NQ, N], F32, name="prob")
         sums = [keep.tile([NQ, 1], F32, name=f"row_sum{h}") for h in range(2)]
         p_turned = psum.tile([P, PACK, NQ], F32, name="p_turned")
@@ -184,8 +186,8 @@ def tile_attend_x_draft_cap_topk_kernel(tc, qT, kT, vT, vs, pos, qpos, offs, out
             )
         for t in range(PACK):
             nc.tensor.transpose(p_turned[:, t, :], prob[:, quarter(t)], ident[:])
-        v_bf0 = keep.tile([P, P * PACK], BF16, name="v_bf0", tag="visible", align_bytes=64)
-        nc.scalar.copy(out=words(v_bf0), in_=v_turned0)
+        v_bf1 = keep.tile([P, P * PACK], BF16, name="v_bf1", tag="visible", align_bytes=64)
+        nc.scalar.copy(out=words(v_bf1), in_=v_turned1)
 
         w_bf = keep.tile([P, NQ * PACK], BF16, name="w_bf", align_bytes=64)
         w_codes = keep.tile([P, NQ], U32, name="w_codes", align_bytes=64)
@@ -200,11 +202,11 @@ def tile_attend_x_draft_cap_topk_kernel(tc, qT, kT, vT, vs, pos, qpos, offs, out
                 in1=vs_columns.unsqueeze(1).to_broadcast([P, NQ // 2, PACK]), op=ALU.mult,
             )
         nc.vector.quantize_mx(out=w_codes[:, rows[0]].bitcast(FP8X4), scales=w_scales[:, rows[0]], in_=w_bf[:, half(0)])
-        nc.vector.quantize_mx(out=v_codes[0][:].bitcast(FP8X4), scales=v_scales[0][:], in_=v_bf0[:])
+        nc.vector.quantize_mx(out=v_codes[1][:].bitcast(FP8X4), scales=v_scales[1][:], in_=v_bf1[:])
         nc.vector.quantize_mx(out=w_codes[:, rows[1]].bitcast(FP8X4), scales=w_scales[:, rows[1]], in_=w_bf[:, half(1)])
         nc.vector.reciprocal(out=inverse, in_=row_sum[:])
         result = keep.tile([NQ, DV], F32, name="result")
-        for h, tag in ((1, "bank_a"), (0, "bank_b")):
+        for h, tag in ((0, "bank_a"), (1, "bank_b")):
             cols = slice(h * P, (h + 1) * P)
             y = psum.tile([NQ, P], F32, name=f"y{h}", tag=tag)
             nc.tensor.matmul_mx(

@@ -13,6 +13,7 @@ P = 128
 PACK = 4
 HALF = N // 2
 FIRST = T // 4
+BESIDE = 352
 LATE = 96
 LAST = P - 1
 MID = P // 2 - 1
@@ -100,11 +101,10 @@ def tile_attend_x_draft_cap_topk_kernel(tc, qT, kT, vT, vs, pos, qpos, offs, out
             nc.tensor.transpose(vs_turned[:, t, :], vs_g[:, t::PACK], ident[:])
         gather("scalar", planes01[:, 1, :], k_pool[1], 0, N)
 
-        work = keep.tile([P, HALF + P + N], F32, name="work", align_bytes=64)
+        work = keep.tile([P, HALF + BESIDE // 2 + N], F32, name="work", align_bytes=64)
         q_bf = work[:, :HALF].bitcast(BF16)
-        v_got1 = work[:, P : P + HALF]
-        hide = work[:, HALF + P :]
-        v_got0 = hide[:, HALF - LATE // 2 : N - LATE // 2]
+        v_got1 = work[:, BESIDE // 2 : BESIDE // 2 + HALF]
+        hide = work[:, HALF + BESIDE // 2 :]
         nc.vector.tensor_scalar(
             out=hide.rearrange("p (h t s) -> p h t s", h=2, t=PACK),
             in0=pos_spread[:].rearrange("p j s -> p (j s)").rearrange("p (h s t) -> p h t s", h=2, t=PACK),
@@ -123,7 +123,7 @@ def tile_attend_x_draft_cap_topk_kernel(tc, qT, kT, vT, vs, pos, qpos, offs, out
         for slots in (quarter(2), quarter(3), half(0)):
             nc.vector.tensor_copy(out=k_got[:, slots, 2:4], in_=planes23[:, :, slots].rearrange("p e c -> p c e"))
 
-        q_codes = keep.tile([P, NQ], U32, name="q_codes", align_bytes=64)
+        q_codes = keep.tile([P, NQ], U32, name="q_codes", tag="q_codes", align_bytes=64)
         q_scales = keep.tile([P, NQ], U8, name="q_scales", align_bytes=64)
         nc.scalar.copy(out=q_bf.rearrange("p (c i j) -> p c j i", i=PACK, j=PACK), in_=q_raw[:].rearrange("p j (c i) -> p c j i", i=PACK))
         nc.vector.quantize_mx(out=q_codes[:].bitcast(FP8X4), scales=q_scales[:], in_=q_bf)
@@ -155,8 +155,11 @@ def tile_attend_x_draft_cap_topk_kernel(tc, qT, kT, vT, vs, pos, qpos, offs, out
         def words(v_bf):
             return v_bf[:].bitcast(F32).rearrange("p (e u) -> p e u", u=2)
 
-        gather("scalar", v_got1.bitcast(BF16), v_pool[1], HALF, N)
-        gather("vector", v_got1.bitcast(BF16), v_pool[1], 0, HALF)
+        v_late = keep.tile([P, HALF], F32, name="v_late", tag="q_codes", align_bytes=64)
+        v_got0 = v_late[:]
+        gather("scalar", v_got1.bitcast(BF16), v_pool[1], N - BESIDE, N)
+        gather("vector", v_got1.bitcast(BF16), v_pool[1], 0, N - BESIDE)
+        gather("vector", v_got0.bitcast(BF16), v_pool[0], N - LATE, N)
         dealt = capped[:].rearrange("p (h t j s) -> p h j t s", h=2, t=PACK, j=2)
         for j in order:
             nc.scalar.activation(out=dealt[:, j // 2, j % 2, :, :], in_=score[j][:].rearrange("p (s t) -> p t s", t=PACK), func=ACT.Tanh, scale=1.0 / CAP)
@@ -165,36 +168,37 @@ def tile_attend_x_draft_cap_topk_kernel(tc, qT, kT, vT, vs, pos, qpos, offs, out
         for j in range(2):
             part = [x[:, half(0)].rearrange("p (t j s) -> p j t s", t=PACK, j=2)[:, j, :, :] for x in (visible, capped, hide)]
             nc.vector.scalar_tensor_tensor(out=part[0], in0=part[1], scalar=CAP, in1=part[2], op0=ALU.mult, op1=ALU.add)
-        gather("vector", v_got0.bitcast(BF16), v_pool[0], 0, LATE)
-        gather("scalar", v_got0.bitcast(BF16), v_pool[0], LATE, N)
+        gather("scalar", v_got0.bitcast(BF16), v_pool[0], 0, N - LATE)
         neg_max = keep.tile([NQ, 1], F32, name="neg_max")
-        nc.vector.tensor_reduce(out=neg_max[:], in_=visible[:], axis=mybir.AxisListType.X, op=ALU.max, negate=True)
+        negated = keep.tile([NQ, N], F32, name="negated", tag="negated", align_bytes=64)
+        nc.vector.tensor_scalar(out=negated[:], in0=visible[:], scalar1=-1.0, scalar2=None, op0=ALU.mult, op1=ALU.min, accum_out=neg_max[:])
 
         v_turned1 = turn_v(1, v_got1, "score2")
         v_turned0 = turn_v(0, v_got0, "score3")
-        v_bf0 = keep.tile([P, P * PACK], BF16, name="v_bf0", tag="capped", align_bytes=64)
-        nc.vector.tensor_copy(out=words(v_bf0), in_=v_turned0)
-        nc.vector.quantize_mx(out=v_codes[0][:].bitcast(FP8X4), scales=v_scales[0][:], in_=v_bf0[:])
+        v_bf1 = keep.tile([P, P * PACK], BF16, name="v_bf1", tag="visible", align_bytes=64)
+        nc.vector.tensor_copy(out=words(v_bf1), in_=v_turned1)
+        nc.vector.quantize_mx(out=v_codes[1][:].bitcast(FP8X4), scales=v_scales[1][:], in_=v_bf1[:])
         prob = keep.tile([NQ, N], F32, name="prob")
-        sums = [keep.tile([NQ, 1], F32, name=f"row_sum{h}") for h in range(2)]
+        pieces = ((0, 2), (2, 3), (3, 4))
+        sums = keep.tile([NQ, len(pieces)], F32, name="sums")
         p_turned = psum.tile([P, PACK, NQ], F32, name="p_turned")
-        by_place = visible[:].rearrange("p (h t s) -> p t h s", h=2, t=PACK)
-        for u in range(2):
+        by_place = negated[:].rearrange("p (h t s) -> p t h s", h=2, t=PACK)
+        for i, (a, b) in enumerate(pieces):
             nc.scalar.activation(
-                out=prob[:, half(u)].rearrange("p (t h s) -> p t h s", t=2, h=2), in_=by_place[:, 2 * u : 2 * u + 2, :, :],
-                func=ACT.Exp, bias=neg_max[:, 0:1], accum_out=sums[u][:],
+                out=prob[:, a * P : b * P].rearrange("p (t h s) -> p t h s", t=b - a, h=2), in_=by_place[:, a:b, :, :],
+                func=ACT.Exp, scale=-1.0, bias=neg_max[:, 0:1], accum_out=sums[:, i : i + 1],
             )
         for t in range(PACK):
             nc.tensor.transpose(p_turned[:, t, :], prob[:, quarter(t)], ident[:])
-        v_bf1 = keep.tile([P, P * PACK], BF16, name="v_bf1", tag="visible", align_bytes=64)
-        nc.scalar.copy(out=words(v_bf1), in_=v_turned1)
+        v_bf0 = keep.tile([P, P * PACK], BF16, name="v_bf0", tag="negated", align_bytes=64)
+        nc.scalar.copy(out=words(v_bf0), in_=v_turned0)
 
         w_bf = keep.tile([P, NQ * PACK], BF16, name="w_bf", align_bytes=64)
         w_codes = keep.tile([P, NQ], U32, name="w_codes", align_bytes=64)
         w_scales = keep.tile([P, NQ], U8, name="w_scales", align_bytes=64)
         row_sum = keep.tile([NQ, 1], F32, name="row_sum")
         inverse = vs_columns[:, 0:1]
-        nc.vector.tensor_tensor(out=row_sum[:], in0=sums[0][:], in1=sums[1][:], op=ALU.add)
+        nc.vector.tensor_reduce(out=row_sum[:], in_=sums[:], axis=mybir.AxisListType.X, op=ALU.add)
         rows = [slice(h * NQ // 2, (h + 1) * NQ // 2) for h in range(2)]
         for h in range(2):
             nc.vector.tensor_tensor(
@@ -202,11 +206,11 @@ def tile_attend_x_draft_cap_topk_kernel(tc, qT, kT, vT, vs, pos, qpos, offs, out
                 in1=vs_columns.unsqueeze(1).to_broadcast([P, NQ // 2, PACK]), op=ALU.mult,
             )
         nc.vector.quantize_mx(out=w_codes[:, rows[0]].bitcast(FP8X4), scales=w_scales[:, rows[0]], in_=w_bf[:, half(0)])
-        nc.vector.quantize_mx(out=v_codes[1][:].bitcast(FP8X4), scales=v_scales[1][:], in_=v_bf1[:])
+        nc.vector.quantize_mx(out=v_codes[0][:].bitcast(FP8X4), scales=v_scales[0][:], in_=v_bf0[:])
         nc.vector.quantize_mx(out=w_codes[:, rows[1]].bitcast(FP8X4), scales=w_scales[:, rows[1]], in_=w_bf[:, half(1)])
         nc.vector.reciprocal(out=inverse, in_=row_sum[:])
         result = keep.tile([NQ, DV], F32, name="result")
-        for h, tag in ((0, "bank_a"), (1, "bank_b")):
+        for h, tag in ((1, "bank_a"), (0, "bank_b")):
             cols = slice(h * P, (h + 1) * P)
             y = psum.tile([NQ, P], F32, name=f"y{h}", tag=tag)
             nc.tensor.matmul_mx(

@@ -13,8 +13,7 @@ P = 128
 PACK = 4
 HALF = N // 2
 FIRST = T // 4
-BESIDE = 352
-LATE = 96
+BESIDE = 256
 LAST = P - 1
 MID = P // 2 - 1
 
@@ -113,9 +112,6 @@ def tile_attend_x_draft_cap_topk_kernel(tc, qT, kT, vT, vs, pos, qpos, offs, out
         k_got = keep.tile([P, N, PACK], BF16, name="k_got", tag="k_got", align_bytes=64)
         nc.vector.tensor_copy(out=k_got[:, :, 0:2], in_=planes01.rearrange("p e c -> p c e"))
 
-        vs_tile = keep.tile([P, PACK], F32, name="vs_tile")
-        vs_columns = vs_tile[:]
-        nc.vector.tensor_copy(out=vs_columns, in_=vs_turned[:, :, LAST])
         gather("scalar", planes23[:, 0, :], k_pool[2], 0, N)
         for j in (2, 3):
             gather("vector", planes23[:, 1, :], k_pool[3], j * P, (j + 1) * P)
@@ -153,13 +149,12 @@ def tile_attend_x_draft_cap_topk_kernel(tc, qT, kT, vT, vs, pos, qpos, offs, out
             return turned[:].rearrange("p u e -> p e u")
 
         def words(v_bf):
-            return v_bf[:].bitcast(F32).rearrange("p (e u) -> p e u", u=2)
+            return v_bf.bitcast(F32).rearrange("p (e u) -> p e u", u=2)
 
         v_late = keep.tile([P, HALF], F32, name="v_late", tag="q_codes", align_bytes=64)
         v_got0 = v_late[:]
         gather("scalar", v_got1.bitcast(BF16), v_pool[1], N - BESIDE, N)
         gather("vector", v_got1.bitcast(BF16), v_pool[1], 0, N - BESIDE)
-        gather("vector", v_got0.bitcast(BF16), v_pool[0], N - LATE, N)
         dealt = capped[:].rearrange("p (h t j s) -> p h j t s", h=2, t=PACK, j=2)
         for j in order:
             nc.scalar.activation(out=dealt[:, j // 2, j % 2, :, :], in_=score[j][:].rearrange("p (s t) -> p t s", t=PACK), func=ACT.Tanh, scale=1.0 / CAP)
@@ -168,16 +163,19 @@ def tile_attend_x_draft_cap_topk_kernel(tc, qT, kT, vT, vs, pos, qpos, offs, out
         for j in range(2):
             part = [x[:, half(0)].rearrange("p (t j s) -> p j t s", t=PACK, j=2)[:, j, :, :] for x in (visible, capped, hide)]
             nc.vector.scalar_tensor_tensor(out=part[0], in0=part[1], scalar=CAP, in1=part[2], op0=ALU.mult, op1=ALU.add)
-        gather("scalar", v_got0.bitcast(BF16), v_pool[0], 0, N - LATE)
+        gather("scalar", v_got0.bitcast(BF16), v_pool[0], 0, N)
         neg_max = keep.tile([NQ, 1], F32, name="neg_max")
         negated = keep.tile([NQ, N], F32, name="negated", tag="negated", align_bytes=64)
         nc.vector.tensor_scalar(out=negated[:], in0=visible[:], scalar1=-1.0, scalar2=None, op0=ALU.mult, op1=ALU.min, accum_out=neg_max[:])
 
         v_turned1 = turn_v(1, v_got1, "score2")
         v_turned0 = turn_v(0, v_got0, "score3")
-        v_bf1 = keep.tile([P, P * PACK], BF16, name="v_bf1", tag="visible", align_bytes=64)
+        after_max = keep.tile([P, HALF + PACK], F32, name="after_max", tag="visible", align_bytes=64)
+        v_bf1 = after_max[:, :HALF].bitcast(BF16)
+        vs_columns = after_max[:, HALF:]
+        nc.vector.tensor_copy(out=vs_columns, in_=vs_turned[:, :, LAST])
         nc.vector.tensor_copy(out=words(v_bf1), in_=v_turned1)
-        nc.vector.quantize_mx(out=v_codes[1][:].bitcast(FP8X4), scales=v_scales[1][:], in_=v_bf1[:])
+        nc.vector.quantize_mx(out=v_codes[1][:].bitcast(FP8X4), scales=v_scales[1][:], in_=v_bf1)
         prob = keep.tile([NQ, N], F32, name="prob")
         pieces = ((0, 2), (2, 3), (3, 4))
         sums = keep.tile([NQ, len(pieces)], F32, name="sums")
@@ -191,7 +189,7 @@ def tile_attend_x_draft_cap_topk_kernel(tc, qT, kT, vT, vs, pos, qpos, offs, out
         for t in range(PACK):
             nc.tensor.transpose(p_turned[:, t, :], prob[:, quarter(t)], ident[:])
         v_bf0 = keep.tile([P, P * PACK], BF16, name="v_bf0", tag="negated", align_bytes=64)
-        nc.scalar.copy(out=words(v_bf0), in_=v_turned0)
+        nc.scalar.copy(out=words(v_bf0[:]), in_=v_turned0)
 
         w_bf = keep.tile([P, NQ * PACK], BF16, name="w_bf", align_bytes=64)
         w_codes = keep.tile([P, NQ], U32, name="w_codes", align_bytes=64)

@@ -5,7 +5,8 @@ from concourse.masks import make_identity
 
 D, T, N, DV, NQ = 512, 1024, 512, 256, 128
 CAP = 2.0
-HIDDEN = -float(2**27)
+HIDDEN = float(2**27)
+STEEP = float(2**64)
 FLOPS = 2 * D * NQ * N + 2 * N * NQ * DV
 BYTES = 4 * (D * T + DV * T + D * NQ + 2 * T + NQ + NQ * DV) + 2 * 128 * N // 16
 
@@ -14,6 +15,8 @@ PACK = 4
 HALF = N // 2
 FIRST = T // 4
 BESIDE = 256
+AHEAD = 192
+LATE = 96
 LAST = P - 1
 MID = P // 2 - 1
 
@@ -74,10 +77,11 @@ def tile_attend_x_draft_cap_topk_kernel(tc, qT, kT, vT, vs, pos, qpos, offs, out
             else:
                 nc.vector.tensor_copy(dst[:, a:b], picked)
 
-        front = keep.tile([P, HALF + N], F32, name="front")
-        pos_g = front[:, HALF:]
-        planes01 = front[:].bitcast(BF16).rearrange("p (r c) -> p r c", c=N)[:, 0::2, :]
-        planes23 = keep.tile([P, 2, N], BF16, name="planes23")
+        stage = keep.tile([P, 3 * N - P], F32, name="stage")
+        pos_g = stage[:, :N]
+        planes23 = stage[:, N - P : 2 * N - P].bitcast(BF16).rearrange("p (e c) -> p e c", e=2)
+        planes01 = stage[:, 2 * N - P :].bitcast(BF16).rearrange("p (e c) -> p e c", e=2)
+        hide = stage[:, N + HALF : 2 * N + HALF]
         vs_g = keep.tile([P, N], F32, name="vs_g")
 
         gather("vector", pos_g, pos_pool, 0, HALF)
@@ -88,40 +92,41 @@ def tile_attend_x_draft_cap_topk_kernel(tc, qT, kT, vT, vs, pos, qpos, offs, out
         nc.tensor.matmul(pos_turned[:, PACK - 1, :], lhsT=qpos_row[:], rhs=ident[:], is_transpose=True, start=True, stop=False)
         nc.tensor.matmul(pos_turned[:, PACK - 1, :], lhsT=pos_g[:, quarter(PACK - 1)], rhs=ident[:], is_transpose=True, start=False, stop=True)
         gather("vector", planes01[:, 0, :], k_pool[0], 0, N)
-        gather("scalar", vs_g, vs_pool, HALF, N)
-        gather("vector", vs_g, vs_pool, 0, HALF)
-        pos_columns = keep.tile([P, PACK, 2], F32, name="pos_columns", tag="k_got", align_bytes=64)
-        nc.scalar.copy(out=pos_columns[:], in_=pos_turned[:, :, MID :: P // 2])
+        gather("scalar", vs_g, vs_pool, P, N)
+        gather("vector", vs_g, vs_pool, 0, P)
+        pos_columns = keep.tile([P, PACK, 2], F32, name="pos_columns")
+        nc.scalar.activation(out=pos_columns[:], in_=pos_turned[:, :, MID :: P // 2], func=ACT.Copy, scale=-STEEP)
         pos_spread = psum.tile([NQ, PACK, P], F32, name="pos_spread", tag="bank_b")
         for t in range(PACK):
             nc.tensor.transpose(pos_spread[:, t, :], pos_columns[:, t, 1:2].to_broadcast([P, P]), ident[:])
         vs_turned = psum.tile([P, PACK, P], F32, name="vs_turned", tag="bank_a")
         for t in range(PACK):
             nc.tensor.transpose(vs_turned[:, t, :], vs_g[:, t::PACK], ident[:])
-        gather("scalar", planes01[:, 1, :], k_pool[1], 0, N)
+        gather("scalar", planes01[:, 1, :], k_pool[1], 0, HALF)
+        gather("vector", planes01[:, 1, :], k_pool[1], HALF, N)
 
-        work = keep.tile([P, HALF + BESIDE // 2 + N], F32, name="work", align_bytes=64)
+        work = keep.tile([P, HALF + BESIDE // 2], F32, name="work", align_bytes=64)
         q_bf = work[:, :HALF].bitcast(BF16)
         v_got1 = work[:, BESIDE // 2 : BESIDE // 2 + HALF]
-        hide = work[:, HALF + BESIDE // 2 :]
-        nc.vector.tensor_scalar(
-            out=hide.rearrange("p (h t s) -> p h t s", h=2, t=PACK),
-            in0=pos_spread[:].rearrange("p j s -> p (j s)").rearrange("p (h s t) -> p h t s", h=2, t=PACK),
-            scalar1=pos_columns[:, PACK - 1, 0:1], scalar2=HIDDEN, op0=ALU.is_gt, op1=ALU.mult,
-        )
-        k_got = keep.tile([P, N, PACK], BF16, name="k_got", tag="k_got", align_bytes=64)
+        k_got = keep.tile([P, N, PACK], BF16, name="k_got", align_bytes=64)
         nc.vector.tensor_copy(out=k_got[:, :, 0:2], in_=planes01.rearrange("p e c -> p c e"))
 
-        gather("scalar", planes23[:, 0, :], k_pool[2], 0, N)
+        gather("scalar", planes23[:, 0, :], k_pool[2], 0, N - AHEAD)
+        gather("vector", planes23[:, 0, :], k_pool[2], N - AHEAD, N)
         for j in (2, 3):
             gather("vector", planes23[:, 1, :], k_pool[3], j * P, (j + 1) * P)
         gather("scalar", planes23[:, 1, :], k_pool[3], 0, HALF)
         for slots in (quarter(2), quarter(3), half(0)):
             nc.vector.tensor_copy(out=k_got[:, slots, 2:4], in_=planes23[:, :, slots].rearrange("p e c -> p c e"))
 
-        q_codes = keep.tile([P, NQ], U32, name="q_codes", tag="q_codes", align_bytes=64)
+        q_codes = keep.tile([P, NQ], U32, name="q_codes", align_bytes=64)
         q_scales = keep.tile([P, NQ], U8, name="q_scales", align_bytes=64)
         nc.scalar.copy(out=q_bf.rearrange("p (c i j) -> p c j i", i=PACK, j=PACK), in_=q_raw[:].rearrange("p j (c i) -> p c j i", i=PACK))
+        nc.scalar.activation(
+            out=hide.rearrange("p (h t s) -> p h t s", h=2, t=PACK),
+            in_=pos_spread[:].rearrange("p j s -> p (j s)").rearrange("p (h s t) -> p h t s", h=2, t=PACK),
+            func=ACT.Relu, scale=-1.0, bias=pos_columns[:, PACK - 1, 0:1],
+        )
         nc.vector.quantize_mx(out=q_codes[:].bitcast(FP8X4), scales=q_scales[:], in_=q_bf)
 
         k_codes = keep.tile([P, N], U32, name="k_codes", tag="q_raw", align_bytes=64)
@@ -151,33 +156,33 @@ def tile_attend_x_draft_cap_topk_kernel(tc, qT, kT, vT, vs, pos, qpos, offs, out
         def words(v_bf):
             return v_bf.bitcast(F32).rearrange("p (e u) -> p e u", u=2)
 
-        v_late = keep.tile([P, HALF], F32, name="v_late", tag="q_codes", align_bytes=64)
-        v_got0 = v_late[:]
+        v_got0 = hide[:, HALF - LATE // 2 : N - LATE // 2]
         gather("scalar", v_got1.bitcast(BF16), v_pool[1], N - BESIDE, N)
         gather("vector", v_got1.bitcast(BF16), v_pool[1], 0, N - BESIDE)
         dealt = capped[:].rearrange("p (h t j s) -> p h j t s", h=2, t=PACK, j=2)
         for j in order:
             nc.scalar.activation(out=dealt[:, j // 2, j % 2, :, :], in_=score[j][:].rearrange("p (s t) -> p t s", t=PACK), func=ACT.Tanh, scale=1.0 / CAP)
         visible = keep.tile([NQ, N], F32, name="visible", tag="visible", align_bytes=64)
-        nc.vector.scalar_tensor_tensor(out=visible[:, half(1)], in0=capped[:, half(1)], scalar=CAP, in1=hide[:, half(1)], op0=ALU.mult, op1=ALU.add)
+        nc.vector.scalar_tensor_tensor(out=visible[:, half(1)], in0=hide[:, half(1)], scalar=HIDDEN, in1=capped[:, half(1)], op0=ALU.min, op1=ALU.subtract)
         for j in range(2):
             part = [x[:, half(0)].rearrange("p (t j s) -> p j t s", t=PACK, j=2)[:, j, :, :] for x in (visible, capped, hide)]
-            nc.vector.scalar_tensor_tensor(out=part[0], in0=part[1], scalar=CAP, in1=part[2], op0=ALU.mult, op1=ALU.add)
-        gather("scalar", v_got0.bitcast(BF16), v_pool[0], 0, N)
+            nc.vector.scalar_tensor_tensor(out=part[0], in0=part[2], scalar=HIDDEN, in1=part[1], op0=ALU.min, op1=ALU.subtract)
+        gather("vector", v_got0.bitcast(BF16), v_pool[0], 0, LATE)
+        gather("scalar", v_got0.bitcast(BF16), v_pool[0], LATE, N)
         neg_max = keep.tile([NQ, 1], F32, name="neg_max")
         negated = keep.tile([NQ, N], F32, name="negated", tag="negated", align_bytes=64)
-        nc.vector.tensor_scalar(out=negated[:], in0=visible[:], scalar1=-1.0, scalar2=None, op0=ALU.mult, op1=ALU.min, accum_out=neg_max[:])
+        nc.vector.tensor_scalar(out=negated[:], in0=visible[:], scalar1=CAP, scalar2=None, op0=ALU.mult, op1=ALU.min, accum_out=neg_max[:])
 
         v_turned1 = turn_v(1, v_got1, "score2")
         v_turned0 = turn_v(0, v_got0, "score3")
         after_max = keep.tile([P, HALF + PACK], F32, name="after_max", tag="visible", align_bytes=64)
-        v_bf1 = after_max[:, :HALF].bitcast(BF16)
+        v_bf0 = after_max[:, :HALF].bitcast(BF16)
         vs_columns = after_max[:, HALF:]
         nc.vector.tensor_copy(out=vs_columns, in_=vs_turned[:, :, LAST])
-        nc.vector.tensor_copy(out=words(v_bf1), in_=v_turned1)
-        nc.vector.quantize_mx(out=v_codes[1][:].bitcast(FP8X4), scales=v_scales[1][:], in_=v_bf1)
+        nc.vector.tensor_copy(out=words(v_bf0), in_=v_turned0)
+        nc.vector.quantize_mx(out=v_codes[0][:].bitcast(FP8X4), scales=v_scales[0][:], in_=v_bf0)
         prob = keep.tile([NQ, N], F32, name="prob")
-        pieces = ((0, 2), (2, 3), (3, 4))
+        pieces = ((0, 2), (2, 4))
         sums = keep.tile([NQ, len(pieces)], F32, name="sums")
         p_turned = psum.tile([P, PACK, NQ], F32, name="p_turned")
         by_place = negated[:].rearrange("p (h t s) -> p t h s", h=2, t=PACK)
@@ -188,8 +193,8 @@ def tile_attend_x_draft_cap_topk_kernel(tc, qT, kT, vT, vs, pos, qpos, offs, out
             )
         for t in range(PACK):
             nc.tensor.transpose(p_turned[:, t, :], prob[:, quarter(t)], ident[:])
-        v_bf0 = keep.tile([P, P * PACK], BF16, name="v_bf0", tag="negated", align_bytes=64)
-        nc.scalar.copy(out=words(v_bf0[:]), in_=v_turned0)
+        v_bf1 = keep.tile([P, P * PACK], BF16, name="v_bf1", tag="negated", align_bytes=64)
+        nc.scalar.copy(out=words(v_bf1[:]), in_=v_turned1)
 
         w_bf = keep.tile([P, NQ * PACK], BF16, name="w_bf", align_bytes=64)
         w_codes = keep.tile([P, NQ], U32, name="w_codes", align_bytes=64)
@@ -204,11 +209,11 @@ def tile_attend_x_draft_cap_topk_kernel(tc, qT, kT, vT, vs, pos, qpos, offs, out
                 in1=vs_columns.unsqueeze(1).to_broadcast([P, NQ // 2, PACK]), op=ALU.mult,
             )
         nc.vector.quantize_mx(out=w_codes[:, rows[0]].bitcast(FP8X4), scales=w_scales[:, rows[0]], in_=w_bf[:, half(0)])
-        nc.vector.quantize_mx(out=v_codes[0][:].bitcast(FP8X4), scales=v_scales[0][:], in_=v_bf0[:])
+        nc.vector.quantize_mx(out=v_codes[1][:].bitcast(FP8X4), scales=v_scales[1][:], in_=v_bf1[:])
         nc.vector.quantize_mx(out=w_codes[:, rows[1]].bitcast(FP8X4), scales=w_scales[:, rows[1]], in_=w_bf[:, half(1)])
         nc.vector.reciprocal(out=inverse, in_=row_sum[:])
         result = keep.tile([NQ, DV], F32, name="result")
-        for h, tag in ((1, "bank_a"), (0, "bank_b")):
+        for h, tag in ((0, "bank_a"), (1, "bank_b")):
             cols = slice(h * P, (h + 1) * P)
             y = psum.tile([NQ, P], F32, name=f"y{h}", tag=tag)
             nc.tensor.matmul_mx(

@@ -14,9 +14,9 @@ P = 128
 PACK = 4
 HALF = N // 2
 FIRST = T // 4
-BESIDE = 256
+BESIDE = 192
 AHEAD = 192
-LATE = 96
+LATE = 128
 LAST = P - 1
 MID = P // 2 - 1
 
@@ -123,8 +123,8 @@ def tile_attend_x_draft_cap_topk_kernel(tc, qT, kT, vT, vs, pos, qpos, offs, out
         q_scales = keep.tile([P, NQ], U8, name="q_scales", align_bytes=64)
         nc.scalar.copy(out=q_bf.rearrange("p (c i j) -> p c j i", i=PACK, j=PACK), in_=q_raw[:].rearrange("p j (c i) -> p c j i", i=PACK))
         nc.scalar.activation(
-            out=hide.rearrange("p (h t s) -> p h t s", h=2, t=PACK),
-            in_=pos_spread[:].rearrange("p j s -> p (j s)").rearrange("p (h s t) -> p h t s", h=2, t=PACK),
+            out=hide.rearrange("p (j t s) -> p j t s", j=PACK, t=PACK),
+            in_=pos_spread[:].rearrange("p j (s t) -> p j t s", t=PACK),
             func=ACT.Relu, scale=-1.0, bias=pos_columns[:, PACK - 1, 0:1],
         )
         nc.vector.quantize_mx(out=q_codes[:].bitcast(FP8X4), scales=q_scales[:], in_=q_bf)
@@ -133,7 +133,7 @@ def tile_attend_x_draft_cap_topk_kernel(tc, qT, kT, vT, vs, pos, qpos, offs, out
         k_scales = [keep.tile([P, P], U8, name=f"k_scales{j}", align_bytes=64) for j in range(PACK)]
         score = [psum.tile([NQ, P], F32, name=f"score{j}", tag=f"score{j}") for j in range(PACK)]
         capped = keep.tile([NQ, N], F32, name="capped", tag="capped", align_bytes=64)
-        order = (2, 3, 0, 1)
+        order = (2, 3, 1, 0)
         for j in order:
             nc.vector.quantize_mx(
                 out=k_codes[:, quarter(j)].bitcast(FP8X4), scales=k_scales[j][:], in_=k_got[:, quarter(j), :].rearrange("p c e -> p (c e)")
@@ -159,14 +159,18 @@ def tile_attend_x_draft_cap_topk_kernel(tc, qT, kT, vT, vs, pos, qpos, offs, out
         v_got0 = hide[:, HALF - LATE // 2 : N - LATE // 2]
         gather("scalar", v_got1.bitcast(BF16), v_pool[1], N - BESIDE, N)
         gather("vector", v_got1.bitcast(BF16), v_pool[1], 0, N - BESIDE)
-        dealt = capped[:].rearrange("p (h t j s) -> p h j t s", h=2, t=PACK, j=2)
+
+        def dealt(tile, j):
+            return tile[:].rearrange("p (h t j s) -> p h j t s", h=2, t=PACK, j=2)[:, j // 2, j % 2, :, :]
+
         for j in order:
-            nc.scalar.activation(out=dealt[:, j // 2, j % 2, :, :], in_=score[j][:].rearrange("p (s t) -> p t s", t=PACK), func=ACT.Tanh, scale=1.0 / CAP)
+            nc.scalar.activation(out=dealt(capped, j), in_=score[j][:].rearrange("p (s t) -> p t s", t=PACK), func=ACT.Tanh, scale=1.0 / CAP)
         visible = keep.tile([NQ, N], F32, name="visible", tag="visible", align_bytes=64)
-        nc.vector.scalar_tensor_tensor(out=visible[:, half(1)], in0=hide[:, half(1)], scalar=HIDDEN, in1=capped[:, half(1)], op0=ALU.min, op1=ALU.subtract)
-        for j in range(2):
-            part = [x[:, half(0)].rearrange("p (t j s) -> p j t s", t=PACK, j=2)[:, j, :, :] for x in (visible, capped, hide)]
-            nc.vector.scalar_tensor_tensor(out=part[0], in0=part[2], scalar=HIDDEN, in1=part[1], op0=ALU.min, op1=ALU.subtract)
+        for j in order:
+            nc.vector.scalar_tensor_tensor(
+                out=dealt(visible, j), in0=hide[:, quarter(j)].rearrange("p (t s) -> p t s", t=PACK), scalar=HIDDEN,
+                in1=dealt(capped, j), op0=ALU.min, op1=ALU.subtract,
+            )
         gather("vector", v_got0.bitcast(BF16), v_pool[0], 0, LATE)
         gather("scalar", v_got0.bitcast(BF16), v_pool[0], LATE, N)
         neg_max = keep.tile([NQ, 1], F32, name="neg_max")

@@ -15,7 +15,7 @@ PACK = 4
 HALF = N // 2
 FIRST = T // 4
 BESIDE = 192
-AHEAD = 192
+SHARE = 192
 LATE = 128
 LAST = P - 1
 MID = P // 2 - 1
@@ -35,12 +35,13 @@ def tile_attend_x_draft_cap_topk_kernel(tc, qT, kT, vT, vs, pos, qpos, offs, out
     with ExitStack() as ctx:
         keep = ctx.enter_context(tc.tile_pool(name="keep", bufs=1))
         psum = ctx.enter_context(tc.psum_pool(name="psum", bufs=1))
+        reuse = ctx.enter_context(tc.tile_pool(name="reuse", bufs=1))
 
         offsets = keep.tile([P, N // 16], U16, name="offsets")
         qpos_row = keep.tile([P, NQ], F32, name="qpos_row")
         pos_pool = keep.tile([P, T], F32, name="pos_pool")
         vs_pool = keep.tile([P, T], F32, name="vs_pool")
-        q_raw = keep.tile([P, PACK, NQ], F32, name="q_raw", tag="q_raw", align_bytes=64)
+        q_raw = reuse.tile([P, PACK, NQ], F32, name="q_raw", align_bytes=64, offset=1024)
         k_rows = kT.rearrange("(p j) t -> p j t", j=PACK)
         k_pool = [keep.tile([P, T], F32, name=f"k_pool{j}") for j in range(PACK)]
         v_pool = [keep.tile([P, T], F32, name=f"v_pool{h}") for h in range(2)]
@@ -77,11 +78,8 @@ def tile_attend_x_draft_cap_topk_kernel(tc, qT, kT, vT, vs, pos, qpos, offs, out
             else:
                 nc.vector.tensor_copy(dst[:, a:b], picked)
 
-        stage = keep.tile([P, 3 * N - P], F32, name="stage")
-        pos_g = stage[:, :N]
-        planes23 = stage[:, N - P : 2 * N - P].bitcast(BF16).rearrange("p (e c) -> p e c", e=2)
-        planes01 = stage[:, 2 * N - P :].bitcast(BF16).rearrange("p (e c) -> p e c", e=2)
-        hide = stage[:, N + HALF : 2 * N + HALF]
+        pos_g = keep.tile([P, N], F32, name="pos_g")
+        k_got = keep.tile([P, N, PACK], BF16, name="k_got", align_bytes=64)
         vs_g = keep.tile([P, N], F32, name="vs_g")
 
         gather("vector", pos_g, pos_pool, 0, HALF)
@@ -91,9 +89,10 @@ def tile_attend_x_draft_cap_topk_kernel(tc, qT, kT, vT, vs, pos, qpos, offs, out
             nc.tensor.transpose(pos_turned[:, t, :], pos_g[:, quarter(t)], ident[:])
         nc.tensor.matmul(pos_turned[:, PACK - 1, :], lhsT=qpos_row[:], rhs=ident[:], is_transpose=True, start=True, stop=False)
         nc.tensor.matmul(pos_turned[:, PACK - 1, :], lhsT=pos_g[:, quarter(PACK - 1)], rhs=ident[:], is_transpose=True, start=False, stop=True)
-        gather("vector", planes01[:, 0, :], k_pool[0], 0, N)
-        gather("scalar", vs_g, vs_pool, P, N)
-        gather("vector", vs_g, vs_pool, 0, P)
+        gather("vector", k_got[:, :, 0], k_pool[0], HALF, N)
+        gather("scalar", k_got[:, :, 0], k_pool[0], 0, HALF)
+        gather("scalar", vs_g, vs_pool, HALF, N)
+        gather("vector", vs_g, vs_pool, 0, HALF)
         pos_columns = keep.tile([P, PACK, 2], F32, name="pos_columns")
         nc.scalar.activation(out=pos_columns[:], in_=pos_turned[:, :, MID :: P // 2], func=ACT.Copy, scale=-STEEP)
         pos_spread = psum.tile([NQ, PACK, P], F32, name="pos_spread", tag="bank_b")
@@ -102,46 +101,46 @@ def tile_attend_x_draft_cap_topk_kernel(tc, qT, kT, vT, vs, pos, qpos, offs, out
         vs_turned = psum.tile([P, PACK, P], F32, name="vs_turned", tag="bank_a")
         for t in range(PACK):
             nc.tensor.transpose(vs_turned[:, t, :], vs_g[:, t::PACK], ident[:])
-        gather("scalar", planes01[:, 1, :], k_pool[1], 0, HALF)
-        gather("vector", planes01[:, 1, :], k_pool[1], HALF, N)
+        gather("scalar", k_got[:, :, 1], k_pool[1], 0, HALF)
+        gather("vector", k_got[:, :, 1], k_pool[1], HALF, N)
 
         work = keep.tile([P, HALF + BESIDE // 2], F32, name="work", align_bytes=64)
         q_bf = work[:, :HALF].bitcast(BF16)
         v_got1 = work[:, BESIDE // 2 : BESIDE // 2 + HALF]
-        k_got = keep.tile([P, N, PACK], BF16, name="k_got", align_bytes=64)
-        nc.vector.tensor_copy(out=k_got[:, :, 0:2], in_=planes01.rearrange("p e c -> p c e"))
 
-        gather("scalar", planes23[:, 0, :], k_pool[2], 0, N - AHEAD)
-        gather("vector", planes23[:, 0, :], k_pool[2], N - AHEAD, N)
-        for j in (2, 3):
-            gather("vector", planes23[:, 1, :], k_pool[3], j * P, (j + 1) * P)
-        gather("scalar", planes23[:, 1, :], k_pool[3], 0, HALF)
-        for slots in (quarter(2), quarter(3), half(0)):
-            nc.vector.tensor_copy(out=k_got[:, slots, 2:4], in_=planes23[:, :, slots].rearrange("p e c -> p c e"))
+        gather("scalar", k_got[:, :, 2], k_pool[2], N - SHARE, N)
+        gather("vector", k_got[:, :, 2], k_pool[2], 0, N - SHARE)
+        gather("scalar", k_got[:, :, 3], k_pool[3], N - P, N)
+        gather("scalar", k_got[:, :, 3], k_pool[3], N - SHARE, N - P)
+        gather("vector", k_got[:, :, 3], k_pool[3], P, N - SHARE)
+        gather("vector", k_got[:, :, 3], k_pool[3], 0, P)
 
         q_codes = keep.tile([P, NQ], U32, name="q_codes", align_bytes=64)
         q_scales = keep.tile([P, NQ], U8, name="q_scales", align_bytes=64)
         nc.scalar.copy(out=q_bf.rearrange("p (c i j) -> p c j i", i=PACK, j=PACK), in_=q_raw[:].rearrange("p j (c i) -> p c j i", i=PACK))
+        hide = reuse.tile([P, N], F32, name="hide", align_bytes=64, offset=2048)[:]
         nc.scalar.activation(
             out=hide.rearrange("p (j t s) -> p j t s", j=PACK, t=PACK),
             in_=pos_spread[:].rearrange("p j (s t) -> p j t s", t=PACK),
             func=ACT.Relu, scale=-1.0, bias=pos_columns[:, PACK - 1, 0:1],
         )
-        nc.vector.quantize_mx(out=q_codes[:].bitcast(FP8X4), scales=q_scales[:], in_=q_bf)
-
-        k_codes = keep.tile([P, N], U32, name="k_codes", tag="q_raw", align_bytes=64)
+        k_first = keep.tile([P, P], U32, name="k_first", align_bytes=64)
+        k_rest = reuse.tile([P, N - P], U32, name="k_rest", align_bytes=64, offset=0)
+        k_codes = [k_rest[:, quarter(j)] for j in range(PACK - 1)] + [k_first[:]]
         k_scales = [keep.tile([P, P], U8, name=f"k_scales{j}", align_bytes=64) for j in range(PACK)]
         score = [psum.tile([NQ, P], F32, name=f"score{j}", tag=f"score{j}") for j in range(PACK)]
         capped = keep.tile([NQ, N], F32, name="capped", tag="capped", align_bytes=64)
-        order = (2, 3, 1, 0)
+        order = (3, 2, 1, 0)
         for j in order:
             nc.vector.quantize_mx(
-                out=k_codes[:, quarter(j)].bitcast(FP8X4), scales=k_scales[j][:], in_=k_got[:, quarter(j), :].rearrange("p c e -> p (c e)")
+                out=k_codes[j].bitcast(FP8X4), scales=k_scales[j][:], in_=k_got[:, quarter(j), :].rearrange("p c e -> p (c e)")
             )
+            if j == order[0]:
+                nc.vector.quantize_mx(out=q_codes[:].bitcast(FP8X4), scales=q_scales[:], in_=q_bf)
         for j in order:
             nc.tensor.matmul_mx(
                 out=score[j][:], lhsT=q_codes[:].bitcast(FP8X4), lhsT_scale=q_scales[:],
-                rhs=k_codes[:, quarter(j)].bitcast(FP8X4), rhs_scale=k_scales[j][:], start=True, stop=True,
+                rhs=k_codes[j].bitcast(FP8X4), rhs_scale=k_scales[j][:], start=True, stop=True,
             )
 
         v_scales = [keep.tile([P, P], U8, name=f"v_scales{h}", align_bytes=64) for h in range(2)]

@@ -16,7 +16,8 @@ HALF = N // 2
 FIRST = T // 4
 BESIDE = 192
 SHARE = 192
-LATE = 128
+FILL = 128
+RUN = 16
 LAST = P - 1
 MID = P // 2 - 1
 
@@ -56,9 +57,9 @@ def tile_attend_x_draft_cap_topk_kernel(tc, qT, kT, vT, vs, pos, qpos, offs, out
         nc.sync.dma_start(out=k_pool[0][:, :FIRST], in_=k_rows[:, 0, :FIRST])
         nc.sync.dma_start(offsets[:], offs)
         nc.sync.dma_start(out=pos_pool[LAST:P, :], in_=pos[0:1, :])
-        nc.sync.dma_start(out=qpos_row[MID : MID + 1, :], in_=qpos.rearrange("b q o -> (b o) q"))
-        nc.sync.dma_start(out=k_pool[0][:, FIRST:], in_=k_rows[:, 0, FIRST:])
         nc.sync.dma_start(out=vs_pool[LAST:P, :], in_=vs[0:1, :])
+        nc.sync.dma_start(out=k_pool[0][:, FIRST:], in_=k_rows[:, 0, FIRST:])
+        nc.sync.dma_start(out=qpos_row[MID : MID + 1, :], in_=qpos.rearrange("b q o -> (b o) q"))
         for j in range(1, PACK):
             nc.sync.dma_start(out=k_pool[j][:], in_=k_rows[:, j, :])
         nc.sync.dma_start(out=q_raw[:], in_=qT.rearrange("b (p j) q -> p (b j) q", j=PACK))
@@ -71,28 +72,36 @@ def tile_attend_x_draft_cap_topk_kernel(tc, qT, kT, vT, vs, pos, qpos, offs, out
         def quarter(t):
             return slice(t * P, (t + 1) * P)
 
+        def dealt(row):
+            return row.rearrange("p (u g i) -> p g u i", u=2, i=RUN)
+
         def gather(engine, dst, pool, a, b):
             picked = pool[:].indirect(offsets[:, a // 16 : b // 16])
             if engine == "scalar":
-                nc.scalar.activation(out=dst[:, a:b], in_=picked, func=ACT.Copy)
+                nc.scalar.activation(out=dst, in_=picked, func=ACT.Copy)
             else:
-                nc.vector.tensor_copy(dst[:, a:b], picked)
+                nc.vector.tensor_copy(dst, picked)
+
+        def gather_dealt(engine, row, pool, a, b):
+            gather(engine, dealt(row)[:, a // (2 * RUN) : b // (2 * RUN), :, :], pool, a, b)
 
         pos_g = keep.tile([P, N], F32, name="pos_g")
-        k_got = keep.tile([P, N, PACK], BF16, name="k_got", align_bytes=64)
         vs_g = keep.tile([P, N], F32, name="vs_g")
+        k_got = keep.tile([P, N, PACK], BF16, name="k_got", align_bytes=64)
 
-        gather("vector", pos_g, pos_pool, 0, HALF)
-        gather("scalar", pos_g, pos_pool, HALF, N)
+        def gather_keys(engine, j, a, b):
+            gather(engine, k_got[:, a:b, j], k_pool[j], a, b)
+
+        for h in range(2):
+            gather("scalar", pos_g[:, half(h)], pos_pool, h * HALF, (h + 1) * HALF)
+        gather_dealt("vector", vs_g[:], vs_pool, 0, N)
         pos_turned = psum.tile([P, PACK, P], F32, name="pos_turned", tag="bank_a")
         for t in range(PACK - 1):
             nc.tensor.transpose(pos_turned[:, t, :], pos_g[:, quarter(t)], ident[:])
         nc.tensor.matmul(pos_turned[:, PACK - 1, :], lhsT=qpos_row[:], rhs=ident[:], is_transpose=True, start=True, stop=False)
         nc.tensor.matmul(pos_turned[:, PACK - 1, :], lhsT=pos_g[:, quarter(PACK - 1)], rhs=ident[:], is_transpose=True, start=False, stop=True)
-        gather("vector", k_got[:, :, 0], k_pool[0], HALF, N)
-        gather("scalar", k_got[:, :, 0], k_pool[0], 0, HALF)
-        gather("scalar", vs_g, vs_pool, HALF, N)
-        gather("vector", vs_g, vs_pool, 0, HALF)
+        gather_keys("scalar", 0, 0, HALF)
+        gather_keys("vector", 0, HALF, N)
         pos_columns = keep.tile([P, PACK, 2], F32, name="pos_columns")
         nc.scalar.activation(out=pos_columns[:], in_=pos_turned[:, :, MID :: P // 2], func=ACT.Copy, scale=-STEEP)
         pos_spread = psum.tile([NQ, PACK, P], F32, name="pos_spread", tag="bank_b")
@@ -100,44 +109,39 @@ def tile_attend_x_draft_cap_topk_kernel(tc, qT, kT, vT, vs, pos, qpos, offs, out
             nc.tensor.transpose(pos_spread[:, t, :], pos_columns[:, t, 1:2].to_broadcast([P, P]), ident[:])
         vs_turned = psum.tile([P, PACK, P], F32, name="vs_turned", tag="bank_a")
         for t in range(PACK):
-            nc.tensor.transpose(vs_turned[:, t, :], vs_g[:, t::PACK], ident[:])
-        gather("scalar", k_got[:, :, 1], k_pool[1], 0, HALF)
-        gather("vector", k_got[:, :, 1], k_pool[1], HALF, N)
+            nc.tensor.transpose(vs_turned[:, t, :], vs_g[:, half(t // 2)][:, t % 2 :: 2], ident[:])
+        gather_keys("scalar", 1, 0, HALF)
+        gather_keys("vector", 1, HALF, N)
+        gather_keys("scalar", 2, 0, SHARE)
+        gather_keys("vector", 2, SHARE, N)
+        gather_keys("scalar", 3, 0, P)
+        gather_keys("scalar", 3, P, SHARE)
+        gather_keys("vector", 3, SHARE, N - P)
+        gather_keys("vector", 3, N - P, N)
 
-        work = keep.tile([P, HALF + BESIDE // 2], F32, name="work", align_bytes=64)
-        q_bf = work[:, :HALF].bitcast(BF16)
-        v_got1 = work[:, BESIDE // 2 : BESIDE // 2 + HALF]
-
-        gather("scalar", k_got[:, :, 2], k_pool[2], N - SHARE, N)
-        gather("vector", k_got[:, :, 2], k_pool[2], 0, N - SHARE)
-        gather("scalar", k_got[:, :, 3], k_pool[3], N - P, N)
-        gather("scalar", k_got[:, :, 3], k_pool[3], N - SHARE, N - P)
-        gather("vector", k_got[:, :, 3], k_pool[3], P, N - SHARE)
-        gather("vector", k_got[:, :, 3], k_pool[3], 0, P)
-
+        q_bf = keep.tile([P, NQ * PACK], BF16, name="q_bf", align_bytes=64)
         q_codes = keep.tile([P, NQ], U32, name="q_codes", align_bytes=64)
         q_scales = keep.tile([P, NQ], U8, name="q_scales", align_bytes=64)
-        nc.scalar.copy(out=q_bf.rearrange("p (c i j) -> p c j i", i=PACK, j=PACK), in_=q_raw[:].rearrange("p j (c i) -> p c j i", i=PACK))
-        hide = reuse.tile([P, N], F32, name="hide", align_bytes=64, offset=2048)[:]
-        nc.scalar.activation(
-            out=hide.rearrange("p (j t s) -> p j t s", j=PACK, t=PACK),
-            in_=pos_spread[:].rearrange("p j (s t) -> p j t s", t=PACK),
-            func=ACT.Relu, scale=-1.0, bias=pos_columns[:, PACK - 1, 0:1],
-        )
+        nc.scalar.copy(out=q_bf[:].rearrange("p (c i j) -> p c j i", i=PACK, j=PACK), in_=q_raw[:].rearrange("p j (c i) -> p c j i", i=PACK))
+        lead = P + BESIDE // PACK
+        stage = reuse.tile([P, lead + N], F32, name="stage", align_bytes=64, offset=2048)
+        hide = stage[:, lead:]
+        v_got = [hide[:, 2 * P - FILL // PACK : 2 * P - FILL // PACK + HALF], stage[:, :HALF]]
+        nc.scalar.activation(out=hide, in_=pos_spread[:].rearrange("p j s -> p (j s)"), func=ACT.Relu, scale=-1.0, bias=pos_columns[:, PACK - 1, 0:1])
+
         k_first = keep.tile([P, P], U32, name="k_first", align_bytes=64)
         k_rest = reuse.tile([P, N - P], U32, name="k_rest", align_bytes=64, offset=0)
-        k_codes = [k_rest[:, quarter(j)] for j in range(PACK - 1)] + [k_first[:]]
+        k_codes = [k_first[:]] + [k_rest[:, quarter(j)] for j in range(PACK - 1)]
         k_scales = [keep.tile([P, P], U8, name=f"k_scales{j}", align_bytes=64) for j in range(PACK)]
         score = [psum.tile([NQ, P], F32, name=f"score{j}", tag=f"score{j}") for j in range(PACK)]
-        capped = keep.tile([NQ, N], F32, name="capped", tag="capped", align_bytes=64)
-        order = (3, 2, 1, 0)
-        for j in order:
+        capped = keep.tile([NQ, N], F32, name="capped", align_bytes=64)
+        for j in range(PACK):
             nc.vector.quantize_mx(
                 out=k_codes[j].bitcast(FP8X4), scales=k_scales[j][:], in_=k_got[:, quarter(j), :].rearrange("p c e -> p (c e)")
             )
-            if j == order[0]:
-                nc.vector.quantize_mx(out=q_codes[:].bitcast(FP8X4), scales=q_scales[:], in_=q_bf)
-        for j in order:
+            if j == 0:
+                nc.vector.quantize_mx(out=q_codes[:].bitcast(FP8X4), scales=q_scales[:], in_=q_bf[:])
+        for j in range(PACK):
             nc.tensor.matmul_mx(
                 out=score[j][:], lhsT=q_codes[:].bitcast(FP8X4), lhsT_scale=q_scales[:],
                 rhs=k_codes[j].bitcast(FP8X4), rhs_scale=k_scales[j][:], start=True, stop=True,
@@ -146,58 +150,54 @@ def tile_attend_x_draft_cap_topk_kernel(tc, qT, kT, vT, vs, pos, qpos, offs, out
         v_scales = [keep.tile([P, P], U8, name=f"v_scales{h}", align_bytes=64) for h in range(2)]
         v_codes = [keep.tile([P, P], U32, name=f"v_codes{h}", align_bytes=64) for h in range(2)]
 
-        def turn_v(h, v_got, tag):
+        def gather_values(engine, h, a, b):
+            gather_dealt(engine, v_got[h].bitcast(BF16), v_pool[h], a, b)
+
+        def turn_v(h, tag):
             turned = psum.tile([P, 2, P], F32, name=f"v_turned{h}", tag=tag)
             for u in range(2):
-                nc.tensor.transpose(turned[:, u, :], v_got[:, u::2], ident[:])
+                nc.tensor.transpose(turned[:, u, :], v_got[h][:, quarter(u)], ident[:])
             return turned[:].rearrange("p u e -> p e u")
 
         def words(v_bf):
             return v_bf.bitcast(F32).rearrange("p (e u) -> p e u", u=2)
 
-        v_got0 = hide[:, HALF - LATE // 2 : N - LATE // 2]
-        gather("scalar", v_got1.bitcast(BF16), v_pool[1], N - BESIDE, N)
-        gather("vector", v_got1.bitcast(BF16), v_pool[1], 0, N - BESIDE)
-
-        def dealt(tile, j):
-            return tile[:].rearrange("p (h t j s) -> p h j t s", h=2, t=PACK, j=2)[:, j // 2, j % 2, :, :]
-
-        for j in order:
-            nc.scalar.activation(out=dealt(capped, j), in_=score[j][:].rearrange("p (s t) -> p t s", t=PACK), func=ACT.Tanh, scale=1.0 / CAP)
-        visible = keep.tile([NQ, N], F32, name="visible", tag="visible", align_bytes=64)
-        for j in order:
+        gather_values("vector", 1, 0, BESIDE)
+        for j in range(PACK):
+            nc.scalar.activation(out=capped[:, quarter(j)], in_=score[j][:], func=ACT.Tanh, scale=1.0 / CAP)
+        visible = keep.tile([NQ, N], F32, name="visible", align_bytes=64)
+        for j in range(PACK):
             nc.vector.scalar_tensor_tensor(
-                out=dealt(visible, j), in0=hide[:, quarter(j)].rearrange("p (t s) -> p t s", t=PACK), scalar=HIDDEN,
-                in1=dealt(capped, j), op0=ALU.min, op1=ALU.subtract,
+                out=visible[:, quarter(j)], in0=hide[:, quarter(j)], scalar=HIDDEN, in1=capped[:, quarter(j)], op0=ALU.min, op1=ALU.subtract,
             )
-        gather("vector", v_got0.bitcast(BF16), v_pool[0], 0, LATE)
-        gather("scalar", v_got0.bitcast(BF16), v_pool[0], LATE, N)
+        gather_values("scalar", 1, BESIDE, N)
+        gather_values("vector", 0, 0, FILL)
         neg_max = keep.tile([NQ, 1], F32, name="neg_max")
-        negated = keep.tile([NQ, N], F32, name="negated", tag="negated", align_bytes=64)
-        nc.vector.tensor_scalar(out=negated[:], in0=visible[:], scalar1=CAP, scalar2=None, op0=ALU.mult, op1=ALU.min, accum_out=neg_max[:])
+        negated = keep.tile([NQ, N], F32, name="negated", align_bytes=64)
+        nc.vector.tensor_scalar(
+            out=dealt(negated[:]), in0=visible[:].rearrange("p (g u i) -> p g u i", u=2, i=RUN),
+            scalar1=CAP, scalar2=None, op0=ALU.mult, op1=ALU.min, accum_out=neg_max[:],
+        )
+        v_turned1 = turn_v(1, "score2")
+        gather_values("vector", 0, FILL, N)
 
-        v_turned1 = turn_v(1, v_got1, "score2")
-        v_turned0 = turn_v(0, v_got0, "score3")
-        after_max = keep.tile([P, HALF + PACK], F32, name="after_max", tag="visible", align_bytes=64)
-        v_bf0 = after_max[:, :HALF].bitcast(BF16)
-        vs_columns = after_max[:, HALF:]
-        nc.vector.tensor_copy(out=vs_columns, in_=vs_turned[:, :, LAST])
-        nc.vector.tensor_copy(out=words(v_bf0), in_=v_turned0)
-        nc.vector.quantize_mx(out=v_codes[0][:].bitcast(FP8X4), scales=v_scales[0][:], in_=v_bf0)
         prob = keep.tile([NQ, N], F32, name="prob")
-        pieces = ((0, 2), (2, 4))
-        sums = keep.tile([NQ, len(pieces)], F32, name="sums")
+        sums = keep.tile([NQ, 2], F32, name="sums")
         p_turned = psum.tile([P, PACK, NQ], F32, name="p_turned")
-        by_place = negated[:].rearrange("p (h t s) -> p t h s", h=2, t=PACK)
-        for i, (a, b) in enumerate(pieces):
+        for u in range(2):
             nc.scalar.activation(
-                out=prob[:, a * P : b * P].rearrange("p (t h s) -> p t h s", t=b - a, h=2), in_=by_place[:, a:b, :, :],
-                func=ACT.Exp, scale=-1.0, bias=neg_max[:, 0:1], accum_out=sums[:, i : i + 1],
+                out=prob[:, half(u)].rearrange("p (e s) -> p e s", e=2), in_=negated[:, half(u)].rearrange("p (s e) -> p e s", e=2),
+                func=ACT.Exp, scale=-1.0, bias=neg_max[:, 0:1], accum_out=sums[:, u : u + 1],
             )
         for t in range(PACK):
             nc.tensor.transpose(p_turned[:, t, :], prob[:, quarter(t)], ident[:])
-        v_bf1 = keep.tile([P, P * PACK], BF16, name="v_bf1", tag="negated", align_bytes=64)
-        nc.scalar.copy(out=words(v_bf1[:]), in_=v_turned1)
+        v_bf1 = negated[:, half(0)].bitcast(BF16)
+        nc.scalar.copy(out=words(v_bf1), in_=v_turned1)
+        vs_columns = negated[:, HALF : HALF + PACK]
+        nc.vector.tensor_copy(out=vs_columns, in_=vs_turned[:, :, LAST])
+        v_turned0 = turn_v(0, "bank_a")
+        v_bf0 = keep.tile([P, P * PACK], BF16, name="v_bf0", align_bytes=64)
+        nc.scalar.copy(out=words(v_bf0[:]), in_=v_turned0)
 
         w_bf = keep.tile([P, NQ * PACK], BF16, name="w_bf", align_bytes=64)
         w_codes = keep.tile([P, NQ], U32, name="w_codes", align_bytes=64)
@@ -205,6 +205,7 @@ def tile_attend_x_draft_cap_topk_kernel(tc, qT, kT, vT, vs, pos, qpos, offs, out
         row_sum = keep.tile([NQ, 1], F32, name="row_sum")
         inverse = vs_columns[:, 0:1]
         nc.vector.tensor_reduce(out=row_sum[:], in_=sums[:], axis=mybir.AxisListType.X, op=ALU.add)
+        nc.vector.quantize_mx(out=v_codes[1][:].bitcast(FP8X4), scales=v_scales[1][:], in_=v_bf1)
         rows = [slice(h * NQ // 2, (h + 1) * NQ // 2) for h in range(2)]
         for h in range(2):
             nc.vector.tensor_tensor(
@@ -212,11 +213,11 @@ def tile_attend_x_draft_cap_topk_kernel(tc, qT, kT, vT, vs, pos, qpos, offs, out
                 in1=vs_columns.unsqueeze(1).to_broadcast([P, NQ // 2, PACK]), op=ALU.mult,
             )
         nc.vector.quantize_mx(out=w_codes[:, rows[0]].bitcast(FP8X4), scales=w_scales[:, rows[0]], in_=w_bf[:, half(0)])
-        nc.vector.quantize_mx(out=v_codes[1][:].bitcast(FP8X4), scales=v_scales[1][:], in_=v_bf1[:])
+        nc.vector.quantize_mx(out=v_codes[0][:].bitcast(FP8X4), scales=v_scales[0][:], in_=v_bf0[:])
         nc.vector.quantize_mx(out=w_codes[:, rows[1]].bitcast(FP8X4), scales=w_scales[:, rows[1]], in_=w_bf[:, half(1)])
         nc.vector.reciprocal(out=inverse, in_=row_sum[:])
         result = keep.tile([NQ, DV], F32, name="result")
-        for h, tag in ((0, "bank_a"), (1, "bank_b")):
+        for h, tag in ((1, "score0"), (0, "score1")):
             cols = slice(h * P, (h + 1) * P)
             y = psum.tile([NQ, P], F32, name=f"y{h}", tag=tag)
             nc.tensor.matmul_mx(

@@ -114,15 +114,19 @@ def tile_attend_x_draft_cap_topk_kernel(tc, qT, kT, vT, vs, pos, qpos, offs, out
         gather_keys("vector", 1, HALF, N)
         gather_keys("scalar", 2, 0, SHARE)
         gather_keys("vector", 2, SHARE, N)
-        gather_keys("scalar", 3, 0, P)
-        gather_keys("scalar", 3, P, SHARE)
+        gather_keys("scalar", 3, 0, SHARE)
         gather_keys("vector", 3, SHARE, N - P)
         gather_keys("vector", 3, N - P, N)
 
         q_bf = keep.tile([P, NQ * PACK], BF16, name="q_bf", align_bytes=64)
         q_codes = keep.tile([P, NQ], U32, name="q_codes", align_bytes=64)
         q_scales = keep.tile([P, NQ], U8, name="q_scales", align_bytes=64)
-        nc.scalar.copy(out=q_bf[:].rearrange("p (c i j) -> p c j i", i=PACK, j=PACK), in_=q_raw[:].rearrange("p j (c i) -> p c j i", i=PACK))
+        rows = [slice(h * NQ // 2, (h + 1) * NQ // 2) for h in range(2)]
+        nc.scalar.copy(
+            out=q_bf[:, half(0)].rearrange("p (c i j) -> p c j i", i=PACK, j=PACK),
+            in_=q_raw[:, :, rows[0]].rearrange("p j (c i) -> p c j i", i=PACK),
+        )
+        nc.gpsimd.tensor_copy(out=q_bf[:, half(1)].rearrange("p (q j) -> p q j", j=PACK), in_=q_raw[:, :, rows[1]].rearrange("p j q -> p q j"))
         lead = P + BESIDE // PACK
         stage = reuse.tile([P, lead + N], F32, name="stage", align_bytes=64, offset=2048)
         hide = stage[:, lead:]
@@ -140,7 +144,8 @@ def tile_attend_x_draft_cap_topk_kernel(tc, qT, kT, vT, vs, pos, qpos, offs, out
                 out=k_codes[j].bitcast(FP8X4), scales=k_scales[j][:], in_=k_got[:, quarter(j), :].rearrange("p c e -> p (c e)")
             )
             if j == 0:
-                nc.vector.quantize_mx(out=q_codes[:].bitcast(FP8X4), scales=q_scales[:], in_=q_bf[:])
+                for h in range(2):
+                    nc.vector.quantize_mx(out=q_codes[:, rows[h]].bitcast(FP8X4), scales=q_scales[:, rows[h]], in_=q_bf[:, half(h)])
         for j in range(PACK):
             nc.tensor.matmul_mx(
                 out=score[j][:], lhsT=q_codes[:].bitcast(FP8X4), lhsT_scale=q_scales[:],
@@ -206,7 +211,6 @@ def tile_attend_x_draft_cap_topk_kernel(tc, qT, kT, vT, vs, pos, qpos, offs, out
         inverse = vs_columns[:, 0:1]
         nc.vector.tensor_reduce(out=row_sum[:], in_=sums[:], axis=mybir.AxisListType.X, op=ALU.add)
         nc.vector.quantize_mx(out=v_codes[1][:].bitcast(FP8X4), scales=v_scales[1][:], in_=v_bf1)
-        rows = [slice(h * NQ // 2, (h + 1) * NQ // 2) for h in range(2)]
         for h in range(2):
             nc.vector.tensor_tensor(
                 out=w_bf[:, half(h)].rearrange("p (q t) -> p q t", t=PACK), in0=p_turned[:].rearrange("p t q -> p q t")[:, rows[h], :],

@@ -14,9 +14,9 @@ P = 128
 PACK = 4
 HALF = N // 2
 FIRST = T // 4
-BESIDE = 192
+BESIDE = 256
 SHARE = 192
-FILL = 128
+AFTER = 384
 RUN = 16
 LAST = P - 1
 MID = P // 2 - 1
@@ -130,7 +130,8 @@ def tile_attend_x_draft_cap_topk_kernel(tc, qT, kT, vT, vs, pos, qpos, offs, out
         lead = P + BESIDE // PACK
         stage = reuse.tile([P, lead + N], F32, name="stage", align_bytes=64, offset=2048)
         hide = stage[:, lead:]
-        v_got = [hide[:, 2 * P - FILL // PACK : 2 * P - FILL // PACK + HALF], stage[:, :HALF]]
+        late = N - 2 * P - (N - AFTER) // PACK
+        v_got = [hide[:, late : late + HALF], stage[:, :HALF]]
         nc.scalar.activation(out=hide, in_=pos_spread[:].rearrange("p j s -> p (j s)"), func=ACT.Relu, scale=-1.0, bias=pos_columns[:, PACK - 1, 0:1])
 
         k_first = keep.tile([P, P], U32, name="k_first", align_bytes=64)
@@ -176,7 +177,7 @@ def tile_attend_x_draft_cap_topk_kernel(tc, qT, kT, vT, vs, pos, qpos, offs, out
                 out=visible[:, quarter(j)], in0=hide[:, quarter(j)], scalar=HIDDEN, in1=capped[:, quarter(j)], op0=ALU.min, op1=ALU.subtract,
             )
         gather_values("scalar", 1, BESIDE, N)
-        gather_values("vector", 0, 0, FILL)
+        gather_values("scalar", 0, 0, N - AFTER)
         neg_max = keep.tile([NQ, 1], F32, name="neg_max")
         negated = keep.tile([NQ, N], F32, name="negated", align_bytes=64)
         nc.vector.tensor_scalar(
@@ -184,7 +185,7 @@ def tile_attend_x_draft_cap_topk_kernel(tc, qT, kT, vT, vs, pos, qpos, offs, out
             scalar1=CAP, scalar2=None, op0=ALU.mult, op1=ALU.min, accum_out=neg_max[:],
         )
         v_turned1 = turn_v(1, "score2")
-        gather_values("vector", 0, FILL, N)
+        gather_values("vector", 0, N - AFTER, N)
 
         prob = keep.tile([NQ, N], F32, name="prob")
         sums = keep.tile([NQ, 2], F32, name="sums")

@@ -16,7 +16,8 @@ HALF = N // 2
 FIRST = T // 4
 BESIDE = 256
 SHARE = 192
-AFTER = 384
+FILL = 128
+AFTER = 256
 RUN = 16
 LAST = P - 1
 MID = P // 2 - 1
@@ -177,7 +178,8 @@ def tile_attend_x_draft_cap_topk_kernel(tc, qT, kT, vT, vs, pos, qpos, offs, out
                 out=visible[:, quarter(j)], in0=hide[:, quarter(j)], scalar=HIDDEN, in1=capped[:, quarter(j)], op0=ALU.min, op1=ALU.subtract,
             )
         gather_values("scalar", 1, BESIDE, N)
-        gather_values("scalar", 0, 0, N - AFTER)
+        gather_values("scalar", 0, 0, N - AFTER - FILL)
+        gather_values("vector", 0, N - AFTER - FILL, N - AFTER)
         neg_max = keep.tile([NQ, 1], F32, name="neg_max")
         negated = keep.tile([NQ, N], F32, name="negated", align_bytes=64)
         nc.vector.tensor_scalar(

@@ -41,12 +41,12 @@ def tile_attend_x_draft_cap_topk_kernel(tc, qT, kT, vT, vs, pos, qpos, offs, out
 
         offsets = keep.tile([P, N // 16], U16, name="offsets")
         qpos_row = keep.tile([P, NQ], F32, name="qpos_row")
-        pos_pool = keep.tile([P, T], F32, name="pos_pool")
-        vs_pool = keep.tile([P, T], F32, name="vs_pool")
-        q_raw = reuse.tile([P, PACK, NQ], F32, name="q_raw", align_bytes=64, offset=1024)
+        pos_pool = keep.tile([P, T], F32, name="pos_pool", align_bytes=256)
+        vs_pool = keep.tile([P, T], F32, name="vs_pool", align_bytes=256)
+        q_raw = reuse.tile([P, PACK, NQ], F32, name="q_raw", align_bytes=256, offset=1024)
         k_rows = kT.rearrange("(p j) t -> p j t", j=PACK)
-        k_pool = [keep.tile([P, T], F32, name=f"k_pool{j}") for j in range(PACK)]
-        v_pool = [keep.tile([P, T], F32, name=f"v_pool{h}") for h in range(2)]
+        k_pool = [keep.tile([P, T], F32, name=f"k_pool{j}", align_bytes=256) for j in range(PACK)]
+        v_pool = [keep.tile([P, T], F32, name=f"v_pool{h}", align_bytes=256) for h in range(2)]
 
         nc.gpsimd.memset(qpos_row[MID + 1 : P, :], 0.0)
         nc.vector.memset(pos_pool[0:LAST, :], 0.0)
@@ -223,7 +223,7 @@ def tile_attend_x_draft_cap_topk_kernel(tc, qT, kT, vT, vs, pos, qpos, offs, out
         nc.vector.quantize_mx(out=v_codes[0][:].bitcast(FP8X4), scales=v_scales[0][:], in_=v_bf0[:])
         nc.vector.quantize_mx(out=w_codes[:, rows[1]].bitcast(FP8X4), scales=w_scales[:, rows[1]], in_=w_bf[:, half(1)])
         nc.vector.reciprocal(out=inverse, in_=row_sum[:])
-        result = keep.tile([NQ, DV], F32, name="result")
+        result = keep.tile([NQ, DV], F32, name="result", align_bytes=256)
         for h, tag in ((1, "score0"), (0, "score1")):
             cols = slice(h * P, (h + 1) * P)
             y = psum.tile([NQ, P], F32, name=f"y{h}", tag=tag)

@@ -13,7 +13,7 @@ BYTES = 4 * (D * T + DV * T + D * NQ + 2 * T + NQ + NQ * DV) + 2 * 128 * N // 16
 P = 128
 PACK = 4
 HALF = N // 2
-FIRST = T // 4
+FIRST = 384
 BESIDE = 256
 SHARE = 192
 FILL = 128

@@ -15,7 +15,7 @@ PACK = 4
 HALF = N // 2
 FIRST = 384
 BESIDE = 256
-SHARE = 192
+SHARE = 224
 FILL = 128
 AFTER = 256
 RUN = 16
@@ -116,8 +116,7 @@ def tile_attend_x_draft_cap_topk_kernel(tc, qT, kT, vT, vs, pos, qpos, offs, out
         gather_keys("scalar", 2, 0, SHARE)
         gather_keys("vector", 2, SHARE, N)
         gather_keys("scalar", 3, 0, SHARE)
-        gather_keys("vector", 3, SHARE, N - P)
-        gather_keys("vector", 3, N - P, N)
+        gather_keys("vector", 3, SHARE, N)
 
         q_bf = keep.tile([P, NQ * PACK], BF16, name="q_bf", align_bytes=64)
         q_codes = keep.tile([P, NQ], U32, name="q_codes", align_bytes=64)
@@ -146,7 +145,7 @@ def tile_attend_x_draft_cap_topk_kernel(tc, qT, kT, vT, vs, pos, qpos, offs, out
                 out=k_codes[j].bitcast(FP8X4), scales=k_scales[j][:], in_=k_got[:, quarter(j), :].rearrange("p c e -> p (c e)")
             )
             if j == 0:
-                for h in range(2):
+                for h in (1, 0):
                     nc.vector.quantize_mx(out=q_codes[:, rows[h]].bitcast(FP8X4), scales=q_scales[:, rows[h]], in_=q_bf[:, half(h)])
         for j in range(PACK):
             nc.tensor.matmul_mx(

from contextlib import ExitStack

import concourse.mybir as mybir
from concourse.masks import make_identity

D, T, N, DV, NQ = 512, 1024, 512, 256, 128
CAP = 2.0
HIDDEN = float(2**27)
STEEP = float(2**64)
FLOPS = 2 * D * NQ * N + 2 * N * NQ * DV
BYTES = 4 * (D * T + DV * T + D * NQ + 2 * T + NQ + NQ * DV) + 2 * 128 * N // 16

P = 128
PACK = 4
HALF = N // 2
FIRST = 384
BESIDE = 256
SHARE = 224
FILL = 128
AFTER = 256
RUN = 16
LAST = P - 1
MID = P // 2 - 1

F32 = mybir.dt.float32
BF16 = mybir.dt.bfloat16
U32 = mybir.dt.uint32
U16 = mybir.dt.uint16
U8 = mybir.dt.uint8
FP8X4 = mybir.dt.float8_e4m3fn_x4
ALU = mybir.AluOpType
ACT = mybir.ActivationFunctionType


def tile_attend_x_draft_cap_topk_kernel(tc, qT, kT, vT, vs, pos, qpos, offs, out):
    nc = tc.nc
    with ExitStack() as ctx:
        keep = ctx.enter_context(tc.tile_pool(name="keep", bufs=1))
        psum = ctx.enter_context(tc.psum_pool(name="psum", bufs=1))
        reuse = ctx.enter_context(tc.tile_pool(name="reuse", bufs=1))

        offsets = keep.tile([P, N // 16], U16, name="offsets")
        qpos_row = keep.tile([P, NQ], F32, name="qpos_row")
        pos_pool = keep.tile([P, T], F32, name="pos_pool", align_bytes=256)
        vs_pool = keep.tile([P, T], F32, name="vs_pool", align_bytes=256)
        q_raw = reuse.tile([P, PACK, NQ], F32, name="q_raw", align_bytes=256, offset=1024)
        k_rows = kT.rearrange("(p j) t -> p j t", j=PACK)
        k_pool = [keep.tile([P, T], F32, name=f"k_pool{j}", align_bytes=256) for j in range(PACK)]
        v_pool = [keep.tile([P, T], F32, name=f"v_pool{h}", align_bytes=256) for h in range(2)]

        nc.gpsimd.memset(qpos_row[MID + 1 : P, :], 0.0)
        nc.vector.memset(pos_pool[0:LAST, :], 0.0)
        nc.scalar.copy(out=qpos_row[0:MID, :], in_=pos_pool[0:MID, :NQ])
        ident = keep.tile([P, P], F32, name="ident")
        nc.vector.memset(ident[:], 0.0)
        make_identity(nc, ident[:], nomemset=True)
        nc.vector.memset(vs_pool[0:LAST, :], 0.0)
        nc.sync.dma_start(out=k_pool[0][:, :FIRST], in_=k_rows[:, 0, :FIRST])
        nc.sync.dma_start(offsets[:], offs)
        nc.sync.dma_start(out=pos_pool[LAST:P, :], in_=pos[0:1, :])
        nc.sync.dma_start(out=vs_pool[LAST:P, :], in_=vs[0:1, :])
        nc.sync.dma_start(out=k_pool[0][:, FIRST:], in_=k_rows[:, 0, FIRST:])
        nc.sync.dma_start(out=qpos_row[MID : MID + 1, :], in_=qpos.rearrange("b q o -> (b o) q"))
        for j in range(1, PACK):
            nc.sync.dma_start(out=k_pool[j][:], in_=k_rows[:, j, :])
        nc.sync.dma_start(out=q_raw[:], in_=qT.rearrange("b (p j) q -> p (b j) q", j=PACK))
        for h in (1, 0):
            nc.sync.dma_start(out=v_pool[h][:], in_=vT[h * P : (h + 1) * P, :])

        def half(h):
            return slice(h * HALF, (h + 1) * HALF)

        def quarter(t):
            return slice(t * P, (t + 1) * P)

        def dealt(row):
            return row.rearrange("p (u g i) -> p g u i", u=2, i=RUN)

        def gather(engine, dst, pool, a, b):
            picked = pool[:].indirect(offsets[:, a // 16 : b // 16])
            if engine == "scalar":
                nc.scalar.activation(out=dst, in_=picked, func=ACT.Copy)
            else:
                nc.vector.tensor_copy(dst, picked)

        def gather_dealt(engine, row, pool, a, b):
            gather(engine, dealt(row)[:, a // (2 * RUN) : b // (2 * RUN), :, :], pool, a, b)

        pos_g = keep.tile([P, N], F32, name="pos_g")
        vs_g = keep.tile([P, N], F32, name="vs_g")
        k_got = keep.tile([P, N, PACK], BF16, name="k_got", align_bytes=64)

        def gather_keys(engine, j, a, b):
            gather(engine, k_got[:, a:b, j], k_pool[j], a, b)

        for h in range(2):
            gather("scalar", pos_g[:, half(h)], pos_pool, h * HALF, (h + 1) * HALF)
        gather_dealt("vector", vs_g[:], vs_pool, 0, N)
        pos_turned = psum.tile([P, PACK, P], F32, name="pos_turned", tag="bank_a")
        for t in range(PACK - 1):
            nc.tensor.transpose(pos_turned[:, t, :], pos_g[:, quarter(t)], ident[:])
        nc.tensor.matmul(pos_turned[:, PACK - 1, :], lhsT=qpos_row[:], rhs=ident[:], is_transpose=True, start=True, stop=False)
        nc.tensor.matmul(pos_turned[:, PACK - 1, :], lhsT=pos_g[:, quarter(PACK - 1)], rhs=ident[:], is_transpose=True, start=False, stop=True)
        gather_keys("scalar", 0, 0, HALF)
        gather_keys("vector", 0, HALF, N)
        pos_columns = keep.tile([P, PACK, 2], F32, name="pos_columns")
        nc.scalar.activation(out=pos_columns[:], in_=pos_turned[:, :, MID :: P // 2], func=ACT.Copy, scale=-STEEP)
        pos_spread = psum.tile([NQ, PACK, P], F32, name="pos_spread", tag="bank_b")
        for t in range(PACK):
            nc.tensor.transpose(pos_spread[:, t, :], pos_columns[:, t, 1:2].to_broadcast([P, P]), ident[:])
        vs_turned = psum.tile([P, PACK, P], F32, name="vs_turned", tag="bank_a")
        for t in range(PACK):
            nc.tensor.transpose(vs_turned[:, t, :], vs_g[:, half(t // 2)][:, t % 2 :: 2], ident[:])
        gather_keys("scalar", 1, 0, HALF)
        gather_keys("vector", 1, HALF, N)
        gather_keys("scalar", 2, 0, SHARE)
        gather_keys("vector", 2, SHARE, N)
        gather_keys("scalar", 3, 0, SHARE)
        gather_keys("vector", 3, SHARE, N)

        q_bf = keep.tile([P, NQ * PACK], BF16, name="q_bf", align_bytes=64)
        q_codes = keep.tile([P, NQ], U32, name="q_codes", align_bytes=64)
        q_scales = keep.tile([P, NQ], U8, name="q_scales", align_bytes=64)
        rows = [slice(h * NQ // 2, (h + 1) * NQ // 2) for h in range(2)]
        nc.scalar.copy(
            out=q_bf[:, half(0)].rearrange("p (c i j) -> p c j i", i=PACK, j=PACK),
            in_=q_raw[:, :, rows[0]].rearrange("p j (c i) -> p c j i", i=PACK),
        )
        nc.gpsimd.tensor_copy(out=q_bf[:, half(1)].rearrange("p (q j) -> p q j", j=PACK), in_=q_raw[:, :, rows[1]].rearrange("p j q -> p q j"))
        lead = P + BESIDE // PACK
        stage = reuse.tile([P, lead + N], F32, name="stage", align_bytes=64, offset=2048)
        hide = stage[:, lead:]
        late = N - 2 * P - (N - AFTER) // PACK
        v_got = [hide[:, late : late + HALF], stage[:, :HALF]]
        nc.scalar.activation(out=hide, in_=pos_spread[:].rearrange("p j s -> p (j s)"), func=ACT.Relu, scale=-1.0, bias=pos_columns[:, PACK - 1, 0:1])

        k_first = keep.tile([P, P], U32, name="k_first", align_bytes=64)
        k_rest = reuse.tile([P, N - P], U32, name="k_rest", align_bytes=64, offset=0)
        k_codes = [k_first[:]] + [k_rest[:, quarter(j)] for j in range(PACK - 1)]
        k_scales = [keep.tile([P, P], U8, name=f"k_scales{j}", align_bytes=64) for j in range(PACK)]
        score = [psum.tile([NQ, P], F32, name=f"score{j}", tag=f"score{j}") for j in range(PACK)]
        capped = keep.tile([NQ, N], F32, name="capped", align_bytes=64)
        for j in range(PACK):
            nc.vector.quantize_mx(
                out=k_codes[j].bitcast(FP8X4), scales=k_scales[j][:], in_=k_got[:, quarter(j), :].rearrange("p c e -> p (c e)")
            )
            if j == 0:
                for h in (1, 0):
                    nc.vector.quantize_mx(out=q_codes[:, rows[h]].bitcast(FP8X4), scales=q_scales[:, rows[h]], in_=q_bf[:, half(h)])
        for j in range(PACK):
            nc.tensor.matmul_mx(
                out=score[j][:], lhsT=q_codes[:].bitcast(FP8X4), lhsT_scale=q_scales[:],
                rhs=k_codes[j].bitcast(FP8X4), rhs_scale=k_scales[j][:], start=True, stop=True,
            )

        v_scales = [keep.tile([P, P], U8, name=f"v_scales{h}", align_bytes=64) for h in range(2)]
        v_codes = [keep.tile([P, P], U32, name=f"v_codes{h}", align_bytes=64) for h in range(2)]

        def gather_values(engine, h, a, b):
            gather_dealt(engine, v_got[h].bitcast(BF16), v_pool[h], a, b)

        def turn_v(h, tag):
            turned = psum.tile([P, 2, P], F32, name=f"v_turned{h}", tag=tag)
            for u in range(2):
                nc.tensor.transpose(turned[:, u, :], v_got[h][:, quarter(u)], ident[:])
            return turned[:].rearrange("p u e -> p e u")

        def words(v_bf):
            return v_bf.bitcast(F32).rearrange("p (e u) -> p e u", u=2)

        gather_values("vector", 1, 0, BESIDE)
        for j in range(PACK):
            nc.scalar.activation(out=capped[:, quarter(j)], in_=score[j][:], func=ACT.Tanh, scale=1.0 / CAP)
        visible = keep.tile([NQ, N], F32, name="visible", align_bytes=64)
        for j in range(PACK):
            nc.vector.scalar_tensor_tensor(
                out=visible[:, quarter(j)], in0=hide[:, quarter(j)], scalar=HIDDEN, in1=capped[:, quarter(j)], op0=ALU.min, op1=ALU.subtract,
            )
        gather_values("scalar", 1, BESIDE, N)
        gather_values("scalar", 0, 0, N - AFTER - FILL)
        gather_values("vector", 0, N - AFTER - FILL, N - AFTER)
        neg_max = keep.tile([NQ, 1], F32, name="neg_max")
        negated = keep.tile([NQ, N], F32, name="negated", align_bytes=64)
        nc.vector.tensor_scalar(
            out=dealt(negated[:]), in0=visible[:].rearrange("p (g u i) -> p g u i", u=2, i=RUN),
            scalar1=CAP, scalar2=None, op0=ALU.mult, op1=ALU.min, accum_out=neg_max[:],
        )
        v_turned1 = turn_v(1, "score2")
        gather_values("vector", 0, N - AFTER, N)

        prob = keep.tile([NQ, N], F32, name="prob")
        sums = keep.tile([NQ, 2], F32, name="sums")
        p_turned = psum.tile([P, PACK, NQ], F32, name="p_turned")
        for u in range(2):
            nc.scalar.activation(
                out=prob[:, half(u)].rearrange("p (e s) -> p e s", e=2), in_=negated[:, half(u)].rearrange("p (s e) -> p e s", e=2),
                func=ACT.Exp, scale=-1.0, bias=neg_max[:, 0:1], accum_out=sums[:, u : u + 1],
            )
        for t in range(PACK):
            nc.tensor.transpose(p_turned[:, t, :], prob[:, quarter(t)], ident[:])
        v_bf1 = negated[:, half(0)].bitcast(BF16)
        nc.scalar.copy(out=words(v_bf1), in_=v_turned1)
        vs_columns = negated[:, HALF : HALF + PACK]
        nc.vector.tensor_copy(out=vs_columns, in_=vs_turned[:, :, LAST])
        v_turned0 = turn_v(0, "bank_a")
        v_bf0 = keep.tile([P, P * PACK], BF16, name="v_bf0", align_bytes=64)
        nc.scalar.copy(out=words(v_bf0[:]), in_=v_turned0)

        w_bf = keep.tile([P, NQ * PACK], BF16, name="w_bf", align_bytes=64)
        w_codes = keep.tile([P, NQ], U32, name="w_codes", align_bytes=64)
        w_scales = keep.tile([P, NQ], U8, name="w_scales", align_bytes=64)
        row_sum = keep.tile([NQ, 1], F32, name="row_sum")
        inverse = vs_columns[:, 0:1]
        nc.vector.tensor_reduce(out=row_sum[:], in_=sums[:], axis=mybir.AxisListType.X, op=ALU.add)
        nc.vector.quantize_mx(out=v_codes[1][:].bitcast(FP8X4), scales=v_scales[1][:], in_=v_bf1)
        for h in range(2):
            nc.vector.tensor_tensor(
                out=w_bf[:, half(h)].rearrange("p (q t) -> p q t", t=PACK), in0=p_turned[:].rearrange("p t q -> p q t")[:, rows[h], :],
                in1=vs_columns.unsqueeze(1).to_broadcast([P, NQ // 2, PACK]), op=ALU.mult,
            )
        nc.vector.quantize_mx(out=w_codes[:, rows[0]].bitcast(FP8X4), scales=w_scales[:, rows[0]], in_=w_bf[:, half(0)])
        nc.vector.quantize_mx(out=v_codes[0][:].bitcast(FP8X4), scales=v_scales[0][:], in_=v_bf0[:])
        nc.vector.quantize_mx(out=w_codes[:, rows[1]].bitcast(FP8X4), scales=w_scales[:, rows[1]], in_=w_bf[:, half(1)])
        nc.vector.reciprocal(out=inverse, in_=row_sum[:])
        result = keep.tile([NQ, DV], F32, name="result", align_bytes=256)
        for h, tag in ((1, "score0"), (0, "score1")):
            cols = slice(h * P, (h + 1) * P)
            y = psum.tile([NQ, P], F32, name=f"y{h}", tag=tag)
            nc.tensor.matmul_mx(
                out=y[:], lhsT=w_codes[:].bitcast(FP8X4), lhsT_scale=w_scales[:],
                rhs=v_codes[h][:].bitcast(FP8X4), rhs_scale=v_scales[h][:], start=True, stop=True,
            )
            nc.vector.tensor_scalar(out=result[:, cols], in0=y[:], scalar1=inverse, scalar2=None, op0=ALU.mult)
        nc.sync.dma_start(out=out.rearrange("b q e -> (b q) e"), in_=result[:])
